import numpy as np, ml_dtypes
CORES = [3,11,19,27,35,43,51,59]
N = 8
BF = ml_dtypes.bfloat16
W, A, L, S, Q, C = 4096, 8, 2, 4, 80, 48
def place(x, wv, kv):
    u = np.sum(wv * x, axis=2) & (W - 1)
    return (((u * u) >> 5)[..., None] + kv[:, :, None, :] * u[..., None]) & (W - 1)
def search(X, q, wv, kv):
    n, m = q.shape[0], q.shape[3]
    pl = place(q, wv, kv); ok = np.ones(pl.shape, bool); line = [pl]; levels, dist = [], []
    for l in range(L):
        k = A ** (l + 1)
        occ = np.take_along_axis(X, pl.reshape(n, 8, 1, m * k), 3)
        d = np.sum(np.abs(occ.reshape(n, 8, 16, m, k) - q[..., None]), axis=2)
        if l == 0: hit = np.any(d == 0, axis=3)
        levels.append(pl); dist.append(np.where(ok, d, -1))
        if l < L - 1:
            good = ok & (occ[:, :, 0].reshape(n, 8, m, k) != 512)
            pl = place(occ, wv, kv).reshape(n, 8, m, k * A)
            line = [np.repeat(a, A, axis=3) for a in line]
            ok = np.repeat(good, A, axis=3)
            for a in line: ok = ok & (pl != a)
            line.append(pl)
    D = np.concatenate(dist, axis=3); v = D.shape[3] - 1 - np.argmax(D[..., ::-1], axis=3)
    path = np.full((n, 8, m, L), -1, np.int64); depth = np.zeros((n, 8, m), np.int64); base = 0
    for l in range(L):
        k = A ** (l + 1); here = (v >= base) & (v < base + k); j = np.clip(v - base, 0, k - 1)
        for h in range(l + 1):
            t = np.take_along_axis(levels[h], (j // A ** (l - h))[..., None], 3)[..., 0]
            path[..., h] = np.where(here, t, path[..., h])
        depth = np.where(here, l, depth); base += k
    return (q[:, :, 0] != 512) & ~hit, depth, path
def step(X, q, wv, kv):
    n, m = q.shape[0], q.shape[3]
    live, depth, path = search(X, q, wv, kv)
    meet = np.zeros((n, 8, m, m), bool)
    for a in range(L):
        for b in range(L):
            meet |= (path[..., a][..., :, None] == path[..., b][..., None, :]) & (path[..., a] >= 0)[..., None]
    go = live & ~np.any(meet & live[:, :, None, :] & np.tri(m, m, -1, dtype=bool), axis=3)
    old = [np.take_along_axis(X, np.maximum(path[..., l], 0)[:, :, None, :], 3) for l in range(L)]
    Y = X.copy(); val = q; vic = old[0]
    for l in range(L):
        r, g, i = np.nonzero(go & (depth >= l))
        Y[r, g, :, path[r, g, i, l]] = val[r, g, :, i]; val = old[l]
        vic = np.where((depth >= l)[:, :, None, :], old[l], vic)
    gone = go & (vic[:, :, 0] != 512); slot = np.add.accumulate(gone.astype(np.int64), axis=2) - 1
    out = np.full((n, 8, 16, C), 512, np.int32); r, g, i = np.nonzero(gone & (slot < C))
    out[r, g, :, slot[r, g, i]] = vic[r, g, :, i]
    return Y, out
def records(rng, k): return rng.integers(0, 256, (N, 8, 16, k)).astype(np.int32)
def hashes(rng): return rng.integers(1, 256, (N, 8, 16, 1)).astype(np.int32), 2 * rng.integers(0, 1024, (N, 8, A)) + 1
def fill(rng, rec, wv, kv, full, bare):
    pl = place(rec, wv, kv); k = rec.shape[3]; X = np.full((N, 8, 16, W), 512, np.int32)
    for r in range(N):
        for g in range(8):
            own = np.full(W, -1); free = np.arange(k)
            for a in range(A):
                p = pl[r, g, free, a]; e = own[p] < 0; own[p[e]] = free[e]; free = free[own[p] != free]
            if full[r, g]: own = np.where(own < 0, rng.integers(0, k, W), own)
            own = np.where(rng.random(W) < bare[r, g], -1, own)
            X[r, g] = np.where(own >= 0, rec[r, g][:, own], 512)
    return X
def ask(rng, X, fresh):
    c = rng.integers(0, W, (N, 8, 1, S * Q)); v = np.take_along_axis(X, c, 3).reshape(N, 8, 16, S, Q)
    q = np.where((rng.random((N, 8, 1, S, Q)) < 0.2) & (v[:, :, :1] != 512), v, fresh.reshape(N, 8, 16, S, Q))
    j = np.where(rng.random((N, 8, 1, S, Q)) < 0.06, rng.integers(0, Q, (N, 8, 1, S, Q)), np.arange(Q))
    return np.take_along_axis(q, j, 4)
def pack(X, q, wv, kv):
    return {"x0": X.reshape(N, 128, W).astype(np.float32).astype(BF), "qs": np.ascontiguousarray(q).reshape(N, 128, S * Q).astype(np.float32).astype(BF),
            "wt": wv.reshape(N, 128, 1).astype(np.float32).astype(BF), "kk": np.repeat(kv, 16, axis=1).astype(np.int32)}
def setup_inputs(rng):
    wv, kv = hashes(rng); full = rng.random((N, 8)) < 0.5; bare = rng.choice(np.array([0.0, 0.002, 0.005, 0.02, 0.1]), (N, 8))
    full[:, 0] = True; bare[:, 0] = 0.0; bare[:, 1] = 0.005; bare[:, 2] = 0.02
    X = fill(rng, records(rng, 2 * W), wv, kv, full, bare)
    return pack(X, ask(rng, X, records(rng, S * Q)), wv, kv)
def setup_inputs_room(rng):
    wv, kv = hashes(rng); X = fill(rng, records(rng, 2 * W), wv, kv, np.ones((N, 8), bool), np.zeros((N, 8)))
    q = ask(rng, X, records(rng, S * Q)); pool = records(rng, 2 * Q); live, depth, path = search(X, pool, wv, kv)
    home = np.any(place(X, wv, kv) == np.arange(W)[:, None], axis=3)
    for r in range(N):
        for g in range(8):
            n = int(rng.choice(np.array([0, 1, C - 1, C, C + 1, Q])))
            if r == 0: n = (C, C + 1, Q, C - 1, 1, 0, C, Q)[g]
            used, take = set(), []
            for i in rng.permutation(2 * Q):
                p = set(path[r, g, i].tolist()) - {-1}
                if len(take) < n and live[r, g, i] and not (p & used):
                    take.append(int(i)); used |= p
            stay = rng.choice(np.nonzero(home[r, g])[0], Q - len(take))
            q[r, g, :, 0] = np.concatenate([pool[r, g][:, np.array(take, np.int64)], X[r, g][:, stay]], axis=1)[:, rng.permutation(Q)]
    return pack(X, q, wv, kv)
def setup_inputs_alike(rng):
    wv, kv = hashes(rng); wv[:] = wv[:1].copy(); kv[:, 2] = kv[:, 2, :1]; kv[:, 3, 1:] = kv[:, 3, 1:2]; kv[:] = kv[:1].copy()
    rec = (255 * rng.integers(0, 2, (N, 8, 16, 2 * W))).astype(np.int32); fresh = (255 * rng.integers(0, 2, (N, 8, 16, S * Q))).astype(np.int32)
    few = rng.integers(0, 256, (16, 24)).astype(np.int32)
    for g in (1, 5):
        for r in range(N):
            rec[r, g] = few[:, rng.integers(0, 24, 2 * W)]
            fresh[r, g] = np.where(rng.random(S * Q) < 0.5, few[:, rng.integers(0, 24, S * Q)], rng.integers(0, 256, (16, S * Q)))
    rec[:, 6, :, ::4] = 0
    rec[:, 7] = rng.integers(0, 3, (N, 16, 2 * W))
    full = rng.random((N, 8)) < 0.7; full[:, 1] = True; bare = rng.choice(np.array([0.0, 0.005, 0.02]), (N, 8))
    X = fill(rng, rec, wv, kv, full, bare); q = ask(rng, X, fresh)
    q[:, 4, :, 1] = q[:, 4, :, 1, :1]; q[:, 6, :, 2, ::5] = 0; q[:, 6, :, 0, Q - 1] = 255
    return pack(X, q, wv, kv)
def setup_inputs_hollow(rng):
    wv, kv = hashes(rng); bare = rng.choice(np.array([0.3, 0.6, 0.9, 0.97, 1.0]), (N, 8)); bare[0, 0] = 1.0; bare[1, 1] = 0.6
    full = rng.random((N, 8)) < 0.5; bare[:, 6:] = 0.0; full[:, 7] = True
    X = fill(rng, records(rng, 2 * W), wv, kv, full, bare); q = ask(rng, X, records(rng, S * Q))
    q[:, :, :, 2] = q[:, :, :, 1][..., rng.permutation(Q)]
    return pack(X, q, wv, kv)
def setup_inputs_edges(rng):
    wv, kv = hashes(rng); wv[:, 0] = 255; kv[:, :2] = rng.choice(np.array([1, 2046, 2047]), (N, 2, A)); kv[:, :2, 0] = 2047
    wv[:, 6, 0] |= 1; kv[:, 6] = kv[:, 6, :1].copy()
    full = rng.random((N, 8)) < 0.5; full[:, 0] = True; full[:, 4] = False; full[::2, 5] = True; full[1::2, 5] = False; full[:, 6] = False
    bare = np.zeros((N, 8)); bare[:, 3] = 0.3; bare[:, 7] = 0.1
    rec, fresh = records(rng, 2 * W), records(rng, S * Q)
    for v in (rec, fresh):
        k = v.shape[3]; v[:, 0] = np.where(rng.random((N, 1, k)) < 0.5, rng.integers(200, 256, (N, 16, k)), v[:, 0])
        v[::2, 5] = v[::2, 5] >> 2
    X = fill(rng, rec, wv, kv, full, bare); q = ask(rng, X, fresh)
    q[:, 0, :, 0, 0] = 255
    q[:, 1:3, :, 0, :8] = records(rng, 8)[:, 1:3]
    t = q[:, :, :, 0, :8].copy(); pl = place(t, wv, kv)[..., 0]; i = rng.integers(0, 16, (N, 8, 1, 8))
    near = np.where(np.arange(16)[:, None] == i, t + np.where(t < 255, 1, -1), t)
    for r in range(N):
        for g in (1, 2):
            for j in range(7, -1, -1): X[r, g, :, pl[r, g, j]] = near[r, g, :, j]
    X[:, 3] = np.where(rng.random((N, 1, W)) < 0.02, 0, X[:, 3]); X[:, 3, :, 0] = 512
    q[:, 3, :, 0, 0] = 0; q[:, 3, :, 1, 0] = 255
    X[:, 7, :, 0] = records(rng, 1)[:, 7, :, 0]; q[:, 7, :, 0, 0] = 0; pe = place(X[..., :1], wv, kv)[:, 7, 0]
    for r in range(N): X[r, 7, :, pe[r]] = 512
    for r in range(N):
        g = 4 + r % 2; c = rng.choice(np.nonzero(X[r, g, 0] != 512)[0], Q); q[r, g, :, 0] = X[r, g][:, c]
    q[1::2, 4, :, 0, 0] = records(rng, 1)[1::2, 4, :, 0]; q[1::2, 4, :, 1] = q[1::2, 4, :, 0, :1]
    rr = np.arange(8) % N; m = 256; pool = rng.integers(128, 256, (1, 8, 16, m)).astype(np.int32)
    live, depth, path = search(X[rr, 5][None], pool, wv[rr, 5][None], kv[rr, 5][None])
    for r in range(1, N, 2):
        p = path[0, r]; same = np.sum((p[:, None, :, None] == p[None, :, None, :]) & (p >= 0)[:, None, :, None], axis=(2, 3))
        fit = (same == 1) & live[0, r][:, None] & (live[0, r] & (depth[0, r] == L - 1))[None, :]
        a, b = divmod(int(np.argmax(fit)), m); z = pool[0, r][:, b:b + 1]
        q[r, 5, :, 1] = z; q[r, 5, :, 1, 0] = pool[0, r, :, a]
        X[r - 1, 5] = np.where(rng.random(W) < 0.125, z, X[r - 1, 5])
    mine = place(rec, wv, kv)[:, 6, :, 0]
    for r in range(1, N, 2):
        e = r - 1; p = mine[e]; i = np.nonzero(np.any(X[e, 6][:, p] != rec[e, 6], axis=0))[0]
        i = i[np.unique(p[i], return_index=True)[1]]
        t = place(X[e, 6][:, p[i]][None, None], wv[r:r + 1, 6:7], kv[r:r + 1, 6:7])[0, 0, :, 0]
        j = rng.permutation(np.unique(t, return_index=True)[1]); last = j[X[r, 6, 0, t[j]] != 512][:1]
        j = j[j != last[0]][:Q - 1]; j = np.concatenate([j[:C - 1], last, j[C - 1:]])
        q[e, 6] = rec[e, 6][:, i[j]][:, None, :]
        z = X[r, 6, :, int(t[last[0]])].copy()
        X[r, 6, :, t[j[:C]]] = 512
        c = rng.choice(np.nonzero(X[r, 6, 0] != 512)[0], S * Q); q[r, 6] = X[r, 6][:, c].reshape(16, S, Q); q[r, 6, :, 1, 0] = z
    return pack(X, q, wv, kv)
def setup_inputs_spread(rng):
    def uneven(k):
        v = np.minimum((np.exp2(2 + 6 * rng.random((N, 8, 1, k))) * rng.random((N, 8, 16, k))).astype(np.int32), 255)
        return np.where(rng.random((N, 8, 16, k)) < 0.02, 255, v).astype(np.int32)
    wv = np.minimum(np.exp2(8 * rng.random((N, 8, 16, 1))).astype(np.int32), 255); kv = np.minimum(np.exp2(11 * rng.random((N, 8, A))).astype(np.int64), 2047)
    X = fill(rng, uneven(2 * W), wv, kv, rng.random((N, 8)) < 0.6, rng.choice(np.array([0.0, 0.003, 0.01]), (N, 8)))
    return pack(X, ask(rng, X, uneven(S * Q)), wv, kv)
def check_inputs(d):
    bad = []
    v = np.asarray(d["x0"]).astype(np.float32); e = v == 512
    if not np.all(e | ((v >= 0) & (v <= 255) & (np.floor(v) == v))): bad.append("range of x0")
    e = e.reshape(N, 8, 16, W)
    if np.any(np.any(e, axis=2) != np.all(e, axis=2)): bad.append("empty records of x0")
    for k, lo in (("qs", 0), ("wt", 1)):
        v = np.asarray(d[k]).astype(np.float32)
        if not np.all((v >= lo) & (v <= 255) & (np.floor(v) == v)): bad.append("range of " + k)
    k = np.asarray(d["kk"])
    if np.min(k) < 1 or np.max(k) > 2047: bad.append("range of kk")
    k = k.reshape(N, 8, 16, A)
    if np.any(k != k[:, :, :1]): bad.append("rows of kk")
    return bad
def reference(x0, qs, wt, kk):
    X = x0.astype(np.float32).astype(np.int32).reshape(N, 8, 16, W); q = qs.astype(np.float32).astype(np.int32).reshape(N, 8, 16, S, Q)
    wv = wt.astype(np.float32).astype(np.int32).reshape(N, 8, 16, 1); kv = kk.reshape(N, 8, 16, A)[:, :, 0].astype(np.int64)
    come = np.full((N, 8, 16, C), 512, np.int32)
    for s in range(S):
        X, out = step(X, np.concatenate([q[:, :, :, s], come], axis=3), wv, kv)
        come = np.roll(out, 1, axis=0)
    return {"y": X.reshape(N, 128, W).astype(np.float32).astype(BF)}

@@ -1,0 +1,560 @@
+from concourse.mybir import AluOpType as O, AxisListType, ActivationFunctionType as F
+
+BIG = float(2 ** 24)
+MID = float(2 ** 23)
+XW = 4368
+SENT = 4352.0
+NB = (5, 3)
+SHARE = ((3, 7), (3,))
+STEPS = 4
+VORD = ("D1 Du Dq Do0 Dv0 Dv1 tab Do1 Dv2 Dv4 Dv5 Dv6 Dx dh con Dh Dl0 Dl1 Dl2 Dl3 Dl4",
+        "D1 send Du Dq Do0 Dv0 Dv1 Do1 Dv2 Dv4 Dv5 Dv6 tab Dx ah A1 Au Aq Ao0 Av0 Av1 Ao1 Av2 Av4 Av5 Av6 Av7 Ax Dh "
+        "Dl0 Dl1 Dl2 Ah Al0 Al1 Al2 Dl3 Dl4")
+SORD = ("Da Dk De8 Dg3 Da0 Da1 Dt3 Dg7 Da2 Dt7 Da4 Da5 Da6 th",
+        "Da Dk De8 Dg3 Da0 Da1 Dt3 Dg7 Da2 arr Da4 Dt7 Da5 pr Da6 Aa Ak Ae8 Ag3 Aa0 Aa1 Aa2 At3 Aa4 Aa5 Aa6 Aa7")
+PORD = ("DU codeD De Dd3 Ds0 Dd7 Ds3 Dp Ds5 Ds7 Dz DH",
+        "DU codeD De Dd3 Ds0 Dd7 AQ Ds3 Dp codeA AU Ds5 Ds7 Ae Ad3 As0 Dz As3 Ap As6 Az DH AH")
+
+SCRATCH = {}
+for _dt, _names in (
+        ("bfloat16", "X:4368 QS:320 WT:1 Q8:2560 QA:384 AR1:48 AR2:48 AR3:48 SB1:256 SB2:256 SB3:256 ONE:128 T1:128 BD:128 "
+                     "ID:128 NI:128 VI:128 TRI:128 LD:128 B1:160 BW:160 KC:576 ZR:8 DM2:8 QE:3 D1_0:640 D1_1:384 D2_0:5120 "
+                     "D2_1:3072 A_0:5760 A_1:3456 VD_0:320 VD_1:192 EM_0:320 EM_1:192 ZH:64 EQ:4096 VB:256 VIC:128 GO:8"),
+        ("float32", "KF:8 W256:1 BDF:128 IC:1 RW:256 MK:256 TH:256 NM:256 HF:16 Z16:16 PW:16 PX:16 NX:8 PC:1 NC:1 DM:16 "
+                    "R16:256 R32:256 KR:160 P1F:160 KRA:24 P1FA:24 UF:40 KM:8 LV:8 E:256 SC:256 PD:16 "
+                    "L2:8 CM:256 CS:256 OF:16 GW:8 SL:8"),
+        ("int32", "KI:8 PI:1 ICI:1 C1:8 UI0:160 UR0:160 SQ0:160 HH0:160 KU0:160 PM0:160 P1I:160 UIA:24 URA:24 SQA:24 "
+                  "HHA:24 KUA:24 PMA:24 UI:40 UR:40 SQ:40 HH:160 PM:320 TAB_0:400 TAB_1:240 KMI:8 BI:8 BT:8 IX:16"),
+        ("uint16", "P1U:160 P1UA:24 P2U:320 IU:16 PU:16 P16:256 OU:16 SU:8")):
+    for _n in _names.split():
+        SCRATCH[_n.split(":")[0]] = ("sbuf", [128, int(_n.split(":")[1])], _dt)
+PSUM = "pu pk0 pk1 pp pc ph st0 st1".split()
+for _n in PSUM:
+    SCRATCH[_n] = ("psum", [128, 512], "float32")
+HALF = (0, 320)
+SEMAPHORES = "cv cs cp cg lqs lwt lki lx sy arr1 arr2 arr3 ls1 ls2 ls3".split()
+
+
+def rank_program(g, core, T, topo):
+    rank = T.rank_of(core)
+    if rank is None:
+        return
+    queue = {"v": g.vector, "s": g.scalar, "p": g.tensor, "g": g, "y": g.sync}
+    count = {}
+    clock = {q: {} for q in queue}
+    seen = {}
+
+    def R(name, lo=0, hi=None, step=1):
+        if hi is None:
+            hi = T[name].shape[1]
+        return (name, lo, hi, T[name][:, lo:hi:step] if step != 1 else T[name][:, lo:hi])
+
+    def order(q, reads, writes):
+        need = []
+        for kind, refs in ((False, reads), (True, writes)):
+            for (name, lo, hi, _) in refs:
+                bank = name in PSUM
+                for a in seen.get(name, []):
+                    if bank and a[3] != q:
+                        need.append(a)
+                    elif bank and q == "p":
+                        pass
+                    elif a[0] < hi and lo < a[1] and (kind or a[2]):
+                        need.append(a)
+        best = {}
+        for a in need:
+            if clock[q].get(a[4], 0) < a[5] and (a[4] not in best or best[a[4]][5] < a[5]):
+                best[a[4]] = a
+        for s in list(best):
+            a = best[s]
+            if any(o != s and best[o][6].get(s, 0) >= a[5] for o in best):
+                continue
+            queue[q].wait_ge(T.sem[s], a[5])
+        for s in best:
+            a = best[s]
+            for k in a[6]:
+                clock[q][k] = max(clock[q].get(k, 0), a[6][k])
+            clock[q][s] = max(clock[q].get(s, 0), a[5])
+
+    def note(q, reads, writes, sem, n):
+        count[sem] = count.get(sem, 0) + n
+        snap = dict(clock[q])
+        snap[sem] = count[sem]
+        for kind, refs in ((False, reads), (True, writes)):
+            for (name, lo, hi, _) in refs:
+                old = seen.get(name, [])
+                if name in PSUM:
+                    old = [a for a in old if a[3] != q or (a[2] and not kind)]
+                elif kind:
+                    old = [a for a in old if not (lo <= a[0] and a[1] <= hi)]
+                else:
+                    old = [a for a in old if not (not a[2] and a[3] == q and lo <= a[0] and a[1] <= hi)]
+                old.append((lo, hi, kind, q, sem, count[sem], snap))
+                seen[name] = old
+
+    def op(q, call, args, reads, writes, sem=None, n=1, **kw):
+        order(q, reads, writes)
+        sem = sem or "c" + q
+        call(*args, **kw).then_inc(T.sem[sem], n)
+        note(q, reads, writes, sem, n)
+
+    def ref(x):
+        return x[3] if isinstance(x, tuple) else x
+
+    def refs(*xs):
+        return [x for x in xs if isinstance(x, tuple)]
+
+    V, S, P = g.vector, g.scalar, g.tensor
+
+    def cp(out, in_):
+        op("v", V.tensor_copy, (out[3], in_[3]), [in_], [out])
+
+    def tt(out, a, b, o):
+        op("v", V.tensor_tensor, (out[3], a[3], b[3], o), [a, b], [out])
+
+    def ts(out, a, s1, o1, *more):
+        s2 = more[0] if more else None
+        op("v", V.tensor_scalar, (out[3], a[3], ref(s1), ref(s2), o1) + more[1:], [a] + refs(s1, s2), [out])
+
+    def red(out, a, o):
+        op("v", V.tensor_reduce, (out[3], a[3], AxisListType.X, o), [a], [out])
+
+    def scan(out, d0, d1, init, o0, o1):
+        op("v", V.tensor_tensor_scan, (out[3], d0[3], d1[3], init, o0, o1), [d0, d1], [out])
+
+    def ms(out, c):
+        op("v", V.memset, (out[3], c), [], [out])
+
+    def act(out, in_, func, scale=1.0):
+        op("s", S.activation, (out[3], in_[3], func), [in_] + refs(scale), [out], scale=ref(scale))
+
+    def mm(out, l, r, start, stop):
+        op("p", P.matmul, (out[3], l[3], r[3], start, stop), [l, r], [out])
+
+    def tgather(out, win, off, in1, o):
+        op("v", V.tensor_tensor, (out[3], win[3].indirect(off[3]), in1[3], o), [win, off, in1], [out])
+
+    def sgather(out, win, off):
+        op("s", S.activation, (out[3], win[3].indirect(off[3]), F.Copy), [win, off], [out])
+
+    def scatter(win, off, in_):
+        op("v", V.tensor_copy, (win[3].indirect(off[3]), in_[3]), [in_, off], [win])
+
+    def run(tasks, orders):
+        at = {q: 0 for q in orders}
+        done = []
+        left = sum(len(orders[q]) for q in orders)
+        while left:
+            before = left
+            for q in orders:
+                while at[q] < len(orders[q]):
+                    label = orders[q][at[q]]
+                    want, f = tasks[label]
+                    if any(b not in done for b in want.split()):
+                        break
+                    f()
+                    done.append(label)
+                    at[q] += 1
+                    left -= 1
+            if left == before:
+                raise ValueError("the orders wait for one another")
+
+    op("y", g.sync.dma_start, (T.QS[:], T.qs[:]), [], [R("QS")], "lqs", 16)
+    op("s", S.dma_start, (T.WT[:], T.wt[:]), [], [R("WT")], "lwt", 16)
+    op("s", S.dma_start, (T.KI[:], T.kk[:]), [], [R("KI")], "lki", 16)
+    op("y", g.sync.dma_start, (T.X[:, 0:4096], T.x0[:]), [], [R("X", 0, 4096)], "lx", 16)
+
+    dst = T.cores[(rank + 1) % len(T.cores)]
+    src = T.cores[(rank - 1) % len(T.cores)]
+    rid, pid, _ = topo.addr(dst)
+
+    def mask_of(a, b):
+        return sum(1 << e for e in topo.engines(a, b)[::2])
+
+    def bits(m):
+        return bin(m).count("1")
+    for s in (1, 2, 3):
+        nm = "arr%d" % s
+        count[nm] = bits(mask_of(src, core))
+        seen["AR%d" % s] = [(0, 48, True, "remote", nm, count[nm], {})]
+
+    POOL = ("pool", 0, 1, None)
+
+    def aff(out, in_, pattern, cmp, base, cm):
+        op("g", g.affine_select, (out[3], in_[3], pattern, cmp, 0.0, base, cm), [in_], [out, POOL])
+
+    def iota(out, pattern, base, cm):
+        kw = {} if SCRATCH[out[0]][2] == "int32" else {"allow_small_or_imprecise_dtypes": True}
+        op("g", g.iota, (out[3], pattern, base, cm), [], [out, POOL], **kw)
+
+    def row(p, lo, hi):
+        return ("KC", lo, hi, T.KC[p:p + 1, lo:hi])
+
+    def double(f, name, lo, w, n, *a):
+        while w < n:
+            f(R(name, lo + w, lo + 2 * w), R(name, lo, lo + w), *a)
+            w *= 2
+
+    def eight(s):
+        more = (F.Copy,) if s else ()
+        f = act if s else cp
+        f(R("Q8", 640 * s, 640 * s + 80), R("QS", 80 * s, 80 * s + 80), *more)
+        double(f, "Q8", 640 * s, 80, 640, *more)
+
+    def hashes(out, data, base, width):
+        for r in range(16):
+            mm(out, R("BW", 16 - r, 144 - r), R(data, base + r, base + 16 * width, 16), r == 0, r == 15)
+
+    def drawn_hash(lo, hi):
+        cp(R("UI0", lo, hi), R("pu", lo, hi))
+        ts(R("UR0", lo, hi), R("UI0", lo, hi), 4095, O.bitwise_and)
+        tt(R("SQ0", lo, hi), R("UR0", lo, hi), R("UR0", lo, hi), O.mult)
+        tt(R("KU0", lo, hi), R("UR0", lo, hi), R("KR", lo, hi), O.mult)
+        ts(R("HH0", lo, hi), R("SQ0", lo, hi), 5, O.arith_shift_right)
+        tt(R("PM0", lo, hi), R("HH0", lo, hi), R("KU0", lo, hi), O.add)
+        ts(R("P1I", lo, hi), R("PM0", lo, hi), 4095, O.bitwise_and)
+        cp(R("P1U", lo, hi), R("P1I", lo, hi))
+        cp(R("P1F", lo, hi), R("P1I", lo, hi))
+
+    def parents(s):
+        act(R("pp", 0, 40), R("P1F", 40 * s, 40 * s + 40), F.Copy)
+        double(act, "pp", 0, 40, 320, F.Copy)
+
+    ms(R("ONE"), 1.0)
+    ms(R("KC"), 0.0)
+    aff(R("T1"), R("ONE"), [[-16, 8], [0, 16]], O.is_ge, 0, 1)
+    aff(R("BD"), R("T1"), [[16, 8], [0, 16]], O.is_ge, 15, -1)
+    aff(R("ID"), R("ONE"), [[-1, 128]], O.is_equal, 0, 1)
+    ms(row(0, 0, 576), -MID)
+    for h in (0, 1):
+        n1 = 8 * NB[h]
+        at = 360 * h
+        iota(row(32, at, at + n1), [[16, n1]], 16, 0)
+        iota(row(32, at + n1, at + 9 * n1), [[0, 8], [16, n1]], 1040, 0)
+        iota(row(64, at + n1, at + 9 * n1), [[1, 8], [0, n1]], 1, 0)
+    iota(R("PI"), [[0, 1]], 0, 1)
+    iota(R("RW"), [[0, 16], [1, 16]], 0, 0)
+    aff(R("TRI"), R("BD"), [[1, 128]], O.is_ge, -1, -1)
+    iota(R("DM"), [[16, 16]], 4096, 0)
+    iota(R("DM2"), [[16, 8]], 128, 0)
+
+    ms(R("B1"), 0.0)
+    ms(R("BW"), 0.0)
+    ms(R("X", 4096, XW), 512.0)
+    ms(R("ZR"), 0.0)
+    cp(R("B1", 16, 144, 16), R("BD", 0, 128, 16))
+    ts(R("BW", 16, 144, 16), R("B1", 16, 144, 16), R("WT"), O.mult)
+    eight(0)
+    hashes(R("pu", 0, 40), "Q8", 0, 40)
+    mm(R("ph", 0, 1), R("BD"), R("WT"), True, True)
+    cp(R("KF"), R("KI"))
+    for l in range(5):
+        cp(R("KR", l, 40, 5), R("KI"))
+    drawn_hash(0, 40)
+    ts(R("W256"), R("ph", 0, 1), 256.0, O.mult)
+    ts(R("B1", 16, 144, 16), R("B1", 16, 144, 16), 2048.0, O.mult)
+    for s in (1, 2, 3):
+        eight(s)
+    parents(0)
+    hashes(R("pu", 40, 160), "Q8", 640, 120)
+    act(R("NI"), R("ID"), F.Copy, -1.0)
+    act(R("VI"), R("ID"), F.Copy, -BIG)
+    act(R("BDF"), R("BD"), F.Copy)
+    double(act, "KR", 0, 40, 160, F.Copy)
+    ts(R("ICI"), R("PI"), 15, O.bitwise_and)
+    cp(R("IC"), R("ICI"))
+    ts(R("MK"), R("RW"), R("IC"), O.is_equal)
+    ms(R("HF", 0, 1), 1.0)
+    ms(R("HF", 1, 16, 2), 0.5)
+    ms(R("HF", 2, 16, 2), 0.25)
+    ms(R("Z16"), 0.0)
+    scan(R("PW"), R("HF"), R("Z16"), 1.0, O.mult, O.add)
+    tt(R("PX"), R("MK", 0, 16), R("PW"), O.mult)
+    red(R("PC"), R("PX"), O.add)
+    ts(R("PX", 0, 16, 2), R("PX", 0, 16, 2), 4.2, O.mult)
+    ts(R("PX", 1, 16, 2), R("PX", 1, 16, 2), 2.93, O.mult)
+    red(R("NC"), R("PX"), O.add)
+    ms(R("HF", 1, 8), 2.0 ** -24)
+    scan(R("PX", 0, 8), R("HF", 0, 8), R("Z16", 0, 8), 2.0 ** 84, O.mult, O.add)
+    ts(R("NX"), R("PX", 0, 8), R("NC"), O.mult)
+    PLACES = R("X", 0, XW)
+
+    def thresholds():
+        for l in range(8):
+            act(R("TH", 32 * l, 32 * l + 32), R("MK", 32 * l, 32 * l + 32), F.Copy, R("NX", l, l + 1))
+        act(R("LD"), R("BD"), F.Copy, R("PC"))
+
+    def constants1():
+        ts(R("NM"), R("MK"), 0.5, O.is_lt, 1e29, O.mult)
+        ms(R("R16"), 1.0)
+        ms(R("R32"), 0.0)
+        ms(R("C1", 0, 5), 40)
+        ms(R("C1", 5, 8), 24)
+        ms(R("R16", 0, 256, 16), 0.0)
+        ms(R("R32", 0, 256, 32), 1.0)
+        ts(R("DM"), R("DM"), R("IC"), O.add)
+        ts(R("DM2"), R("DM2"), R("IC"), O.add)
+        ms(R("TAB_0", 0, 1), SENT)
+
+    def constants2():
+        ms(R("TAB_1", 0, 1), SENT)
+        for l in range(3):
+            cp(R("KRA", l, 24, 3), R("KI"))
+        for s in (1, 2, 3):
+            ms(R("SB%d" % s, 0, 48), 512.0)
+        tt(R("TH"), R("TH"), R("NM"), O.max)
+
+    def queries(h, s, lo=0, hi=None):
+        return R("Q8", 640 * s + lo, 640 * s + (hi or 640)) if h == 0 else R("QA", lo, hi or 384)
+
+    def sums(h, blk, nblk):
+        n = 8 * NB[h]
+        for r in range(16):
+            mm(R("pk%d" % h, blk * n, (blk + nblk) * n), R("B1", 16 - r, 144 - r),
+               R("A_%d" % h, blk * 16 * n + r, (blk + nblk) * 16 * n, 16), False, False)
+
+    def gather1(h, s):
+        off = R("P1U", 40 * s, 40 * s + 40) if h == 0 else R("P1UA")
+        tgather(R("D1_%d" % h), PLACES, off, queries(h, s), O.subtract)
+
+    def codes(h):
+        n = 8 * NB[h]
+        mm(R("pk%d" % h, 0, 9 * n), R("ONE"), R("KC", 360 * h, 360 * h + 9 * n), True, False)
+
+    def remainder(h, s):
+        n = 8 * NB[h]
+        uq = R("UI0", 40 * s, 40 * s + 40) if h == 0 else R("UIA")
+        tt(R("UI", 0, n), R("pu", 0, n), uq, O.add)
+        ts(R("UR", 0, n), R("UI", 0, n), 4095, O.bitwise_and)
+        cp(R("UF", 0, n), R("UR", 0, n))
+
+    def multiples(h):
+        n = 8 * NB[h]
+        for b in range(8):
+            act(R("st%d" % (b // 4), (b % 4) * n, (b % 4 + 1) * n), R("UF", 0, n), F.Copy, R("KF", b, b + 1))
+
+    def squares(h):
+        n = 8 * NB[h]
+        tt(R("SQ", 0, n), R("UR", 0, n), R("UR", 0, n), O.mult)
+        ts(R("HH", 0, n), R("SQ", 0, n), 5, O.arith_shift_right)
+        double(cp, "HH", 0, n, 4 * n)
+        ts(R("EM_%d" % h, 0, n), R("UI", 0, n), R("W256"), O.is_gt)
+
+    def offsets(h, half):
+        n = 8 * NB[h]
+        lo, hi = half * 4 * n, half * 4 * n + 4 * n
+        tab = R("TAB_%d" % h, 1 + n + lo, 1 + n + hi)
+        tt(R("PM", lo, hi), R("st%d" % half, 0, 4 * n), R("HH", 0, 4 * n), O.add)
+        ts(tab, R("PM", lo, hi), 4095, O.bitwise_and)
+        cp(R("P2U", lo, hi), tab)
+
+    def vgather2(h, s, b):
+        n = 8 * NB[h]
+        tgather(R("D2_%d" % h, b * 16 * n, (b + 1) * 16 * n), PLACES, R("P2U", b * n, b * n + n), queries(h, s), O.subtract)
+
+    def sgather2(h, b):
+        n = 8 * NB[h]
+        sgather(R("D2_%d" % h, b * 16 * n, (b + 1) * 16 * n), PLACES, R("P2U", b * n, b * n + n))
+
+    def pieces(h):
+        return (0, 320, 640) if h == 0 else (0, 384)
+
+    def stage(h, b, k):
+        c = pieces(h)
+        return R("st%d" % ((k + SHARE[h].index(b)) % 2), 0, c[k + 1] - c[k])
+
+    def psub2(h, s, b):
+        at = b * 128 * NB[h]
+        c = pieces(h)
+        for k in range(len(c) - 1):
+            mm(stage(h, b, k), R("NI"), queries(h, s, c[k], c[k + 1]), True, False)
+            mm(stage(h, b, k), R("ID"), R("D2_%d" % h, at + c[k], at + c[k + 1]), False, True)
+
+    def abs_of_psum(h, b):
+        at = (1 + b) * 128 * NB[h]
+        c = pieces(h)
+        for k in range(len(c) - 1):
+            act(R("A_%d" % h, at + c[k], at + c[k + 1]), stage(h, b, k), F.Abs)
+
+    def abs2(h, b):
+        n = 128 * NB[h]
+        act(R("A_%d" % h, (1 + b) * n, (2 + b) * n), R("D2_%d" % h, b * n, b * n + n), F.Abs)
+
+    def eightfold(h):
+        double(act, "EM_%d" % h, 0, 8 * NB[h], 64 * NB[h], F.Copy)
+
+    def void(h, name):
+        n = 8 * NB[h]
+        mm(R("pk%d" % h, n, 9 * n), R("VI"), R("%s_%d" % (name, h)), False, False)
+
+    def same(h):
+        n = 8 * NB[h]
+        tt(R("VD_%d" % h), R("TAB_%d" % h, 1 + n, 1 + 9 * n), R("pp", HALF[h], HALF[h] + 8 * n), O.is_equal)
+
+    def close(h):
+        mm(R("pk%d" % h, 0, 8), R("ID"), R("ZR"), False, True)
+
+    def hits(h):
+        n = 8 * NB[h]
+        ts(R("ZH", 40 * h, 40 * h + n), R("pk%d" % h, 0, n), 2048.0 - MID, O.is_lt)
+
+    def phits(h):
+        nb = NB[h]
+        l0 = 5 * h
+        for a in range(8):
+            z = R("ZH", 40 * h + a * nb, 40 * h + a * nb + nb)
+            mm(R("ph", l0, l0 + nb), R("ID"), z, a == 0, a == 7 and h == 0)
+        if h == 1:
+            mm(R("ph", l0, l0 + nb), R("ID"), R("QE"), False, True)
+
+    def largest(h, l):
+        nb = NB[h]
+        red(R("KM", 5 * h + l, 5 * h + l + 1), R("pk%d" % h, l, 9 * 8 * nb, nb), O.max)
+
+    def arrivals(s):
+        act(R("QA", 0, 48), R("AR%d" % s), F.Copy)
+        double(act, "QA", 0, 48, 384, F.Copy)
+
+    def arrivals_hash():
+        p1 = R("TAB_1", 1, 25)
+        cp(R("UIA"), R("pu", 0, 24))
+        ts(R("URA"), R("UIA"), 4095, O.bitwise_and)
+        tt(R("SQA"), R("URA"), R("URA"), O.mult)
+        tt(R("KUA"), R("URA"), R("KRA"), O.mult)
+        ts(R("HHA"), R("SQA"), 5, O.arith_shift_right)
+        tt(R("PMA"), R("HHA"), R("KUA"), O.add)
+        ts(p1, R("PMA"), 4095, O.bitwise_and)
+        cp(R("P1UA"), p1)
+        cp(R("P1FA"), p1)
+        ts(R("QE"), R("UIA", 0, 3), R("W256"), O.is_gt)
+
+    def arrivals_parents():
+        act(R("pp", 320, 344), R("P1FA"), F.Copy)
+        double(act, "pp", 320, 24, 192, F.Copy)
+
+    def ranks(nl):
+        mm(R("ph", 16, 16 + nl), R("TRI"), R("GO", 0, nl), True, False)
+        for k in range(1, nl):
+            mm(R("ph", 16 + k, 16 + nl), R("BD"), R("GO", 0, nl - k), False, False)
+        mm(R("ph", 16, 16 + nl), R("NI"), R("DM2", 0, nl), False, True)
+
+    def send_slots(nl, s):
+        tt(R("SL", 0, nl), R("ph", 16, 16 + nl), R("GO", 0, nl), O.mult)
+        tt(R("SL", 0, nl), R("SL", 0, nl), R("DM2", 0, nl), O.add)
+        cp(R("SU", 0, nl), R("SL", 0, nl))
+        scatter(R("SB%d" % s), R("SU", 0, nl), R("VIC", 0, 16 * nl))
+        m = mask_of(core, dst)
+        order("g", [R("SB%d" % s, 0, 48)], [])
+        g.remote_dma(T["AR%d" % s][:], T["SB%d" % s][:, 0:48], T.sem["arr%d" % s], T.sem["ls%d" % s], pid, rid, m)
+        note("g", [R("SB%d" % s, 0, 48)], [], "ls%d" % s, bits(m))
+
+    for s in range(STEPS):
+        two = s > 0
+        more = s < STEPS - 1
+        nl = 8 if two else 5
+        was = 8 if s > 1 else 5
+        tasks = {}
+
+        def task(label, before, f, *args):
+            tasks[label] = (before, lambda: f(*args))
+
+        for h in (0, 1):
+            H = "DA"[h]
+            n = 8 * NB[h]
+            task(H + "1", "", gather1, h, s)
+            task(H + "a", H + "1", act, R("A_%d" % h, 0, 16 * n), R("D1_%d" % h), F.Abs)
+            task(H + "U", H + "1", hashes, R("pu", 0, n), "D1_%d" % h, 0, n)
+            task("code" + H, "", codes, h)
+            task(H + "u", H + "U", remainder, h, s)
+            task(H + "k", H + "u", multiples, h)
+            task(H + "q", H + "u", squares, h)
+            task(H + "e8", H + "q", eightfold, h)
+            task(H + "e", H + "e8", void, h, "EM")
+            for half in (0, 1):
+                task(H + "o%d" % half, H + "k " + H + "q", offsets, h, half)
+            for b in range(8):
+                o = H + "o%d" % (b // 4)
+                task(H + "v%d" % b, o, vgather2, h, s, b)
+                task(H + "g%d" % b, o, sgather2, h, b)
+                task(H + "d%d" % b, H + "g%d" % b, psub2, h, s, b)
+                task(H + "a%d" % b, H + "v%d" % b, abs2, h, b)
+                task(H + "t%d" % b, H + "d%d" % b, abs_of_psum, h, b)
+            for blk, k in ((0, 3), (3, 2), (5, 2), (7, 2)) if h == 0 else ((0, 3), (3, 3), (6, 3)):
+                want = [H + ("t" if b in SHARE[h] else "a") + str(b) for b in range(max(blk - 1, 0), blk + k - 1)]
+                task(H + "s%d" % blk, " ".join(want + [H + "a"]), sums, h, blk, k)
+            task(H + "x", H + "o1" + (" pr" if h else ""), same, h)
+            task(H + "p", H + "x", void, h, "VD")
+            task(H + "z", "", close, h)
+            task(H + "h", H + "z", hits, h)
+            task(H + "H", H + "h", phits, h)
+            for l in range(NB[h]):
+                task(H + "l%d" % l, H + "z", largest, h, l)
+        task("dh", "", drawn_hash, 40, 160)
+        task("con", "", constants1)
+        task("th", "", thresholds)
+        task("tab", "", cp, R("TAB_0", 1, 41), R("P1I", 40 * s, 40 * s + 40))
+        task("send", "", send_slots, was, s)
+        task("arr", "", arrivals, s)
+        task("AQ", "arr", hashes, R("pu", 0, 24), "QA", 0, 24)
+        task("ah", "AQ", arrivals_hash)
+        task("pr", "ah", arrivals_parents)
+        if two:
+            ranks(was)
+        run(tasks, {"v": VORD[two].split(), "s": SORD[two].split(), "p": PORD[two].split()})
+        w = 32 * nl
+        ts(R("LV", 0, nl), R("ph", 0, nl), 0.5, O.is_lt)
+        tt(R("KMI", 0, nl), R("KM", 0, nl), R("LV", 0, nl), O.mult)
+        i1, iv = R("IX", 0, 2 * nl, 2), R("IX", 1, 2 * nl, 2)
+        ts(R("BI", 0, nl), R("KMI", 0, nl), 15, O.bitwise_and)
+        ts(i1, R("KMI", 0, nl), 4, O.arith_shift_right, 63, O.bitwise_and)
+        tt(R("BT", 0, nl), R("BI", 0, nl), R("C1", 0, nl), O.mult)
+        tt(iv, i1, R("BT", 0, nl), O.add)
+        cp(R("IU", 0, 2 * nl), R("IX", 0, 2 * nl))
+        tgather(R("E", 0, 160), R("TAB_0", 0, 361), R("IU", 0, 10), R("MK", 0, 160), O.mult)
+        if two:
+            tgather(R("E", 160, 256), R("TAB_1", 0, 217), R("IU", 10, 16), R("MK", 160, 256), O.mult)
+        mm(R("pp", 0, w), R("BDF"), R("E", 0, w), True, True)
+        scan(R("SC", 0, w), R("R16", 0, w), R("E", 0, w), 0.0, O.mult, O.add)
+        p1, pv = R("SC", 15, w, 32), R("SC", 31, w, 32)
+        cp(R("PU", 0, nl), p1)
+        if more:
+            cp(R("PU", 8, 8 + nl), pv)
+        act(R("VB", 0, 80), R("QS", 80 * s, 80 * s + 80), F.Copy)
+        if two:
+            act(R("VB", 80, 128), R("AR%d" % s), F.Copy)
+        sgather(R("VB", 16 * nl, 32 * nl), PLACES, R("PU", 0, nl))
+        if more:
+            sgather(R("VIC", 0, 16 * nl), PLACES, R("PU", 8, 8 + nl))
+        tt(R("PD", 0, nl), p1, R("DM", 0, nl), O.subtract)
+        tt(R("PD", nl, 2 * nl), pv, R("DM", nl, 2 * nl), O.subtract)
+        tt(R("L2", 0, nl), p1, pv, O.not_equal)
+        if more:
+            ts(R("GW", 0, nl), R("KMI", 0, nl), 0, O.is_lt)
+        tt(R("PD", nl, 2 * nl), R("PD", nl, 2 * nl), R("L2", 0, nl), O.mult)
+        if not two:
+            constants2()
+        cp(R("P16", 0, w), R("pp", 0, w))
+        for l in range(nl):
+            for pa in range(2):
+                at = (2 * l + pa) * 256
+                k = w - 32 * l
+                own = R("SC", 32 * l + 16 * pa + 15, 32 * l + 16 * pa + 16)
+                ts(R("EQ", at, at + k), R("P16", 32 * l, w), own, O.is_equal, 2.0 ** (84 - 24 * l), O.mult)
+                mm(R("pc", 32 * l, w), R("LD"), R("EQ", at, at + k), l == 0 and pa == 0, l == nl - 1 and pa == 1)
+        tt(R("PD", 0, nl), R("PD", 0, nl), R("LV", 0, nl), O.mult)
+        if more:
+            parents(s + 1)
+        tt(R("CM", 0, w), R("pc", 0, w), R("TH", 0, w), O.is_lt)
+        scan(R("CS", 0, w), R("R32", 0, w), R("CM", 0, w), 0.0, O.max, O.min)
+        go = R("CS", 31, w, 32)
+        tt(R("OF", 0, nl), go, R("PD", 0, nl), O.mult)
+        tt(R("OF", nl, 2 * nl), go, R("PD", nl, 2 * nl), O.mult)
+        tt(R("OF", 0, 2 * nl), R("OF", 0, 2 * nl), R("DM", 0, 2 * nl), O.add)
+        cp(R("OU", 0, 2 * nl), R("OF", 0, 2 * nl))
+        scatter(PLACES, R("OU", 0, 2 * nl), R("VB", 0, 32 * nl))
+        if more:
+            tt(R("GO", 0, nl), go, R("GW", 0, nl), O.mult)
+    op("y", g.sync.dma_start, (T.y[:], T.X[:, 0:4096]), [R("X", 0, 4096)], [], "sy", 16)
+    for sem in count:
+        if clock["y"].get(sem, 0) < count[sem]:
+            g.sync.wait_ge(T.sem[sem], count[sem])

@@ -2,37 +2,91 @@ from concourse.mybir import AluOpType as O, AxisListType, ActivationFunctionType
 
 BIG = float(2 ** 24)
 MID = float(2 ** 23)
+HIT = float(2 ** 25)
+FLOOR = -0.5 + 2.0 ** -13
+SENT = 4096
 XW = 4368
-SENT = 4352.0
 NB = (5, 3)
-SHARE = ((3, 7), (3,))
+SHARE = ((1, 3, 5), (2,))
+GROUPS = (((0, 2), (2, 3), (5, 2), (7, 2)), ((0, 3), (3, 3), (6, 3)))
+CUT = 1
 STEPS = 4
-VORD = ("D1 Du Dq Do0 Dv0 Dv1 tab Do1 Dv2 Dv4 Dv5 Dv6 Dx dh con Dh Dl0 Dl1 Dl2 Dl3 Dl4",
-        "D1 send Du Dq Do0 Dv0 Dv1 Do1 Dv2 Dv4 Dv5 Dv6 tab Dx ah A1 Au Aq Ao0 Av0 Av1 Ao1 Av2 Av4 Av5 Av6 Av7 Ax Dh "
-        "Dl0 Dl1 Dl2 Ah Al0 Al1 Al2 Dl3 Dl4")
-SORD = ("Da Dk De8 Dg3 Da0 Da1 Dt3 Dg7 Da2 Dt7 Da4 Da5 Da6 th",
-        "Da Dk De8 Dg3 Da0 Da1 Dt3 Dg7 Da2 arr Da4 Dt7 Da5 pr Da6 Aa Ak Ae8 Ag3 Aa0 Aa1 Aa2 At3 Aa4 Aa5 Aa6 Aa7")
-PORD = ("DU codeD De Dd3 Ds0 Dd7 Ds3 Dp Ds5 Ds7 Dz DH",
-        "DU codeD De Dd3 Ds0 Dd7 AQ Ds3 Dp codeA AU Ds5 Ds7 Ae Ad3 As0 Dz As3 Ap As6 Az DH AH")
+HOP = 150.0
+PATIENCE = 0.5
+PASSES = 6
+PCYC = 0.5
+CYC, GATHER, SCATTER = 0.83, 1.56, 3.8
 
 SCRATCH = {}
 for _dt, _names in (
-        ("bfloat16", "X:4368 QS:320 WT:1 Q8:2560 QA:384 AR1:48 AR2:48 AR3:48 SB1:256 SB2:256 SB3:256 ONE:128 T1:128 BD:128 "
-                     "ID:128 NI:128 VI:128 TRI:128 LD:128 B1:160 BW:160 KC:576 ZR:8 DM2:8 QE:3 D1_0:640 D1_1:384 D2_0:5120 "
-                     "D2_1:3072 A_0:5760 A_1:3456 VD_0:320 VD_1:192 EM_0:320 EM_1:192 ZH:64 EQ:4096 VB:256 VIC:128 GO:8"),
-        ("float32", "KF:8 W256:1 BDF:128 IC:1 RW:256 MK:256 TH:256 NM:256 HF:16 Z16:16 PW:16 PX:16 NX:8 PC:1 NC:1 DM:16 "
-                    "R16:256 R32:256 KR:160 P1F:160 KRA:24 P1FA:24 UF:40 KM:8 LV:8 E:256 SC:256 PD:16 "
-                    "L2:8 CM:256 CS:256 OF:16 GW:8 SL:8"),
-        ("int32", "KI:8 PI:1 ICI:1 C1:8 UI0:160 UR0:160 SQ0:160 HH0:160 KU0:160 PM0:160 P1I:160 UIA:24 URA:24 SQA:24 "
-                  "HHA:24 KUA:24 PMA:24 UI:40 UR:40 SQ:40 HH:160 PM:320 TAB_0:400 TAB_1:240 KMI:8 BI:8 BT:8 IX:16"),
-        ("uint16", "P1U:160 P1UA:24 P2U:320 IU:16 PU:16 P16:256 OU:16 SU:8")):
+        ("bfloat16", "X:4368 QS:320 WT:1 Q8:2560 QA:384 AR1:48 AR2:48 AR3:48 SB1:384 SB2:384 SB3:384 ONE:128 T1:128 BD:128 "
+                     "ID:128 NI:128 VI:128 TRI:128 B1:160 BW:160 KC:592 DM2:8 QE:3 D1_0:640 D1_1:384 D2_0:5120 "
+                     "D2_1:3072 A_0:5760 A_1:3456 VD_0:320 VD_1:192 EM_0:40 EM_1:24 ZH_0:40 ZH_1:24 EQ:4096 VB:256 VIC:128 "
+                     "GO:8 BL:8 CW:8 NM:256"),
+        ("float32", "KF:8 W256:1 BDF:128 IDF:128 IC:1 RW:256 MK:256 DM:16 R16:256 R32:256 KR:160 F0:160 SQ0:160 KU0:160 "
+                    "P1F:160 KRA:24 FA:24 SQA:24 KUA:24 P1FA:24 UF_0:40 UF_1:24 SQ_0:40 SQ_1:24 KM:8 E:256 SC:256 PZ:16 "
+                    "L2:8 CS:256 MM:16 OF:16 GW:8 GC:8"),
+        ("int32", "KI:8 PI:1 ICI:1 C1:8 T0:160 HH0:160 PM0:160 P1I:160 TA:24 HHA:24 PMA:24 UI_0:40 UI_1:24 HH_0:80 HH_1:48 "
+                  "PM_0:320 PM_1:192 TAB_0:400 TAB_1:240 KMI:8 BI:8 BT:8 IX:16"),
+        ("uint16", "P1U:160 P1UA:24 P2U_0:320 P2U_1:192 IU:16 PU:16 P16:256 OU:16 SU:8")):
     for _n in _names.split():
         SCRATCH[_n.split(":")[0]] = ("sbuf", [128, int(_n.split(":")[1])], _dt)
 PSUM = "pu pk0 pk1 pp pc ph st0 st1".split()
 for _n in PSUM:
     SCRATCH[_n] = ("psum", [128, 512], "float32")
 HALF = (0, 320)
+CODE = (0, 368)
 SEMAPHORES = "cv cs cp cg lqs lwt lki lx sy arr1 arr2 arr3 ls1 ls2 ls3".split()
+
+
+def place(calls, before, after, urge):
+    left = [len(b) for b in before]
+    ready = [0.0] * len(calls)
+    end = [0.0] * len(calls)
+    free = {c["q"]: 0.0 for c in calls}
+    open_ = {q: [] for q in free}
+    for i, c in enumerate(calls):
+        if not left[i]:
+            open_[c["q"]].append(i)
+    out = []
+    while len(out) < len(calls):
+        t, q = min((max(free[q], min(ready[i] for i in open_[q])), q) for q in open_ if open_[q])
+        i = max((k for k in open_[q] if ready[k] <= t), key=lambda k: (urge[k], -k))
+        soon = [k for k in open_[q] if t < ready[k] < t + PATIENCE * calls[i]["busy"] and urge[k] > urge[i]]
+        if soon:
+            i = max(soon, key=lambda k: (urge[k], -k))
+            t = ready[i]
+        open_[q].remove(i)
+        free[q] = t + calls[i]["busy"]
+        end[i] = t + calls[i]["done"]
+        out.append(i)
+        for k, gap in after[i]:
+            ready[k] = max(ready[k], end[i] + gap)
+            left[k] -= 1
+            if not left[k]:
+                open_[calls[k]["q"]].append(k)
+    return out, end
+
+
+def arrange(calls):
+    before = [list(c["after"].items()) for c in calls]
+    after = [[] for _ in calls]
+    for i, b in enumerate(before):
+        for j, gap in b:
+            after[j].append((i, gap))
+    urge = [0.0] * len(calls)
+    for i in range(len(calls) - 1, -1, -1):
+        urge[i] = calls[i]["done"] + max([gap + urge[k] for k, gap in after[i]] + [0.0])
+    best = None
+    for _ in range(PASSES):
+        out, end = place(calls, before, after, urge)
+        if best is None or max(end) < best[0]:
+            best = (max(end), out)
+        urge = place(calls, after, before, end)[1]
+    return best[1]
+
+
+ORDER = []
 
 
 def rank_program(g, core, T, topo):
@@ -40,19 +94,400 @@ def rank_program(g, core, T, topo):
     if rank is None:
         return
     queue = {"v": g.vector, "s": g.scalar, "p": g.tensor, "g": g, "y": g.sync}
-    count = {}
-    clock = {q: {} for q in queue}
-    seen = {}
+    calls = []
+    wrote, read, turns = {}, {}, {}
 
     def R(name, lo=0, hi=None, step=1):
         if hi is None:
             hi = T[name].shape[1]
         return (name, lo, hi, T[name][:, lo:hi:step] if step != 1 else T[name][:, lo:hi])
 
-    def order(q, reads, writes):
-        need = []
-        for kind, refs in ((False, reads), (True, writes)):
+    def width(r):
+        return r[3].shape[1]
+
+    def narrow(*rs):
+        return all(r[0] in SCRATCH and SCRATCH[r[0]][2] in ("bfloat16", "uint16") for r in rs)
+
+    def op(q, call, args, reads, writes, busy, sem=None, n=1, done=None, lands=(), **kw):
+        i = len(calls)
+        after = {}
+        for kind, refs in ((False, reads), (True, list(writes) + list(lands))):
             for (name, lo, hi, _) in refs:
+                if name in PSUM:
+                    t = turns.setdefault(name, [q, [], []])
+                    if t[0] != q:
+                        t[:] = [q, [], t[1][-1:] if t[0] == "p" else t[1]]
+                    for j in t[2]:
+                        after[j] = HOP
+                    if q == "p":
+                        for j in t[1][-1:]:
+                            after.setdefault(j, 0.0)
+                        t[1].append(i)
+                        continue
+                    t[1].append(i)
+                for a in wrote.get(name, []) + (read.get(name, []) if kind else []):
+                    if a[0] < hi and lo < a[1]:
+                        after[a[2]] = HOP
+        for (name, lo, hi, _) in reads:
+            read.setdefault(name, []).append((lo, hi, i))
+        for (name, lo, hi, _) in list(writes) + list(lands):
+            for d in (wrote, read):
+                d[name] = [a for a in d.get(name, []) if not (lo <= a[0] and a[1] <= hi)]
+            wrote[name].append((lo, hi, i))
+        after.pop(i, None)
+        calls.append({"q": q, "call": call, "args": args, "kw": kw, "reads": reads, "writes": writes, "sem": sem or "c" + q,
+                      "n": n, "busy": busy, "done": done or busy, "after": after})
+
+    def ref(x):
+        return x[3] if isinstance(x, tuple) else x
+
+    def refs(*xs):
+        return [x for x in xs if isinstance(x, tuple)]
+
+    def cost(n, rate=1.0):
+        return max(64.0, n * rate) * CYC
+
+    V, S, P = g.vector, g.scalar, g.tensor
+
+    def cp(out, in_):
+        op("v", V.tensor_copy, (out[3], in_[3]), [in_], [out], cost(width(out), 0.5 if narrow(out, in_) else 1))
+
+    def tt(out, a, b, o):
+        op("v", V.tensor_tensor, (out[3], a[3], b[3], o), [a, b], [out],
+           cost(width(out), 1 if a[0] in PSUM or b[0] in PSUM else 2))
+
+    def ts(out, a, s1, o1, *more):
+        s2 = more[0] if more else None
+        op("v", V.tensor_scalar, (out[3], a[3], ref(s1), ref(s2), o1) + more[1:], [a] + refs(s1, s2), [out],
+           cost(width(out), 0.5 if narrow(out, a) else 1))
+
+    def red(out, a, o):
+        op("v", V.tensor_reduce, (out[3], a[3], AxisListType.X, o), [a], [out], cost(width(a)))
+
+    def scan(out, d0, d1, init, o0, o1):
+        op("v", V.tensor_tensor_scan, (out[3], d0[3], d1[3], init, o0, o1), [d0, d1], [out], cost(width(out)))
+
+    def ms(out, c):
+        op("v", V.memset, (out[3], c), [], [out], cost(width(out), 0.5 if narrow(out) else 1))
+
+    def act(out, in_, func=F.Copy, scale=1.0, bias=None):
+        kw = {} if bias is None else {"bias": bias}
+        op("s", S.activation, (out[3], in_[3], func), [in_] + refs(scale), [out], cost(width(out)), scale=ref(scale), **kw)
+
+    def mm(out, l, r, start=False, stop=False):
+        op("p", P.matmul, (out[3], l[3], r[3], start, stop), [l, r], [out],
+           max(64, width(out)) * PCYC * (1 if narrow(l) else 4))
+
+    def tgather(out, win, off, in1, o):
+        op("v", V.tensor_tensor, (out[3], win[3].indirect(off[3]), in1[3], o), [win, off, in1], [out],
+           50 + width(out) * GATHER * CYC)
+
+    def sgather(out, win, off):
+        op("s", S.activation, (out[3], win[3].indirect(off[3]), F.Copy), [win, off], [out], 65 + width(out) * GATHER * CYC)
+
+    def scatter(win, off, in_):
+        op("v", V.tensor_copy, (win[3].indirect(off[3]), in_[3]), [in_, off], [win], 50 + width(in_) * SCATTER * CYC)
+
+    def dma(q, out, in_, reads, writes, sem, done):
+        op(q, queue[q].dma_start, (out, in_), reads, writes, 50.0, sem, 16, done)
+
+    dma("y", T.QS[:], T.qs[:], [], [R("QS")], "lqs", 2000.0)
+    dma("s", T.WT[:], T.wt[:], [], [R("WT")], "lwt", 2000.0)
+    dma("s", T.KI[:], T.kk[:], [], [R("KI")], "lki", 2000.0)
+    dma("y", T.X[:, 0:4096], T.x0[:], [], [R("X", 0, 4096)], "lx", 1999.0)
+
+    dst = T.cores[(rank + 1) % len(T.cores)]
+    src = T.cores[(rank - 1) % len(T.cores)]
+    rid, pid, _ = topo.addr(dst)
+
+    def mask_of(a, b):
+        return sum(1 << e for e in topo.engines(a, b)[::2])
+
+    def bits(m):
+        return bin(m).count("1")
+
+    POOL = ("pool", 0, 1, None)
+
+    def aff(out, in_, pattern, cmp, base, cm):
+        op("g", g.affine_select, (out[3], in_[3], pattern, cmp, 0.0, base, cm), [in_], [out, POOL],
+           170 + 2 * CYC * width(out))
+
+    def iota(out, pattern, base, cm):
+        kw = {} if SCRATCH[out[0]][2] == "int32" else {"allow_small_or_imprecise_dtypes": True}
+        op("g", g.iota, (out[3], pattern, base, cm), [], [out, POOL], 130 + 2 * CYC * width(out), **kw)
+
+    def row(p, lo, hi):
+        return ("KC", lo, hi, T.KC[p:p + 1, lo:hi])
+
+    def double(f, name, lo, w, n):
+        while w < n:
+            f(R(name, lo + w, lo + 2 * w), R(name, lo, lo + w))
+            w *= 2
+
+    def eight(s):
+        f = act if s else cp
+        f(R("Q8", 640 * s, 640 * s + 80), R("QS", 80 * s, 80 * s + 80))
+        double(f, "Q8", 640 * s, 80, 640)
+
+    def hashes(out, data, base, n, start=True):
+        for r in range(16):
+            mm(out, R("BW", 16 - r, 144 - r), R(data, base + r, base + 16 * n, 16), start and r == 0, r == 15)
+
+    def remainder(u, whole, frac, square):
+        ts(whole, u, FLOOR, O.add)
+        tt(frac, u, whole, O.subtract)
+        tt(square, frac, frac, O.mult)
+
+    def h_of(out, square):
+        ts(out, square, 2.0 ** 19, O.mult, -0.375, O.add)
+
+    def first_level(u, names, lo, hi, p1):
+        whole, frac, square, k, ku, hh, pm, p1u, p1f = [R(x, lo, hi) for x in names.split()]
+        remainder(u, whole, frac, square)
+        tt(ku, frac, k, O.mult)
+        h_of(hh, square)
+        tt(pm, hh, ku, O.add)
+        ts(p1, pm, 4095, O.bitwise_and)
+        cp(p1u, p1)
+        cp(p1f, p1)
+
+    def drawn(lo, hi):
+        first_level(R("pu", lo, hi), "T0 F0 SQ0 KR KU0 HH0 PM0 P1U P1F", lo, hi, R("P1I", lo, hi))
+
+    def parents(h, p1f):
+        n = 8 * NB[h]
+        act(R("pp", HALF[h], HALF[h] + n), p1f)
+        double(act, "pp", HALF[h], n, 8 * n)
+
+    ms(R("ONE"), 1.0)
+    ms(R("KC"), 0.0)
+    aff(R("T1"), R("ONE"), [[-16, 8], [0, 16]], O.is_ge, 0, 1)
+    aff(R("BD"), R("T1"), [[16, 8], [0, 16]], O.is_ge, 15, -1)
+    aff(R("ID"), R("ONE"), [[-1, 128]], O.is_equal, 0, 1)
+    ms(row(0, 0, 592), -MID)
+    for h in (0, 1):
+        n1 = 8 * NB[h]
+        at = CODE[h]
+        iota(row(32, at, at + n1), [[16, n1]], 16, 0)
+        iota(row(32, at + n1, at + 9 * n1), [[0, 8], [16, n1]], 1040, 0)
+        iota(row(64, at + n1, at + 9 * n1), [[1, 8], [0, n1]], 1, 0)
+        ms(row(32, at + 9 * n1, at + 9 * n1 + NB[h]), -MID)
+    iota(R("PI"), [[0, 1]], 0, 1)
+    iota(R("RW"), [[0, 16], [1, 16]], 0, 0)
+    aff(R("TRI"), R("BD"), [[1, 128]], O.is_ge, -1, -1)
+    iota(R("DM"), [[16, 16]], SENT + 16, 0)
+    iota(R("DM2"), [[16, 8]], 128, 0)
+
+    ms(R("B1"), 0.0)
+    ms(R("BW"), 0.0)
+    ms(R("X", 4096, XW), 512.0)
+    cp(R("B1", 16, 144, 16), R("BD", 0, 128, 16))
+    ts(R("BW", 16, 144, 16), R("B1", 16, 144, 16), R("WT"), O.mult, 2.0 ** -12, O.mult)
+    ts(R("B1", 16, 144, 16), R("B1", 16, 144, 16), 2048.0, O.mult)
+    eight(0)
+    hashes(R("pu", 0, 40), "Q8", 0, 40)
+    mm(R("ph", 0, 1), R("BD"), R("WT"), True, True)
+    ts(R("KF"), R("KI"), 4096.0, O.mult)
+    for l in range(5):
+        ts(R("KR", l, 40, 5), R("KI"), 4096.0, O.mult)
+    drawn(0, 40)
+    ts(R("W256"), R("ph", 0, 1), 2.0 ** -4, O.mult)
+    act(R("IDF"), R("ID"))
+    act(R("NI"), R("ID"), F.Copy, -1.0)
+    act(R("VI"), R("ID"), F.Copy, -BIG)
+    act(R("BDF"), R("BD"))
+    ts(R("ICI"), R("PI"), 15, O.bitwise_and)
+    cp(R("IC"), R("ICI"))
+    ts(R("MK"), R("RW"), R("IC"), O.is_equal)
+    ts(R("NM"), R("RW"), R("IC"), O.not_equal, -BIG, O.mult)
+    ms(R("R16"), 1.0)
+    ms(R("R32"), 1.0)
+    ms(R("C1", 0, 5), 40)
+    ms(R("C1", 5, 8), 24)
+    ms(R("R16", 0, 256, 16), 0.0)
+    ms(R("R32", 0, 256, 32), 0.0)
+    ts(R("DM"), R("DM"), R("IC"), O.add)
+    ts(R("DM2"), R("DM2"), R("IC"), O.add)
+    ms(R("TAB_0", 0, 1), SENT)
+    ms(R("TAB_1", 0, 1), SENT)
+    for l in range(3):
+        ts(R("KRA", l, 24, 3), R("KI"), 4096.0, O.mult)
+    for s in (1, 2, 3):
+        ms(R("SB%d" % s), 512.0)
+    PLACES = R("X", 0, XW)
+
+    def queries(h, s, lo=0, hi=None):
+        return R("Q8", 640 * s + lo, 640 * s + (hi or 640)) if h == 0 else R("QA", lo, hi or 384)
+
+    def tree(h, s):
+        nb = NB[h]
+        n = 8 * nb
+        pk = "pk%d" % h
+        B = lambda name, lo=0, hi=None, step=1: R("%s_%d" % (name, h), lo, hi, step)
+        u = R("pu", 0, n)
+        mm(u, R("IDF"), R("F0", 40 * s, 40 * s + 40) if h == 0 else R("FA"), True)
+        tgather(B("D1"), PLACES, R("P1U", 40 * s, 40 * s + 40) if h == 0 else R("P1UA"), queries(h, s), O.subtract)
+        hashes(u, "D1_%d" % h, 0, n, False)
+        act(B("A", 0, 16 * n), B("D1"), F.Abs)
+        mm(R(pk, 0, 9 * n + nb), R("ONE"), R("KC", CODE[h], CODE[h] + 9 * n + nb), True)
+        remainder(u, B("UI"), B("UF"), B("SQ"))
+        for k in (0, 1):
+            h_of(B("HH", k * n, k * n + n), B("SQ"))
+        for bank, b0, b1 in (("ph", 0, 2), ("pc", 2, 8)):
+            for b in range(b0, b1):
+                act(R(bank, (b - b0) * n, (b - b0 + 1) * n), B("UF"), F.Copy, R("KF", b, b + 1))
+            for b in range(b0, b1, 2):
+                tt(B("PM", b * n, (b + 2) * n), R(bank, (b - b0) * n, (b - b0 + 2) * n), B("HH"), O.add)
+            tab = B("TAB", 1 + n + b0 * n, 1 + n + b1 * n)
+            ts(tab, B("PM", b0 * n, b1 * n), 4095, O.bitwise_and)
+            cp(B("P2U", b0 * n, b1 * n), tab)
+        for r in range(16):
+            mm(R("ph", 0, n), R("B1", 16 - r, 144 - r), B("A", r, 16 * n, 16), r == 0, r == 15)
+        act(B("EM"), R("ph", 0, n), F.Relu, 2.0 ** 11, -4088.0 * 2.0 ** 22)
+        act(B("ZH"), R("ph", 0, n), F.Relu, -2.0 ** 14, HIT)
+        cuts = (0, 320, 640) if h == 0 else (0, 384)
+        turn = [0]
+
+        def child(b):
+            at = b * 16 * n
+            if b not in SHARE[h]:
+                c = CUT if h == 0 else 1
+                for k in range(c):
+                    lo, hi = k * n // c, (k + 1) * n // c
+                    tgather(B("D2", at + 16 * lo, at + 16 * hi), PLACES, B("P2U", b * n + lo, b * n + hi),
+                            queries(h, s, 16 * lo, 16 * hi), O.subtract)
+                act(B("A", at + 16 * n, at + 32 * n), B("D2", at, at + 16 * n), F.Abs)
+                return
+            sgather(B("D2", at, at + 16 * n), PLACES, B("P2U", b * n, b * n + n))
+            for lo, hi in zip(cuts, cuts[1:]):
+                stage = R("st%d" % (turn[0] % 2), 0, hi - lo)
+                turn[0] += 1
+                mm(stage, R("NI"), queries(h, s, lo, hi), True)
+                mm(stage, R("ID"), B("D2", at + lo, at + hi), False, True)
+                act(B("A", at + 16 * n + lo, at + 16 * n + hi), stage, F.Abs)
+
+        for b in range(8):
+            child(b)
+        tt(B("VD"), B("TAB", 1 + n, 1 + 9 * n), R("pp", HALF[h], HALF[h] + 8 * n), O.is_equal)
+        last = len(GROUPS[h]) - 1
+        for k, (blk, nblk) in enumerate(GROUPS[h]):
+            if k == last:
+                for b in range(8):
+                    mm(R(pk, (1 + b) * n, (2 + b) * n), R("NI"), B("EM"))
+                    mm(R(pk, 9 * n, 9 * n + nb), R("ID"), B("ZH", b * nb, b * nb + nb))
+                if h == 1:
+                    mm(R(pk, 9 * n, 9 * n + nb), R("ID"), R("QE"))
+                mm(R(pk, n, 9 * n), R("VI"), B("VD"))
+            for r in range(16):
+                mm(R(pk, blk * n, (blk + nblk) * n), R("B1", 16 - r, 144 - r),
+                   B("A", blk * 16 * n + r, (blk + nblk) * 16 * n, 16), False, k == last and r == 15)
+        for l in range(nb):
+            red(R("KM", 5 * h + l, 5 * h + l + 1), R(pk, l, 73 * nb, nb), O.max)
+
+    def arrivals(s):
+        for k in (0, 1):
+            act(R("QA", 48 * k, 48 * k + 48), R("AR%d" % s))
+        for k in (1, 2, 3):
+            act(R("QA", 96 * k, 96 * k + 96), R("QA", 0, 96))
+        hashes(R("pu", 0, 24), "QA", 0, 24)
+        first_level(R("pu", 0, 24), "TA FA SQA KRA KUA HHA PMA P1UA P1FA", 0, 24, R("TAB_1", 1, 25))
+        ts(R("QE"), R("pu", 0, 3), R("W256"), O.is_gt, HIT, O.mult)
+        parents(1, R("P1FA"))
+
+    def send(nl, s, blocked):
+        slot = R("ph", 0, nl)
+        tt(R("GO", 0, nl), blocked, R("GW", 0, nl), O.is_lt)
+        tt(R("BL", 0, nl), blocked, R("GC", 0, nl), O.min)
+        mm(slot, R("ID"), R("CW", 0, nl), True)
+        mm(slot, R("TRI"), R("GO", 0, nl))
+        for k in range(1, nl):
+            mm(R("ph", k, nl), R("BD"), R("GO", 0, nl - k))
+        mm(slot, R("ID"), R("BL", 0, nl), False, True)
+        cp(R("SU", 0, nl), slot)
+        scatter(R("SB%d" % s), R("SU", 0, nl), R("VIC", 0, 16 * nl))
+        m = mask_of(core, dst)
+        op("g", g.remote_dma, (T["AR%d" % s][:], T["SB%d" % s][:, 0:48], T.sem["arr%d" % s], T.sem["ls%d" % s], pid, rid, m),
+           [R("SB%d" % s, 0, 48)], [], 200.0, "ls%d" % s, bits(m), 2500.0, [R("AR%d" % s)])
+
+    for s in range(STEPS):
+        two = s > 0
+        more = s < STEPS - 1
+        nl = 8 if two else 5
+        w = 32 * nl
+        parents(0, R("P1F", 40 * s, 40 * s + 40))
+        cp(R("TAB_0", 1, 41), R("P1I", 40 * s, 40 * s + 40))
+        tree(0, s)
+        if two:
+            arrivals(s)
+            tree(1, s)
+        else:
+            for k in (1, 2, 3):
+                eight(k)
+            hashes(R("pu", 40, 160), "Q8", 640, 120)
+            double(act, "KR", 0, 40, 160)
+            drawn(40, 160)
+        cp(R("KMI", 0, nl), R("KM", 0, nl))
+        i1, iv = R("IX", 0, 2 * nl, 2), R("IX", 1, 2 * nl, 2)
+        ts(R("BI", 0, nl), R("KMI", 0, nl), 15, O.bitwise_and)
+        ts(i1, R("KMI", 0, nl), 4, O.arith_shift_right, 63, O.bitwise_and)
+        tt(R("BT", 0, nl), R("BI", 0, nl), R("C1", 0, nl), O.mult)
+        tt(iv, i1, R("BT", 0, nl), O.add)
+        cp(R("IU", 0, 2 * nl), R("IX", 0, 2 * nl))
+        tgather(R("E", 0, 160), R("TAB_0", 0, 361), R("IU", 0, 10), R("MK", 0, 160), O.mult)
+        if two:
+            tgather(R("E", 160, 256), R("TAB_1", 0, 217), R("IU", 10, 16), R("MK", 160, 256), O.mult)
+        mm(R("pu", 0, w), R("BDF"), R("E", 0, w), True, True)
+        scan(R("SC", 0, w), R("R16", 0, w), R("E", 0, w), 0.0, O.mult, O.add)
+        p1, pv = R("SC", 15, w, 32), R("SC", 31, w, 32)
+        cp(R("P16", 0, w), R("pu", 0, w))
+        cp(R("PU", 0, nl), p1)
+        act(R("VB", 0, 80), R("QS", 80 * s, 80 * s + 80))
+        if two:
+            act(R("VB", 80, 128), R("AR%d" % s))
+        sgather(R("VB", 16 * nl, 32 * nl), PLACES, R("PU", 0, nl))
+        if more:
+            cp(R("PU", 8, 8 + nl), pv)
+            sgather(R("VIC", 0, 16 * nl), PLACES, R("PU", 8, 8 + nl))
+            ts(R("GW", 0, nl), R("KM", 0, nl), 0.0, O.is_lt)
+            tt(R("GC", 0, nl), R("GW", 0, nl), R("DM2", 0, nl), O.mult)
+            tt(R("CW", 0, nl), R("DM2", 0, nl), R("GC", 0, nl), O.subtract)
+        cp(R("PZ", 0, nl), p1)
+        tt(R("L2", 0, nl), p1, pv, O.is_equal)
+        tt(R("L2", 0, nl), R("L2", 0, nl), R("DM", nl, 2 * nl), O.mult)
+        tt(R("PZ", nl, 2 * nl), R("L2", 0, nl), pv, O.max)
+        mm(R("pc", 0, w), R("ID"), R("NM", 0, w), True)
+        for l in range(nl):
+            for pa in range(2):
+                at = (2 * l + pa) * 256
+                k = w - 32 * l
+                own = R("SC", 32 * l + 16 * pa + 15, 32 * l + 16 * pa + 16)
+                ts(R("EQ", at, at + k), R("P16", 32 * l, w), own, O.is_equal, 8192.0, O.mult)
+                if l < nl - 1:
+                    mm(R("pc", 32 * l + 32, w), R("BD"), R("EQ", at + 32, at + k))
+                mm(R("pc", 32 * l, 32 * l + 32), R("TRI"), R("EQ", at, at + 32), False, l == nl - 1 and pa == 1)
+        scan(R("CS", 0, w), R("R32", 0, w), R("pc", 0, w), 0.0, O.mult, O.max)
+        blocked = R("CS", 31, w, 32)
+        tt(R("MM", 0, nl), blocked, R("DM", 0, nl), O.min)
+        tt(R("MM", nl, 2 * nl), blocked, R("DM", nl, 2 * nl), O.min)
+        tt(R("OF", 0, 2 * nl), R("MM", 0, 2 * nl), R("PZ", 0, 2 * nl), O.max)
+        cp(R("OU", 0, 2 * nl), R("OF", 0, 2 * nl))
+        scatter(PLACES, R("OU", 0, 2 * nl), R("VB", 0, 32 * nl))
+        if more:
+            send(nl, s + 1, blocked)
+    dma("y", T.y[:], T.X[:, 0:4096], [R("X", 0, 4096)], [], "sy", 5000.0)
+
+    count = {}
+    clock = {q: {} for q in queue}
+    seen = {}
+    for s in (1, 2, 3):
+        nm = "arr%d" % s
+        count[nm] = bits(mask_of(src, core))
+        seen["AR%d" % s] = [(0, 48, True, "remote", nm, count[nm], {})]
+
+    def wait(q, reads, writes):
+        need = []
+        for kind, rs in ((False, reads), (True, writes)):
+            for (name, lo, hi, _) in rs:
                 bank = name in PSUM
                 for a in seen.get(name, []):
                     if bank and a[3] != q:
@@ -80,8 +515,8 @@ def rank_program(g, core, T, topo):
         count[sem] = count.get(sem, 0) + n
         snap = dict(clock[q])
         snap[sem] = count[sem]
-        for kind, refs in ((False, reads), (True, writes)):
-            for (name, lo, hi, _) in refs:
+        for kind, rs in ((False, reads), (True, writes)):
+            for (name, lo, hi, _) in rs:
                 old = seen.get(name, [])
                 if name in PSUM:
                     old = [a for a in old if a[3] != q or (a[2] and not kind)]
@@ -92,469 +527,15 @@ def rank_program(g, core, T, topo):
                 old.append((lo, hi, kind, q, sem, count[sem], snap))
                 seen[name] = old
 
-    def op(q, call, args, reads, writes, sem=None, n=1, **kw):
-        order(q, reads, writes)
-        sem = sem or "c" + q
-        call(*args, **kw).then_inc(T.sem[sem], n)
-        note(q, reads, writes, sem, n)
-
-    def ref(x):
-        return x[3] if isinstance(x, tuple) else x
-
-    def refs(*xs):
-        return [x for x in xs if isinstance(x, tuple)]
-
-    V, S, P = g.vector, g.scalar, g.tensor
-
-    def cp(out, in_):
-        op("v", V.tensor_copy, (out[3], in_[3]), [in_], [out])
-
-    def tt(out, a, b, o):
-        op("v", V.tensor_tensor, (out[3], a[3], b[3], o), [a, b], [out])
-
-    def ts(out, a, s1, o1, *more):
-        s2 = more[0] if more else None
-        op("v", V.tensor_scalar, (out[3], a[3], ref(s1), ref(s2), o1) + more[1:], [a] + refs(s1, s2), [out])
-
-    def red(out, a, o):
-        op("v", V.tensor_reduce, (out[3], a[3], AxisListType.X, o), [a], [out])
-
-    def scan(out, d0, d1, init, o0, o1):
-        op("v", V.tensor_tensor_scan, (out[3], d0[3], d1[3], init, o0, o1), [d0, d1], [out])
-
-    def ms(out, c):
-        op("v", V.memset, (out[3], c), [], [out])
-
-    def act(out, in_, func, scale=1.0):
-        op("s", S.activation, (out[3], in_[3], func), [in_] + refs(scale), [out], scale=ref(scale))
-
-    def mm(out, l, r, start, stop):
-        op("p", P.matmul, (out[3], l[3], r[3], start, stop), [l, r], [out])
-
-    def tgather(out, win, off, in1, o):
-        op("v", V.tensor_tensor, (out[3], win[3].indirect(off[3]), in1[3], o), [win, off, in1], [out])
-
-    def sgather(out, win, off):
-        op("s", S.activation, (out[3], win[3].indirect(off[3]), F.Copy), [win, off], [out])
-
-    def scatter(win, off, in_):
-        op("v", V.tensor_copy, (win[3].indirect(off[3]), in_[3]), [in_, off], [win])
-
-    def run(tasks, orders):
-        at = {q: 0 for q in orders}
-        done = []
-        left = sum(len(orders[q]) for q in orders)
-        while left:
-            before = left
-            for q in orders:
-                while at[q] < len(orders[q]):
-                    label = orders[q][at[q]]
-                    want, f = tasks[label]
-                    if any(b not in done for b in want.split()):
-                        break
-                    f()
-                    done.append(label)
-                    at[q] += 1
-                    left -= 1
-            if left == before:
-                raise ValueError("the orders wait for one another")
-
-    op("y", g.sync.dma_start, (T.QS[:], T.qs[:]), [], [R("QS")], "lqs", 16)
-    op("s", S.dma_start, (T.WT[:], T.wt[:]), [], [R("WT")], "lwt", 16)
-    op("s", S.dma_start, (T.KI[:], T.kk[:]), [], [R("KI")], "lki", 16)
-    op("y", g.sync.dma_start, (T.X[:, 0:4096], T.x0[:]), [], [R("X", 0, 4096)], "lx", 16)
-
-    dst = T.cores[(rank + 1) % len(T.cores)]
-    src = T.cores[(rank - 1) % len(T.cores)]
-    rid, pid, _ = topo.addr(dst)
-
-    def mask_of(a, b):
-        return sum(1 << e for e in topo.engines(a, b)[::2])
-
-    def bits(m):
-        return bin(m).count("1")
-    for s in (1, 2, 3):
-        nm = "arr%d" % s
-        count[nm] = bits(mask_of(src, core))
-        seen["AR%d" % s] = [(0, 48, True, "remote", nm, count[nm], {})]
-
-    POOL = ("pool", 0, 1, None)
-
-    def aff(out, in_, pattern, cmp, base, cm):
-        op("g", g.affine_select, (out[3], in_[3], pattern, cmp, 0.0, base, cm), [in_], [out, POOL])
-
-    def iota(out, pattern, base, cm):
-        kw = {} if SCRATCH[out[0]][2] == "int32" else {"allow_small_or_imprecise_dtypes": True}
-        op("g", g.iota, (out[3], pattern, base, cm), [], [out, POOL], **kw)
-
-    def row(p, lo, hi):
-        return ("KC", lo, hi, T.KC[p:p + 1, lo:hi])
-
-    def double(f, name, lo, w, n, *a):
-        while w < n:
-            f(R(name, lo + w, lo + 2 * w), R(name, lo, lo + w), *a)
-            w *= 2
-
-    def eight(s):
-        more = (F.Copy,) if s else ()
-        f = act if s else cp
-        f(R("Q8", 640 * s, 640 * s + 80), R("QS", 80 * s, 80 * s + 80), *more)
-        double(f, "Q8", 640 * s, 80, 640, *more)
-
-    def hashes(out, data, base, width):
-        for r in range(16):
-            mm(out, R("BW", 16 - r, 144 - r), R(data, base + r, base + 16 * width, 16), r == 0, r == 15)
-
-    def drawn_hash(lo, hi):
-        cp(R("UI0", lo, hi), R("pu", lo, hi))
-        ts(R("UR0", lo, hi), R("UI0", lo, hi), 4095, O.bitwise_and)
-        tt(R("SQ0", lo, hi), R("UR0", lo, hi), R("UR0", lo, hi), O.mult)
-        tt(R("KU0", lo, hi), R("UR0", lo, hi), R("KR", lo, hi), O.mult)
-        ts(R("HH0", lo, hi), R("SQ0", lo, hi), 5, O.arith_shift_right)
-        tt(R("PM0", lo, hi), R("HH0", lo, hi), R("KU0", lo, hi), O.add)
-        ts(R("P1I", lo, hi), R("PM0", lo, hi), 4095, O.bitwise_and)
-        cp(R("P1U", lo, hi), R("P1I", lo, hi))
-        cp(R("P1F", lo, hi), R("P1I", lo, hi))
-
-    def parents(s):
-        act(R("pp", 0, 40), R("P1F", 40 * s, 40 * s + 40), F.Copy)
-        double(act, "pp", 0, 40, 320, F.Copy)
-
-    ms(R("ONE"), 1.0)
-    ms(R("KC"), 0.0)
-    aff(R("T1"), R("ONE"), [[-16, 8], [0, 16]], O.is_ge, 0, 1)
-    aff(R("BD"), R("T1"), [[16, 8], [0, 16]], O.is_ge, 15, -1)
-    aff(R("ID"), R("ONE"), [[-1, 128]], O.is_equal, 0, 1)
-    ms(row(0, 0, 576), -MID)
-    for h in (0, 1):
-        n1 = 8 * NB[h]
-        at = 360 * h
-        iota(row(32, at, at + n1), [[16, n1]], 16, 0)
-        iota(row(32, at + n1, at + 9 * n1), [[0, 8], [16, n1]], 1040, 0)
-        iota(row(64, at + n1, at + 9 * n1), [[1, 8], [0, n1]], 1, 0)
-    iota(R("PI"), [[0, 1]], 0, 1)
-    iota(R("RW"), [[0, 16], [1, 16]], 0, 0)
-    aff(R("TRI"), R("BD"), [[1, 128]], O.is_ge, -1, -1)
-    iota(R("DM"), [[16, 16]], 4096, 0)
-    iota(R("DM2"), [[16, 8]], 128, 0)
-
-    ms(R("B1"), 0.0)
-    ms(R("BW"), 0.0)
-    ms(R("X", 4096, XW), 512.0)
-    ms(R("ZR"), 0.0)
-    cp(R("B1", 16, 144, 16), R("BD", 0, 128, 16))
-    ts(R("BW", 16, 144, 16), R("B1", 16, 144, 16), R("WT"), O.mult)
-    eight(0)
-    hashes(R("pu", 0, 40), "Q8", 0, 40)
-    mm(R("ph", 0, 1), R("BD"), R("WT"), True, True)
-    cp(R("KF"), R("KI"))
-    for l in range(5):
-        cp(R("KR", l, 40, 5), R("KI"))
-    drawn_hash(0, 40)
-    ts(R("W256"), R("ph", 0, 1), 256.0, O.mult)
-    ts(R("B1", 16, 144, 16), R("B1", 16, 144, 16), 2048.0, O.mult)
-    for s in (1, 2, 3):
-        eight(s)
-    parents(0)
-    hashes(R("pu", 40, 160), "Q8", 640, 120)
-    act(R("NI"), R("ID"), F.Copy, -1.0)
-    act(R("VI"), R("ID"), F.Copy, -BIG)
-    act(R("BDF"), R("BD"), F.Copy)
-    double(act, "KR", 0, 40, 160, F.Copy)
-    ts(R("ICI"), R("PI"), 15, O.bitwise_and)
-    cp(R("IC"), R("ICI"))
-    ts(R("MK"), R("RW"), R("IC"), O.is_equal)
-    ms(R("HF", 0, 1), 1.0)
-    ms(R("HF", 1, 16, 2), 0.5)
-    ms(R("HF", 2, 16, 2), 0.25)
-    ms(R("Z16"), 0.0)
-    scan(R("PW"), R("HF"), R("Z16"), 1.0, O.mult, O.add)
-    tt(R("PX"), R("MK", 0, 16), R("PW"), O.mult)
-    red(R("PC"), R("PX"), O.add)
-    ts(R("PX", 0, 16, 2), R("PX", 0, 16, 2), 4.2, O.mult)
-    ts(R("PX", 1, 16, 2), R("PX", 1, 16, 2), 2.93, O.mult)
-    red(R("NC"), R("PX"), O.add)
-    ms(R("HF", 1, 8), 2.0 ** -24)
-    scan(R("PX", 0, 8), R("HF", 0, 8), R("Z16", 0, 8), 2.0 ** 84, O.mult, O.add)
-    ts(R("NX"), R("PX", 0, 8), R("NC"), O.mult)
-    PLACES = R("X", 0, XW)
-
-    def thresholds():
-        for l in range(8):
-            act(R("TH", 32 * l, 32 * l + 32), R("MK", 32 * l, 32 * l + 32), F.Copy, R("NX", l, l + 1))
-        act(R("LD"), R("BD"), F.Copy, R("PC"))
-
-    def constants1():
-        ts(R("NM"), R("MK"), 0.5, O.is_lt, 1e29, O.mult)
-        ms(R("R16"), 1.0)
-        ms(R("R32"), 0.0)
-        ms(R("C1", 0, 5), 40)
-        ms(R("C1", 5, 8), 24)
-        ms(R("R16", 0, 256, 16), 0.0)
-        ms(R("R32", 0, 256, 32), 1.0)
-        ts(R("DM"), R("DM"), R("IC"), O.add)
-        ts(R("DM2"), R("DM2"), R("IC"), O.add)
-        ms(R("TAB_0", 0, 1), SENT)
-
-    def constants2():
-        ms(R("TAB_1", 0, 1), SENT)
-        for l in range(3):
-            cp(R("KRA", l, 24, 3), R("KI"))
-        for s in (1, 2, 3):
-            ms(R("SB%d" % s, 0, 48), 512.0)
-        tt(R("TH"), R("TH"), R("NM"), O.max)
-
-    def queries(h, s, lo=0, hi=None):
-        return R("Q8", 640 * s + lo, 640 * s + (hi or 640)) if h == 0 else R("QA", lo, hi or 384)
-
-    def sums(h, blk, nblk):
-        n = 8 * NB[h]
-        for r in range(16):
-            mm(R("pk%d" % h, blk * n, (blk + nblk) * n), R("B1", 16 - r, 144 - r),
-               R("A_%d" % h, blk * 16 * n + r, (blk + nblk) * 16 * n, 16), False, False)
-
-    def gather1(h, s):
-        off = R("P1U", 40 * s, 40 * s + 40) if h == 0 else R("P1UA")
-        tgather(R("D1_%d" % h), PLACES, off, queries(h, s), O.subtract)
-
-    def codes(h):
-        n = 8 * NB[h]
-        mm(R("pk%d" % h, 0, 9 * n), R("ONE"), R("KC", 360 * h, 360 * h + 9 * n), True, False)
-
-    def remainder(h, s):
-        n = 8 * NB[h]
-        uq = R("UI0", 40 * s, 40 * s + 40) if h == 0 else R("UIA")
-        tt(R("UI", 0, n), R("pu", 0, n), uq, O.add)
-        ts(R("UR", 0, n), R("UI", 0, n), 4095, O.bitwise_and)
-        cp(R("UF", 0, n), R("UR", 0, n))
-
-    def multiples(h):
-        n = 8 * NB[h]
-        for b in range(8):
-            act(R("st%d" % (b // 4), (b % 4) * n, (b % 4 + 1) * n), R("UF", 0, n), F.Copy, R("KF", b, b + 1))
-
-    def squares(h):
-        n = 8 * NB[h]
-        tt(R("SQ", 0, n), R("UR", 0, n), R("UR", 0, n), O.mult)
-        ts(R("HH", 0, n), R("SQ", 0, n), 5, O.arith_shift_right)
-        double(cp, "HH", 0, n, 4 * n)
-        ts(R("EM_%d" % h, 0, n), R("UI", 0, n), R("W256"), O.is_gt)
-
-    def offsets(h, half):
-        n = 8 * NB[h]
-        lo, hi = half * 4 * n, half * 4 * n + 4 * n
-        tab = R("TAB_%d" % h, 1 + n + lo, 1 + n + hi)
-        tt(R("PM", lo, hi), R("st%d" % half, 0, 4 * n), R("HH", 0, 4 * n), O.add)
-        ts(tab, R("PM", lo, hi), 4095, O.bitwise_and)
-        cp(R("P2U", lo, hi), tab)
-
-    def vgather2(h, s, b):
-        n = 8 * NB[h]
-        tgather(R("D2_%d" % h, b * 16 * n, (b + 1) * 16 * n), PLACES, R("P2U", b * n, b * n + n), queries(h, s), O.subtract)
-
-    def sgather2(h, b):
-        n = 8 * NB[h]
-        sgather(R("D2_%d" % h, b * 16 * n, (b + 1) * 16 * n), PLACES, R("P2U", b * n, b * n + n))
-
-    def pieces(h):
-        return (0, 320, 640) if h == 0 else (0, 384)
-
-    def stage(h, b, k):
-        c = pieces(h)
-        return R("st%d" % ((k + SHARE[h].index(b)) % 2), 0, c[k + 1] - c[k])
-
-    def psub2(h, s, b):
-        at = b * 128 * NB[h]
-        c = pieces(h)
-        for k in range(len(c) - 1):
-            mm(stage(h, b, k), R("NI"), queries(h, s, c[k], c[k + 1]), True, False)
-            mm(stage(h, b, k), R("ID"), R("D2_%d" % h, at + c[k], at + c[k + 1]), False, True)
-
-    def abs_of_psum(h, b):
-        at = (1 + b) * 128 * NB[h]
-        c = pieces(h)
-        for k in range(len(c) - 1):
-            act(R("A_%d" % h, at + c[k], at + c[k + 1]), stage(h, b, k), F.Abs)
-
-    def abs2(h, b):
-        n = 128 * NB[h]
-        act(R("A_%d" % h, (1 + b) * n, (2 + b) * n), R("D2_%d" % h, b * n, b * n + n), F.Abs)
-
-    def eightfold(h):
-        double(act, "EM_%d" % h, 0, 8 * NB[h], 64 * NB[h], F.Copy)
-
-    def void(h, name):
-        n = 8 * NB[h]
-        mm(R("pk%d" % h, n, 9 * n), R("VI"), R("%s_%d" % (name, h)), False, False)
-
-    def same(h):
-        n = 8 * NB[h]
-        tt(R("VD_%d" % h), R("TAB_%d" % h, 1 + n, 1 + 9 * n), R("pp", HALF[h], HALF[h] + 8 * n), O.is_equal)
-
-    def close(h):
-        mm(R("pk%d" % h, 0, 8), R("ID"), R("ZR"), False, True)
-
-    def hits(h):
-        n = 8 * NB[h]
-        ts(R("ZH", 40 * h, 40 * h + n), R("pk%d" % h, 0, n), 2048.0 - MID, O.is_lt)
-
-    def phits(h):
-        nb = NB[h]
-        l0 = 5 * h
-        for a in range(8):
-            z = R("ZH", 40 * h + a * nb, 40 * h + a * nb + nb)
-            mm(R("ph", l0, l0 + nb), R("ID"), z, a == 0, a == 7 and h == 0)
-        if h == 1:
-            mm(R("ph", l0, l0 + nb), R("ID"), R("QE"), False, True)
-
-    def largest(h, l):
-        nb = NB[h]
-        red(R("KM", 5 * h + l, 5 * h + l + 1), R("pk%d" % h, l, 9 * 8 * nb, nb), O.max)
-
-    def arrivals(s):
-        act(R("QA", 0, 48), R("AR%d" % s), F.Copy)
-        double(act, "QA", 0, 48, 384, F.Copy)
-
-    def arrivals_hash():
-        p1 = R("TAB_1", 1, 25)
-        cp(R("UIA"), R("pu", 0, 24))
-        ts(R("URA"), R("UIA"), 4095, O.bitwise_and)
-        tt(R("SQA"), R("URA"), R("URA"), O.mult)
-        tt(R("KUA"), R("URA"), R("KRA"), O.mult)
-        ts(R("HHA"), R("SQA"), 5, O.arith_shift_right)
-        tt(R("PMA"), R("HHA"), R("KUA"), O.add)
-        ts(p1, R("PMA"), 4095, O.bitwise_and)
-        cp(R("P1UA"), p1)
-        cp(R("P1FA"), p1)
-        ts(R("QE"), R("UIA", 0, 3), R("W256"), O.is_gt)
-
-    def arrivals_parents():
-        act(R("pp", 320, 344), R("P1FA"), F.Copy)
-        double(act, "pp", 320, 24, 192, F.Copy)
-
-    def ranks(nl):
-        mm(R("ph", 16, 16 + nl), R("TRI"), R("GO", 0, nl), True, False)
-        for k in range(1, nl):
-            mm(R("ph", 16 + k, 16 + nl), R("BD"), R("GO", 0, nl - k), False, False)
-        mm(R("ph", 16, 16 + nl), R("NI"), R("DM2", 0, nl), False, True)
-
-    def send_slots(nl, s):
-        tt(R("SL", 0, nl), R("ph", 16, 16 + nl), R("GO", 0, nl), O.mult)
-        tt(R("SL", 0, nl), R("SL", 0, nl), R("DM2", 0, nl), O.add)
-        cp(R("SU", 0, nl), R("SL", 0, nl))
-        scatter(R("SB%d" % s), R("SU", 0, nl), R("VIC", 0, 16 * nl))
-        m = mask_of(core, dst)
-        order("g", [R("SB%d" % s, 0, 48)], [])
-        g.remote_dma(T["AR%d" % s][:], T["SB%d" % s][:, 0:48], T.sem["arr%d" % s], T.sem["ls%d" % s], pid, rid, m)
-        note("g", [R("SB%d" % s, 0, 48)], [], "ls%d" % s, bits(m))
-
-    for s in range(STEPS):
-        two = s > 0
-        more = s < STEPS - 1
-        nl = 8 if two else 5
-        was = 8 if s > 1 else 5
-        tasks = {}
-
-        def task(label, before, f, *args):
-            tasks[label] = (before, lambda: f(*args))
-
-        for h in (0, 1):
-            H = "DA"[h]
-            n = 8 * NB[h]
-            task(H + "1", "", gather1, h, s)
-            task(H + "a", H + "1", act, R("A_%d" % h, 0, 16 * n), R("D1_%d" % h), F.Abs)
-            task(H + "U", H + "1", hashes, R("pu", 0, n), "D1_%d" % h, 0, n)
-            task("code" + H, "", codes, h)
-            task(H + "u", H + "U", remainder, h, s)
-            task(H + "k", H + "u", multiples, h)
-            task(H + "q", H + "u", squares, h)
-            task(H + "e8", H + "q", eightfold, h)
-            task(H + "e", H + "e8", void, h, "EM")
-            for half in (0, 1):
-                task(H + "o%d" % half, H + "k " + H + "q", offsets, h, half)
-            for b in range(8):
-                o = H + "o%d" % (b // 4)
-                task(H + "v%d" % b, o, vgather2, h, s, b)
-                task(H + "g%d" % b, o, sgather2, h, b)
-                task(H + "d%d" % b, H + "g%d" % b, psub2, h, s, b)
-                task(H + "a%d" % b, H + "v%d" % b, abs2, h, b)
-                task(H + "t%d" % b, H + "d%d" % b, abs_of_psum, h, b)
-            for blk, k in ((0, 3), (3, 2), (5, 2), (7, 2)) if h == 0 else ((0, 3), (3, 3), (6, 3)):
-                want = [H + ("t" if b in SHARE[h] else "a") + str(b) for b in range(max(blk - 1, 0), blk + k - 1)]
-                task(H + "s%d" % blk, " ".join(want + [H + "a"]), sums, h, blk, k)
-            task(H + "x", H + "o1" + (" pr" if h else ""), same, h)
-            task(H + "p", H + "x", void, h, "VD")
-            task(H + "z", "", close, h)
-            task(H + "h", H + "z", hits, h)
-            task(H + "H", H + "h", phits, h)
-            for l in range(NB[h]):
-                task(H + "l%d" % l, H + "z", largest, h, l)
-        task("dh", "", drawn_hash, 40, 160)
-        task("con", "", constants1)
-        task("th", "", thresholds)
-        task("tab", "", cp, R("TAB_0", 1, 41), R("P1I", 40 * s, 40 * s + 40))
-        task("send", "", send_slots, was, s)
-        task("arr", "", arrivals, s)
-        task("AQ", "arr", hashes, R("pu", 0, 24), "QA", 0, 24)
-        task("ah", "AQ", arrivals_hash)
-        task("pr", "ah", arrivals_parents)
-        if two:
-            ranks(was)
-        run(tasks, {"v": VORD[two].split(), "s": SORD[two].split(), "p": PORD[two].split()})
-        w = 32 * nl
-        ts(R("LV", 0, nl), R("ph", 0, nl), 0.5, O.is_lt)
-        tt(R("KMI", 0, nl), R("KM", 0, nl), R("LV", 0, nl), O.mult)
-        i1, iv = R("IX", 0, 2 * nl, 2), R("IX", 1, 2 * nl, 2)
-        ts(R("BI", 0, nl), R("KMI", 0, nl), 15, O.bitwise_and)
-        ts(i1, R("KMI", 0, nl), 4, O.arith_shift_right, 63, O.bitwise_and)
-        tt(R("BT", 0, nl), R("BI", 0, nl), R("C1", 0, nl), O.mult)
-        tt(iv, i1, R("BT", 0, nl), O.add)
-        cp(R("IU", 0, 2 * nl), R("IX", 0, 2 * nl))
-        tgather(R("E", 0, 160), R("TAB_0", 0, 361), R("IU", 0, 10), R("MK", 0, 160), O.mult)
-        if two:
-            tgather(R("E", 160, 256), R("TAB_1", 0, 217), R("IU", 10, 16), R("MK", 160, 256), O.mult)
-        mm(R("pp", 0, w), R("BDF"), R("E", 0, w), True, True)
-        scan(R("SC", 0, w), R("R16", 0, w), R("E", 0, w), 0.0, O.mult, O.add)
-        p1, pv = R("SC", 15, w, 32), R("SC", 31, w, 32)
-        cp(R("PU", 0, nl), p1)
-        if more:
-            cp(R("PU", 8, 8 + nl), pv)
-        act(R("VB", 0, 80), R("QS", 80 * s, 80 * s + 80), F.Copy)
-        if two:
-            act(R("VB", 80, 128), R("AR%d" % s), F.Copy)
-        sgather(R("VB", 16 * nl, 32 * nl), PLACES, R("PU", 0, nl))
-        if more:
-            sgather(R("VIC", 0, 16 * nl), PLACES, R("PU", 8, 8 + nl))
-        tt(R("PD", 0, nl), p1, R("DM", 0, nl), O.subtract)
-        tt(R("PD", nl, 2 * nl), pv, R("DM", nl, 2 * nl), O.subtract)
-        tt(R("L2", 0, nl), p1, pv, O.not_equal)
-        if more:
-            ts(R("GW", 0, nl), R("KMI", 0, nl), 0, O.is_lt)
-        tt(R("PD", nl, 2 * nl), R("PD", nl, 2 * nl), R("L2", 0, nl), O.mult)
-        if not two:
-            constants2()
-        cp(R("P16", 0, w), R("pp", 0, w))
-        for l in range(nl):
-            for pa in range(2):
-                at = (2 * l + pa) * 256
-                k = w - 32 * l
-                own = R("SC", 32 * l + 16 * pa + 15, 32 * l + 16 * pa + 16)
-                ts(R("EQ", at, at + k), R("P16", 32 * l, w), own, O.is_equal, 2.0 ** (84 - 24 * l), O.mult)
-                mm(R("pc", 32 * l, w), R("LD"), R("EQ", at, at + k), l == 0 and pa == 0, l == nl - 1 and pa == 1)
-        tt(R("PD", 0, nl), R("PD", 0, nl), R("LV", 0, nl), O.mult)
-        if more:
-            parents(s + 1)
-        tt(R("CM", 0, w), R("pc", 0, w), R("TH", 0, w), O.is_lt)
-        scan(R("CS", 0, w), R("R32", 0, w), R("CM", 0, w), 0.0, O.max, O.min)
-        go = R("CS", 31, w, 32)
-        tt(R("OF", 0, nl), go, R("PD", 0, nl), O.mult)
-        tt(R("OF", nl, 2 * nl), go, R("PD", nl, 2 * nl), O.mult)
-        tt(R("OF", 0, 2 * nl), R("OF", 0, 2 * nl), R("DM", 0, 2 * nl), O.add)
-        cp(R("OU", 0, 2 * nl), R("OF", 0, 2 * nl))
-        scatter(PLACES, R("OU", 0, 2 * nl), R("VB", 0, 32 * nl))
-        if more:
-            tt(R("GO", 0, nl), go, R("GW", 0, nl), O.mult)
-    op("y", g.sync.dma_start, (T.y[:], T.X[:, 0:4096]), [R("X", 0, 4096)], [], "sy", 16)
+    if not ORDER:
+        ORDER.extend(arrange(calls))
+    for i in ORDER:
+        c = calls[i]
+        wait(c["q"], c["reads"], c["writes"])
+        done = c["call"](*c["args"], **c["kw"])
+        if not c["sem"].startswith("ls"):
+            done.then_inc(T.sem[c["sem"]], c["n"])
+        note(c["q"], c["reads"], c["writes"], c["sem"], c["n"])
     for sem in count:
         if clock["y"].get(sem, 0) < count[sem]:
             g.sync.wait_ge(T.sem[sem], count[sem])

@@ -7,12 +7,17 @@ FLOOR = -0.5 + 2.0 ** -13
 SENT = 4096
 XW = 4368
 NB = (5, 3)
-SHARE = ((1, 3, 5), (2,))
+SHARE = ((1, 3), (1, 3))
 GROUPS = (((0, 2), (2, 3), (5, 2), (7, 2)), ((0, 3), (3, 3), (6, 3)))
-CUT = 1
+SHARE0 = (1, 4)
+FIRST = (20, 12)
+CUT = (2, 1)
+LAST = (1, 2)
+RINT = True
+EARLY = 0.0
 STEPS = 4
-HOP = 150.0
-PATIENCE = 0.5
+HOP = 180.0
+PATIENCE = 0.2
 PASSES = 6
 PCYC = 0.5
 CYC, GATHER, SCATTER = 0.83, 1.56, 3.8
@@ -21,14 +26,14 @@ SCRATCH = {}
 for _dt, _names in (
         ("bfloat16", "X:4368 QS:320 WT:1 Q8:2560 QA:384 AR1:48 AR2:48 AR3:48 SB1:384 SB2:384 SB3:384 ONE:128 T1:128 BD:128 "
                      "ID:128 NI:128 VI:128 TRI:128 B1:160 BW:160 KC:592 DM2:8 QE:3 D1_0:640 D1_1:384 D2_0:5120 "
-                     "D2_1:3072 A_0:5760 A_1:3456 VD_0:320 VD_1:192 EM_0:40 EM_1:24 ZH_0:40 ZH_1:24 EQ:4096 VB:256 VIC:128 "
-                     "GO:8 BL:8 CW:8 NM:256"),
+                     "D2_1:3072 A_0:5760 A_1:3456 VD_0:320 VD_1:192 EM_0:40 EM_1:24 ZH_0:40 ZH_1:24 EQ:3136 VB_0:160 VB_1:96 "
+                     "VIC:128 GO:8 BL:8 GC:8 NM:256 ZR:32"),
         ("float32", "KF:8 W256:1 BDF:128 IDF:128 IC:1 RW:256 MK:256 DM:16 R16:256 R32:256 KR:160 F0:160 SQ0:160 KU0:160 "
-                    "P1F:160 KRA:24 FA:24 SQA:24 KUA:24 P1FA:24 UF_0:40 UF_1:24 SQ_0:40 SQ_1:24 KM:8 E:256 SC:256 PZ:16 "
-                    "L2:8 CS:256 MM:16 OF:16 GW:8 GC:8"),
+                    "P1F:160 KRA:24 FA:24 SQA:24 KUA:24 P1FA:24 UF_0:40 UF_1:24 SQ_0:40 SQ_1:24 KM:8 E:256 SC:256 "
+                    "PZ_0:10 PZ_1:6 L2:8 CS:256 MM_0:10 MM_1:6 OF_0:10 OF_1:6 GW:8"),
         ("int32", "KI:8 PI:1 ICI:1 C1:8 T0:160 HH0:160 PM0:160 P1I:160 TA:24 HHA:24 PMA:24 UI_0:40 UI_1:24 HH_0:80 HH_1:48 "
                   "PM_0:320 PM_1:192 TAB_0:400 TAB_1:240 KMI:8 BI:8 BT:8 IX:16"),
-        ("uint16", "P1U:160 P1UA:24 P2U_0:320 P2U_1:192 IU:16 PU:16 P16:256 OU:16 SU:8")):
+        ("uint16", "P1U:160 P1UA:24 P2U_0:320 P2U_1:192 IU:16 PU_0:16 PU_1:16 P16:256 OU_0:10 OU_1:6 SU:8")):
     for _n in _names.split():
         SCRATCH[_n.split(":")[0]] = ("sbuf", [128, int(_n.split(":")[1])], _dt)
 PSUM = "pu pk0 pk1 pp pc ph st0 st1".split()
@@ -79,7 +84,7 @@ def arrange(calls):
         urge[i] = calls[i]["done"] + max([gap + urge[k] for k, gap in after[i]] + [0.0])
     best = None
     for _ in range(PASSES):
-        out, end = place(calls, before, after, urge)
+        out, end = place(calls, before, after, [u + c.get("early", 0.0) for u, c in zip(urge, calls)])
         if best is None or max(end) < best[0]:
             best = (max(end), out)
         urge = place(calls, after, before, end)[1]
@@ -194,7 +199,8 @@ def rank_program(g, core, T, topo):
     dma("y", T.QS[:], T.qs[:], [], [R("QS")], "lqs", 2000.0)
     dma("s", T.WT[:], T.wt[:], [], [R("WT")], "lwt", 2000.0)
     dma("s", T.KI[:], T.kk[:], [], [R("KI")], "lki", 2000.0)
-    dma("y", T.X[:, 0:4096], T.x0[:], [], [R("X", 0, 4096)], "lx", 1999.0)
+    dma("y", T.X[:, 0:4096], T.x0[:], [], [R("X", 0, 4096)], "lx", 6000.0)
+    calls[-1]["after"][0] = -2000.0
 
     dst = T.cores[(rank + 1) % len(T.cores)]
     src = T.cores[(rank - 1) % len(T.cores)]
@@ -251,8 +257,8 @@ def rank_program(g, core, T, topo):
         cp(p1u, p1)
         cp(p1f, p1)
 
-    def drawn(lo, hi):
-        first_level(R("pu", lo, hi), "T0 F0 SQ0 KR KU0 HH0 PM0 P1U P1F", lo, hi, R("P1I", lo, hi))
+    def drawn(bank, lo, hi):
+        first_level(R(bank, lo, hi), "T0 F0 SQ0 KR KU0 HH0 PM0 P1U P1F", lo, hi, R("P1I", lo, hi))
 
     def parents(h, p1f):
         n = 8 * NB[h]
@@ -278,6 +284,7 @@ def rank_program(g, core, T, topo):
     iota(R("DM"), [[16, 16]], SENT + 16, 0)
     iota(R("DM2"), [[16, 8]], 128, 0)
 
+    ms(R("ZR"), 0.0)
     ms(R("B1"), 0.0)
     ms(R("BW"), 0.0)
     ms(R("X", 4096, XW), 512.0)
@@ -290,7 +297,12 @@ def rank_program(g, core, T, topo):
     ts(R("KF"), R("KI"), 4096.0, O.mult)
     for l in range(5):
         ts(R("KR", l, 40, 5), R("KI"), 4096.0, O.mult)
-    drawn(0, 40)
+    drawn("pu", 0, 40)
+    for k in (1, 2, 3):
+        eight(k)
+    hashes(R("pk1", 40, 160), "Q8", 640, 120)
+    double(act, "KR", 0, 40, 160)
+    drawn("pk1", 40, 160)
     ts(R("W256"), R("ph", 0, 1), 2.0 ** -4, O.mult)
     act(R("IDF"), R("ID"))
     act(R("NI"), R("ID"), F.Copy, -1.0)
@@ -325,10 +337,26 @@ def rank_program(g, core, T, topo):
         pk = "pk%d" % h
         B = lambda name, lo=0, hi=None, step=1: R("%s_%d" % (name, h), lo, hi, step)
         u = R("pu", 0, n)
-        mm(u, R("IDF"), R("F0", 40 * s, 40 * s + 40) if h == 0 else R("FA"), True)
-        tgather(B("D1"), PLACES, R("P1U", 40 * s, 40 * s + 40) if h == 0 else R("P1UA"), queries(h, s), O.subtract)
+        turn = [0]
+
+        def less_q(out, data, at, lo, hi):
+            stage = R("st%d" % (turn[0] % 2), 0, hi - lo)
+            turn[0] += 1
+            mm(stage, R("NI"), queries(h, s, lo, hi), True)
+            mm(stage, R("ID"), B(data, at + lo, at + hi), False, True)
+            act(B("A", out + lo, out + hi), stage, F.Abs)
+
+        f, p1u, at = ("F0", "P1U", 40 * s) if h == 0 else ("FA", "P1UA", 0)
+        m = n - FIRST[h]
+        mm(R("pu", 0, m), R("IDF"), R(f, at, at + m), True)
+        tgather(B("D1", 0, 16 * m), PLACES, R(p1u, at, at + m), queries(h, s, 0, 16 * m), O.subtract)
+        if m < n:
+            mm(R("pu", m, n), R("ID"), R("ZR", 0, n - m))
+            sgather(B("D1", 16 * m, 16 * n), PLACES, R(p1u, at + m, at + n))
         hashes(u, "D1_%d" % h, 0, n, False)
-        act(B("A", 0, 16 * n), B("D1"), F.Abs)
+        act(B("A", 0, 16 * m), B("D1", 0, 16 * m), F.Abs)
+        if m < n:
+            less_q(0, "D1", 0, 16 * m, 16 * n)
         mm(R(pk, 0, 9 * n + nb), R("ONE"), R("KC", CODE[h], CODE[h] + 9 * n + nb), True)
         remainder(u, B("UI"), B("UF"), B("SQ"))
         for k in (0, 1):
@@ -346,25 +374,23 @@ def rank_program(g, core, T, topo):
         act(B("EM"), R("ph", 0, n), F.Relu, 2.0 ** 11, -4088.0 * 2.0 ** 22)
         act(B("ZH"), R("ph", 0, n), F.Relu, -2.0 ** 14, HIT)
         cuts = (0, 320, 640) if h == 0 else (0, 384)
-        turn = [0]
 
         def child(b):
             at = b * 16 * n
-            if b not in SHARE[h]:
-                c = CUT if h == 0 else 1
+            if b not in (SHARE[h] if s else SHARE0):
+                c = CUT[h] if b < 7 else LAST[h]
                 for k in range(c):
                     lo, hi = k * n // c, (k + 1) * n // c
                     tgather(B("D2", at + 16 * lo, at + 16 * hi), PLACES, B("P2U", b * n + lo, b * n + hi),
                             queries(h, s, 16 * lo, 16 * hi), O.subtract)
-                act(B("A", at + 16 * n, at + 32 * n), B("D2", at, at + 16 * n), F.Abs)
+                    if b == 7:
+                        act(B("A", at + 16 * (n + lo), at + 16 * (n + hi)), B("D2", at + 16 * lo, at + 16 * hi), F.Abs)
+                if b < 7:
+                    act(B("A", at + 16 * n, at + 32 * n), B("D2", at, at + 16 * n), F.Abs)
                 return
             sgather(B("D2", at, at + 16 * n), PLACES, B("P2U", b * n, b * n + n))
             for lo, hi in zip(cuts, cuts[1:]):
-                stage = R("st%d" % (turn[0] % 2), 0, hi - lo)
-                turn[0] += 1
-                mm(stage, R("NI"), queries(h, s, lo, hi), True)
-                mm(stage, R("ID"), B("D2", at + lo, at + hi), False, True)
-                act(B("A", at + 16 * n + lo, at + 16 * n + hi), stage, F.Abs)
+                less_q(at + 16 * n, "D2", at, lo, hi)
 
         for b in range(8):
             child(b)
@@ -382,7 +408,7 @@ def rank_program(g, core, T, topo):
                 mm(R(pk, blk * n, (blk + nblk) * n), R("B1", 16 - r, 144 - r),
                    B("A", blk * 16 * n + r, (blk + nblk) * 16 * n, 16), False, k == last and r == 15)
         for l in range(nb):
-            red(R("KM", 5 * h + l, 5 * h + l + 1), R(pk, l, 73 * nb, nb), O.max)
+            red(R("KMI" if RINT else "KM", 5 * h + l, 5 * h + l + 1), R(pk, l, 73 * nb, nb), O.max)
 
     def arrivals(s):
         for k in (0, 1):
@@ -398,7 +424,8 @@ def rank_program(g, core, T, topo):
         slot = R("ph", 0, nl)
         tt(R("GO", 0, nl), blocked, R("GW", 0, nl), O.is_lt)
         tt(R("BL", 0, nl), blocked, R("GC", 0, nl), O.min)
-        mm(slot, R("ID"), R("CW", 0, nl), True)
+        mm(slot, R("ID"), R("DM2", 0, nl), True)
+        mm(slot, R("NI"), R("GC", 0, nl))
         mm(slot, R("TRI"), R("GO", 0, nl))
         for k in range(1, nl):
             mm(R("ph", k, nl), R("BD"), R("GO", 0, nl - k))
@@ -409,71 +436,77 @@ def rank_program(g, core, T, topo):
         op("g", g.remote_dma, (T["AR%d" % s][:], T["SB%d" % s][:, 0:48], T.sem["arr%d" % s], T.sem["ls%d" % s], pid, rid, m),
            [R("SB%d" % s, 0, 48)], [], 200.0, "ls%d" % s, bits(m), 2500.0, [R("AR%d" % s)])
 
-    for s in range(STEPS):
-        two = s > 0
+    def commit(h, s):
         more = s < STEPS - 1
-        nl = 8 if two else 5
-        w = 32 * nl
+        nb = NB[h]
+        l0 = 5 * h
+        l1, lo, hi = l0 + nb, 32 * l0, 32 * (l0 + nb)
+        B = lambda name, lo=0, hi=None, step=1: R("%s_%d" % (name, h), lo, hi, step)
+        L = lambda name: R(name, l0, l1)
+        W = lambda name: R(name, lo, hi)
+        rows, meet = R("pu", 0, hi - lo), ("pc", "ph")[h]
+        if not RINT:
+            cp(L("KMI"), L("KM"))
+        i1, iv = R("IX", 2 * l0, 2 * l1, 2), R("IX", 2 * l0 + 1, 2 * l1, 2)
+        ts(L("BI"), L("KMI"), 15, O.bitwise_and)
+        ts(i1, L("KMI"), 4, O.arith_shift_right, 63, O.bitwise_and)
+        tt(L("BT"), L("BI"), L("C1"), O.mult)
+        tt(iv, i1, L("BT"), O.add)
+        cp(R("IU", 2 * l0, 2 * l1), R("IX", 2 * l0, 2 * l1))
+        tgather(W("E"), B("TAB", 0, 1 + 72 * nb), R("IU", 2 * l0, 2 * l1), W("MK"), O.mult)
+        mm(rows, R("BDF"), W("E"), True, True)
+        scan(W("SC"), W("R16"), W("E"), 0.0, O.mult, O.add)
+        p1, pv = R("SC", lo + 15, hi, 32), R("SC", lo + 31, hi, 32)
+        cp(W("P16"), rows)
+        cp(B("PU", 0, nb), p1)
+        act(B("VB", 0, 16 * nb), R("QS", 80 * s, 80 * s + 80) if h == 0 else R("AR%d" % s))
+        sgather(B("VB", 16 * nb, 32 * nb), PLACES, B("PU", 0, nb))
+        if more:
+            cp(B("PU", 8, 8 + nb), pv)
+            sgather(R("VIC", 16 * l0, 16 * l1), PLACES, B("PU", 8, 8 + nb))
+            ts(L("GW"), L("KMI"), 0.0, O.is_lt)
+            tt(L("GC"), L("GW"), L("DM2"), O.mult)
+        act(B("PZ", 0, nb), p1)
+        tt(L("L2"), p1, pv, O.is_equal)
+        tt(L("L2"), L("L2"), R("DM", nb, 2 * nb), O.mult)
+        tt(B("PZ", nb, 2 * nb), L("L2"), pv, O.max)
+        mm(R(meet, 0, hi - lo), R("ID"), W("NM"), True)
+        at = 1600 * h
+        for l in range(l1):
+            for pa in range(2):
+                c = max(32 * l, lo)
+                own = R("SC", 32 * l + 16 * pa + 15, 32 * l + 16 * pa + 16)
+                ts(R("EQ", at, at + hi - c), R("P16", c, hi), own, O.is_equal, 8192.0, O.mult)
+                d = 32 if l >= l0 else 0
+                if l < l1 - 1:
+                    mm(R(meet, c + d - lo, hi - lo), R("BD"), R("EQ", at + d, at + hi - c))
+                if d:
+                    mm(R(meet, c - lo, c + d - lo), R("TRI"), R("EQ", at, at + d), False, l == l1 - 1 and pa == 1)
+                at += hi - lo
+        scan(W("CS"), W("R32"), R(meet, 0, hi - lo), 0.0, O.mult, O.max)
+        blocked = R("CS", lo + 31, hi, 32)
+        tt(B("MM", 0, nb), blocked, R("DM", 0, nb), O.min)
+        tt(B("MM", nb, 2 * nb), blocked, R("DM", nb, 2 * nb), O.min)
+        tt(B("OF", 0, 2 * nb), B("MM", 0, 2 * nb), B("PZ", 0, 2 * nb), O.max)
+        cp(B("OU", 0, 2 * nb), B("OF", 0, 2 * nb))
+        scatter(PLACES, B("OU", 0, 2 * nb), B("VB", 0, 32 * nb))
+
+    for s in range(STEPS):
+        nl = 8 if s else 5
         parents(0, R("P1F", 40 * s, 40 * s + 40))
         cp(R("TAB_0", 1, 41), R("P1I", 40 * s, 40 * s + 40))
         tree(0, s)
-        if two:
+        if s:
             arrivals(s)
             tree(1, s)
-        else:
-            for k in (1, 2, 3):
-                eight(k)
-            hashes(R("pu", 40, 160), "Q8", 640, 120)
-            double(act, "KR", 0, 40, 160)
-            drawn(40, 160)
-        cp(R("KMI", 0, nl), R("KM", 0, nl))
-        i1, iv = R("IX", 0, 2 * nl, 2), R("IX", 1, 2 * nl, 2)
-        ts(R("BI", 0, nl), R("KMI", 0, nl), 15, O.bitwise_and)
-        ts(i1, R("KMI", 0, nl), 4, O.arith_shift_right, 63, O.bitwise_and)
-        tt(R("BT", 0, nl), R("BI", 0, nl), R("C1", 0, nl), O.mult)
-        tt(iv, i1, R("BT", 0, nl), O.add)
-        cp(R("IU", 0, 2 * nl), R("IX", 0, 2 * nl))
-        tgather(R("E", 0, 160), R("TAB_0", 0, 361), R("IU", 0, 10), R("MK", 0, 160), O.mult)
-        if two:
-            tgather(R("E", 160, 256), R("TAB_1", 0, 217), R("IU", 10, 16), R("MK", 160, 256), O.mult)
-        mm(R("pu", 0, w), R("BDF"), R("E", 0, w), True, True)
-        scan(R("SC", 0, w), R("R16", 0, w), R("E", 0, w), 0.0, O.mult, O.add)
-        p1, pv = R("SC", 15, w, 32), R("SC", 31, w, 32)
-        cp(R("P16", 0, w), R("pu", 0, w))
-        cp(R("PU", 0, nl), p1)
-        act(R("VB", 0, 80), R("QS", 80 * s, 80 * s + 80))
-        if two:
-            act(R("VB", 80, 128), R("AR%d" % s))
-        sgather(R("VB", 16 * nl, 32 * nl), PLACES, R("PU", 0, nl))
-        if more:
-            cp(R("PU", 8, 8 + nl), pv)
-            sgather(R("VIC", 0, 16 * nl), PLACES, R("PU", 8, 8 + nl))
-            ts(R("GW", 0, nl), R("KM", 0, nl), 0.0, O.is_lt)
-            tt(R("GC", 0, nl), R("GW", 0, nl), R("DM2", 0, nl), O.mult)
-            tt(R("CW", 0, nl), R("DM2", 0, nl), R("GC", 0, nl), O.subtract)
-        cp(R("PZ", 0, nl), p1)
-        tt(R("L2", 0, nl), p1, pv, O.is_equal)
-        tt(R("L2", 0, nl), R("L2", 0, nl), R("DM", nl, 2 * nl), O.mult)
-        tt(R("PZ", nl, 2 * nl), R("L2", 0, nl), pv, O.max)
-        mm(R("pc", 0, w), R("ID"), R("NM", 0, w), True)
-        for l in range(nl):
-            for pa in range(2):
-                at = (2 * l + pa) * 256
-                k = w - 32 * l
-                own = R("SC", 32 * l + 16 * pa + 15, 32 * l + 16 * pa + 16)
-                ts(R("EQ", at, at + k), R("P16", 32 * l, w), own, O.is_equal, 8192.0, O.mult)
-                if l < nl - 1:
-                    mm(R("pc", 32 * l + 32, w), R("BD"), R("EQ", at + 32, at + k))
-                mm(R("pc", 32 * l, 32 * l + 32), R("TRI"), R("EQ", at, at + 32), False, l == nl - 1 and pa == 1)
-        scan(R("CS", 0, w), R("R32", 0, w), R("pc", 0, w), 0.0, O.mult, O.max)
-        blocked = R("CS", 31, w, 32)
-        tt(R("MM", 0, nl), blocked, R("DM", 0, nl), O.min)
-        tt(R("MM", nl, 2 * nl), blocked, R("DM", nl, 2 * nl), O.min)
-        tt(R("OF", 0, 2 * nl), R("MM", 0, 2 * nl), R("PZ", 0, 2 * nl), O.max)
-        cp(R("OU", 0, 2 * nl), R("OF", 0, 2 * nl))
-        scatter(PLACES, R("OU", 0, 2 * nl), R("VB", 0, 32 * nl))
-        if more:
-            send(nl, s + 1, blocked)
+        at = len(calls)
+        commit(0, s)
+        if s:
+            for c in calls[at:-1]:
+                c["early"] = EARLY
+            commit(1, s)
+        if s < STEPS - 1:
+            send(nl, s + 1, R("CS", 31, 32 * nl, 32))
     dma("y", T.y[:], T.X[:, 0:4096], [R("X", 0, 4096)], [], "sy", 5000.0)
 
     count = {}

@@ -1,46 +1,60 @@
 from concourse.mybir import AluOpType as O, AxisListType, ActivationFunctionType as F
 
-BIG = float(2 ** 24)
-MID = float(2 ** 23)
-HIT = float(2 ** 25)
+BIG = float(2 ** 27)
+MID = float(2 ** 26)
+HIT = float(2 ** 28)
 FLOOR = -0.5 + 2.0 ** -13
 SENT = 4096
 XW = 4368
 NB = (5, 3)
 SHARE = ((1, 3), (1, 3))
 GROUPS = (((0, 2), (2, 3), (5, 2), (7, 2)), ((0, 3), (3, 3), (6, 3)))
-SHARE0 = (1, 4)
+SHARE0 = (0, 2)
 FIRST = (20, 12)
 CUT = (2, 1)
 LAST = (1, 2)
 RINT = True
-EARLY = 0.0
+SPLIT = True
+MERGE = True
+DIRECT = True
+INORDER = ""
+SIGNS = ((), ())
+SIGNS0 = ()
+TTU16 = True
+ANDU16 = False
+KPE = (False, False)
+PPE = (False, False)
+VOIDAT = (2, 1)
+REMOTE = 2200.0
+ENG = 2
+LEAD = {"Dpathv": 2000.0, "Dpathp": 2000.0, "Dmeetv": 2000.0, "Dmeetp": 2000.0}
 STEPS = 4
-HOP = 180.0
+HOP = 230.0
 PATIENCE = 0.2
 PASSES = 6
-PCYC = 0.5
-CYC, GATHER, SCATTER = 0.83, 1.56, 3.8
+PCYC = 0.45
+GATHER = 1.3
+CYC, SCATTER = 0.83, 3.8
 
 SCRATCH = {}
 for _dt, _names in (
         ("bfloat16", "X:4368 QS:320 WT:1 Q8:2560 QA:384 AR1:48 AR2:48 AR3:48 SB1:384 SB2:384 SB3:384 ONE:128 T1:128 BD:128 "
-                     "ID:128 NI:128 VI:128 TRI:128 B1:160 BW:160 KC:592 DM2:8 QE:3 D1_0:640 D1_1:384 D2_0:5120 "
-                     "D2_1:3072 A_0:5760 A_1:3456 VD_0:320 VD_1:192 EM_0:40 EM_1:24 ZH_0:40 ZH_1:24 EQ:3136 VB_0:160 VB_1:96 "
+                     "ID:128 NI:128 VI:128 TRI:128 B1:160 BW:160 KC:648 DM2:8 QE:3 D1_0:640 D1_1:384 D2_0:5120 "
+                     "D2_1:3072 A_0:5760 A_1:3456 VD_0:320 VD_1:192 EM_0:40 EM_1:24 ZH_0:40 ZH_1:24 EQ:6272 BDP:128 BDN:128 TRP:128 TRN:128 VB_0:160 VB_1:96 "
                      "VIC:128 GO:8 BL:8 GC:8 NM:256 ZR:32"),
-        ("float32", "KF:8 W256:1 BDF:128 IDF:128 IC:1 RW:256 MK:256 DM:16 R16:256 R32:256 KR:160 F0:160 SQ0:160 KU0:160 "
+        ("float32", "KF:8 KQ:8 KD:1024 W256:1 BDF:128 IDF:128 IC:1 RW:256 MK:256 DM:16 R16:256 R32:256 KR:160 F0:160 SQ0:160 KU0:160 "
                     "P1F:160 KRA:24 FA:24 SQA:24 KUA:24 P1FA:24 UF_0:40 UF_1:24 SQ_0:40 SQ_1:24 KM:8 E:256 SC:256 "
-                    "PZ_0:10 PZ_1:6 L2:8 CS:256 MM_0:10 MM_1:6 OF_0:10 OF_1:6 GW:8"),
-        ("int32", "KI:8 PI:1 ICI:1 C1:8 T0:160 HH0:160 PM0:160 P1I:160 TA:24 HHA:24 PMA:24 UI_0:40 UI_1:24 HH_0:80 HH_1:48 "
-                  "PM_0:320 PM_1:192 TAB_0:400 TAB_1:240 KMI:8 BI:8 BT:8 IX:16"),
-        ("uint16", "P1U:160 P1UA:24 P2U_0:320 P2U_1:192 IU:16 PU_0:16 PU_1:16 P16:256 OU_0:10 OU_1:6 SU:8")):
+                    "SG:20 PZ:8 L2:8 CS:256 MM_0:10 MM_1:6 OF_0:10 OF_1:6 GW:8"),
+        ("int32", "KI:8 PI:1 ICI:1 T0:160 HH0:160 PM0:160 P1I:160 TA:24 HHA:24 PMA:24 UI_0:40 UI_1:24 HH_0:80 HH_1:48 "
+                  "PM_0:320 PM_1:192 TAB_0:1600 TAB_1:240 KMI:8 BI:8 BT:8 IX:16"),
+        ("uint16", "P1U:160 P1UA:24 P2U_0:320 P2U_1:192 IU:16 PU_0:16 PU_1:16 P16:256 OU_0:10 OU_1:6 SU:10")):
     for _n in _names.split():
         SCRATCH[_n.split(":")[0]] = ("sbuf", [128, int(_n.split(":")[1])], _dt)
 PSUM = "pu pk0 pk1 pp pc ph st0 st1".split()
 for _n in PSUM:
     SCRATCH[_n] = ("psum", [128, 512], "float32")
 HALF = (0, 320)
-CODE = (0, 368)
+CODE = (0, 400)
 SEMAPHORES = "cv cs cp cg lqs lwt lki lx sy arr1 arr2 arr3 ls1 ls2 ls3".split()
 
 
@@ -101,11 +115,18 @@ def rank_program(g, core, T, topo):
     queue = {"v": g.vector, "s": g.scalar, "p": g.tensor, "g": g, "y": g.sync}
     calls = []
     wrote, read, turns = {}, {}, {}
+    phase = ["con"]
 
     def R(name, lo=0, hi=None, step=1):
         if hi is None:
             hi = T[name].shape[1]
-        return (name, lo, hi, T[name][:, lo:hi:step] if step != 1 else T[name][:, lo:hi])
+        return (name, lo, hi, T[name][:, lo:hi:step] if step != 1 else T[name][:, lo:hi], step)
+
+    def meets(a, lo, hi, step):
+        return a[0] < hi and lo < a[1] and not (a[-1] == step and (a[0] - lo) % step)
+
+    def within(a, lo, hi, step):
+        return lo <= a[0] and a[1] <= hi and (step == 1 or a[-1] == step and not (a[0] - lo) % step)
 
     def width(r):
         return r[3].shape[1]
@@ -117,7 +138,7 @@ def rank_program(g, core, T, topo):
         i = len(calls)
         after = {}
         for kind, refs in ((False, reads), (True, list(writes) + list(lands))):
-            for (name, lo, hi, _) in refs:
+            for (name, lo, hi, _, step) in refs:
                 if name in PSUM:
                     t = turns.setdefault(name, [q, [], []])
                     if t[0] != q:
@@ -131,16 +152,19 @@ def rank_program(g, core, T, topo):
                         continue
                     t[1].append(i)
                 for a in wrote.get(name, []) + (read.get(name, []) if kind else []):
-                    if a[0] < hi and lo < a[1]:
-                        after[a[2]] = HOP
-        for (name, lo, hi, _) in reads:
-            read.setdefault(name, []).append((lo, hi, i))
-        for (name, lo, hi, _) in list(writes) + list(lands):
+                    if meets(a, lo, hi, step):
+                        if kind and q in INORDER and calls[a[2]]["q"] == q:
+                            after.setdefault(a[2], 0.0)
+                        else:
+                            after[a[2]] = HOP
+        for (name, lo, hi, _, step) in reads:
+            read.setdefault(name, []).append((lo, hi, i, step))
+        for (name, lo, hi, _, step) in list(writes) + list(lands):
             for d in (wrote, read):
-                d[name] = [a for a in d.get(name, []) if not (lo <= a[0] and a[1] <= hi)]
-            wrote[name].append((lo, hi, i))
+                d[name] = [a for a in d.get(name, []) if not within(a, lo, hi, step)]
+            wrote[name].append((lo, hi, i, step))
         after.pop(i, None)
-        calls.append({"q": q, "call": call, "args": args, "kw": kw, "reads": reads, "writes": writes, "sem": sem or "c" + q,
+        calls.append({"early": LEAD.get(phase[0] + q, 0.0), "q": q, "call": call, "args": args, "kw": kw, "reads": reads, "writes": writes, "sem": sem or "c" + q,
                       "n": n, "busy": busy, "done": done or busy, "after": after})
 
     def ref(x):
@@ -176,8 +200,8 @@ def rank_program(g, core, T, topo):
         op("v", V.memset, (out[3], c), [], [out], cost(width(out), 0.5 if narrow(out) else 1))
 
     def act(out, in_, func=F.Copy, scale=1.0, bias=None):
-        kw = {} if bias is None else {"bias": bias}
-        op("s", S.activation, (out[3], in_[3], func), [in_] + refs(scale), [out], cost(width(out)), scale=ref(scale), **kw)
+        kw = {} if bias is None else {"bias": ref(bias)}
+        op("s", S.activation, (out[3], in_[3], func), [in_] + refs(scale, bias), [out], cost(width(out)), scale=ref(scale), **kw)
 
     def mm(out, l, r, start=False, stop=False):
         op("p", P.matmul, (out[3], l[3], r[3], start, stop), [l, r], [out],
@@ -207,12 +231,12 @@ def rank_program(g, core, T, topo):
     rid, pid, _ = topo.addr(dst)
 
     def mask_of(a, b):
-        return sum(1 << e for e in topo.engines(a, b)[::2])
+        return sum(1 << e for e in topo.engines(a, b)[::ENG])
 
     def bits(m):
         return bin(m).count("1")
 
-    POOL = ("pool", 0, 1, None)
+    POOL = ("pool", 0, 1, None, 1)
 
     def aff(out, in_, pattern, cmp, base, cm):
         op("g", g.affine_select, (out[3], in_[3], pattern, cmp, 0.0, base, cm), [in_], [out, POOL],
@@ -223,7 +247,7 @@ def rank_program(g, core, T, topo):
         op("g", g.iota, (out[3], pattern, base, cm), [], [out, POOL], 130 + 2 * CYC * width(out), **kw)
 
     def row(p, lo, hi):
-        return ("KC", lo, hi, T.KC[p:p + 1, lo:hi])
+        return ("KC", lo, hi, T.KC[p:p + 1, lo:hi], 1)
 
     def double(f, name, lo, w, n):
         while w < n:
@@ -232,8 +256,11 @@ def rank_program(g, core, T, topo):
 
     def eight(s):
         f = act if s else cp
-        f(R("Q8", 640 * s, 640 * s + 80), R("QS", 80 * s, 80 * s + 80))
-        double(f, "Q8", 640 * s, 80, 640)
+        at = 640 * s
+        for k in (0, 1):
+            f(R("Q8", at + 80 * k, at + 80 * k + 80), R("QS", 80 * s, 80 * s + 80))
+        for k in (1, 2, 3):
+            f(R("Q8", at + 160 * k, at + 160 * k + 160), R("Q8", at, at + 160))
 
     def hashes(out, data, base, n, start=True):
         for r in range(16):
@@ -247,14 +274,20 @@ def rank_program(g, core, T, topo):
     def h_of(out, square):
         ts(out, square, 2.0 ** 19, O.mult, -0.375, O.add)
 
+    def place_of(pm, whole, offsets):
+        if ANDU16:
+            ts(offsets, pm, 4095, O.bitwise_and)
+        ts(whole, pm, 4095, O.bitwise_and)
+        if not ANDU16:
+            cp(offsets, whole)
+
     def first_level(u, names, lo, hi, p1):
         whole, frac, square, k, ku, hh, pm, p1u, p1f = [R(x, lo, hi) for x in names.split()]
         remainder(u, whole, frac, square)
         tt(ku, frac, k, O.mult)
         h_of(hh, square)
         tt(pm, hh, ku, O.add)
-        ts(p1, pm, 4095, O.bitwise_and)
-        cp(p1u, p1)
+        place_of(pm, p1, p1u)
         cp(p1f, p1)
 
     def drawn(bank, lo, hi):
@@ -262,6 +295,10 @@ def rank_program(g, core, T, topo):
 
     def parents(h, p1f):
         n = 8 * NB[h]
+        if PPE[h]:
+            for b in range(8):
+                mm(R("pp", HALF[h] + b * n, HALF[h] + b * n + n), R("IDF"), p1f, b == 0, b == 7)
+            return
         act(R("pp", HALF[h], HALF[h] + n), p1f)
         double(act, "pp", HALF[h], n, 8 * n)
 
@@ -270,19 +307,21 @@ def rank_program(g, core, T, topo):
     aff(R("T1"), R("ONE"), [[-16, 8], [0, 16]], O.is_ge, 0, 1)
     aff(R("BD"), R("T1"), [[16, 8], [0, 16]], O.is_ge, 15, -1)
     aff(R("ID"), R("ONE"), [[-1, 128]], O.is_equal, 0, 1)
-    ms(row(0, 0, 592), -MID)
+    iota(R("PI"), [[0, 1]], 0, 1)
+    iota(R("DM"), [[16, 16]], SENT + 16, 0)
+    iota(R("DM2"), [[16, 8]], 128, 0)
+    iota(R("RW"), [[0, 16], [1, 16]], 0, 0)
+    aff(R("TRI"), R("BD"), [[1, 128]], O.is_ge, -1, -1)
+    ms(row(0, 0, 648), -MID)
     for h in (0, 1):
         n1 = 8 * NB[h]
         at = CODE[h]
-        iota(row(32, at, at + n1), [[16, n1]], 16, 0)
-        iota(row(32, at + n1, at + 9 * n1), [[0, 8], [16, n1]], 1040, 0)
-        iota(row(64, at + n1, at + 9 * n1), [[1, 8], [0, n1]], 1, 0)
-        ms(row(32, at + 9 * n1, at + 9 * n1 + NB[h]), -MID)
-    iota(R("PI"), [[0, 1]], 0, 1)
-    iota(R("RW"), [[0, 16], [1, 16]], 0, 0)
-    aff(R("TRI"), R("BD"), [[1, 128]], O.is_ge, -1, -1)
-    iota(R("DM"), [[16, 16]], SENT + 16, 0)
-    iota(R("DM2"), [[16, 8]], 128, 0)
+        a, b = ((128, 8), (256, 24))[h]
+        iota(row(32, at, at + n1), [[a, n1]], a, 0)
+        iota(row(32, at + n1, at + 9 * n1), [[0, 8], [a, n1]], 8192 + a, 0)
+        iota(row(64, at + n1, at + 9 * n1), [[b, 8], [0, n1]], b, 0)
+        ms(row(32, at + 9 * n1, at + 10 * n1), -MID)
+    ms(row(32, 640, 643), MID)
 
     ms(R("ZR"), 0.0)
     ms(R("B1"), 0.0)
@@ -290,7 +329,7 @@ def rank_program(g, core, T, topo):
     ms(R("X", 4096, XW), 512.0)
     cp(R("B1", 16, 144, 16), R("BD", 0, 128, 16))
     ts(R("BW", 16, 144, 16), R("B1", 16, 144, 16), R("WT"), O.mult, 2.0 ** -12, O.mult)
-    ts(R("B1", 16, 144, 16), R("B1", 16, 144, 16), 2048.0, O.mult)
+    ts(R("B1", 16, 144, 16), R("B1", 16, 144, 16), 2.0 ** 14, O.mult)
     eight(0)
     hashes(R("pu", 0, 40), "Q8", 0, 40)
     mm(R("ph", 0, 1), R("BD"), R("WT"), True, True)
@@ -305,31 +344,40 @@ def rank_program(g, core, T, topo):
     drawn("pk1", 40, 160)
     ts(R("W256"), R("ph", 0, 1), 2.0 ** -4, O.mult)
     act(R("IDF"), R("ID"))
+    for b in range(8 if any(KPE) else 0):
+        act(R("KD", 128 * b, 128 * b + 128), R("ID"), F.Copy, R("KF", b, b + 1))
     act(R("NI"), R("ID"), F.Copy, -1.0)
     act(R("VI"), R("ID"), F.Copy, -BIG)
     act(R("BDF"), R("BD"))
+    for name, of, c in (("BDP", "BD", 4096.0), ("BDN", "BD", -4096.0), ("TRP", "TRI", 4096.0), ("TRN", "TRI", -4096.0)):
+        act(R(name), R(of), F.Copy, c)
     ts(R("ICI"), R("PI"), 15, O.bitwise_and)
     cp(R("IC"), R("ICI"))
     ts(R("MK"), R("RW"), R("IC"), O.is_equal)
     ts(R("NM"), R("RW"), R("IC"), O.not_equal, -BIG, O.mult)
     ms(R("R16"), 1.0)
     ms(R("R32"), 1.0)
-    ms(R("C1", 0, 5), 40)
-    ms(R("C1", 5, 8), 24)
     ms(R("R16", 0, 256, 16), 0.0)
     ms(R("R32", 0, 256, 32), 0.0)
     ts(R("DM"), R("DM"), R("IC"), O.add)
     ts(R("DM2"), R("DM2"), R("IC"), O.add)
-    ms(R("TAB_0", 0, 1), SENT)
+    ms(R("TAB_0", 0, 1600, 400), SENT)
+    for s in range(STEPS):
+        cp(R("TAB_0", 400 * s + 1, 400 * s + 41), R("P1I", 40 * s, 40 * s + 40))
     ms(R("TAB_1", 0, 1), SENT)
-    for l in range(3):
+    for l in range(0 if DIRECT else 3):
         ts(R("KRA", l, 24, 3), R("KI"), 4096.0, O.mult)
+    ts(R("KQ"), R("KI"), -4096.0, O.add, 32.0, O.mult)
     for s in (1, 2, 3):
         ms(R("SB%d" % s), 512.0)
     PLACES = R("X", 0, XW)
 
     def queries(h, s, lo=0, hi=None):
         return R("Q8", 640 * s + lo, 640 * s + (hi or 640)) if h == 0 else R("QA", lo, hi or 384)
+
+    def table(h, s, lo, hi):
+        at = 0 if h else 400 * s
+        return R("TAB_%d" % h, at + lo, at + hi)
 
     def tree(h, s):
         nb = NB[h]
@@ -338,6 +386,8 @@ def rank_program(g, core, T, topo):
         B = lambda name, lo=0, hi=None, step=1: R("%s_%d" % (name, h), lo, hi, step)
         u = R("pu", 0, n)
         turn = [0]
+        H = "DA"[h] if s else "0"
+        phase[0] = H + "one"
 
         def less_q(out, data, at, lo, hi):
             stage = R("st%d" % (turn[0] % 2), 0, hi - lo)
@@ -348,35 +398,49 @@ def rank_program(g, core, T, topo):
 
         f, p1u, at = ("F0", "P1U", 40 * s) if h == 0 else ("FA", "P1UA", 0)
         m = n - FIRST[h]
-        mm(R("pu", 0, m), R("IDF"), R(f, at, at + m), True)
+        if h and DIRECT:
+            for r in range(16):
+                mm(R("pu", 0, m), R("BW", 16 - r, 144 - r), R("QA", r, 16 * m, 16), r == 0)
+        else:
+            mm(R("pu", 0, m), R("IDF"), R(f, at, at + m), True)
         tgather(B("D1", 0, 16 * m), PLACES, R(p1u, at, at + m), queries(h, s, 0, 16 * m), O.subtract)
         if m < n:
             mm(R("pu", m, n), R("ID"), R("ZR", 0, n - m))
             sgather(B("D1", 16 * m, 16 * n), PLACES, R(p1u, at + m, at + n))
         hashes(u, "D1_%d" % h, 0, n, False)
+        hashed = len(calls) - 1
+        phase[0] = H + "abs1"
         act(B("A", 0, 16 * m), B("D1", 0, 16 * m), F.Abs)
         if m < n:
             less_q(0, "D1", 0, 16 * m, 16 * n)
-        mm(R(pk, 0, 9 * n + nb), R("ONE"), R("KC", CODE[h], CODE[h] + 9 * n + nb), True)
+        phase[0] = H + "hash"
+        keys = 10 * n + h * nb
+        mm(R(pk, 0, keys), R("ONE"), R("KC", CODE[h], CODE[h] + keys), True)
+        calls[-1]["after"].setdefault(hashed, 0.0)
         remainder(u, B("UI"), B("UF"), B("SQ"))
         for k in (0, 1):
             h_of(B("HH", k * n, k * n + n), B("SQ"))
         for bank, b0, b1 in (("ph", 0, 2), ("pc", 2, 8)):
+            phase[0] = H + ("rest" if b0 else "hash")
             for b in range(b0, b1):
-                act(R(bank, (b - b0) * n, (b - b0 + 1) * n), B("UF"), F.Copy, R("KF", b, b + 1))
+                if KPE[h]:
+                    mm(R(bank, (b - b0) * n, (b - b0 + 1) * n), R("KD", 128 * b, 128 * b + 128), B("UF"), b == b0, b == b1 - 1)
+                else:
+                    act(R(bank, (b - b0) * n, (b - b0 + 1) * n), B("UF"), F.Copy, R("KF", b, b + 1))
             for b in range(b0, b1, 2):
                 tt(B("PM", b * n, (b + 2) * n), R(bank, (b - b0) * n, (b - b0 + 2) * n), B("HH"), O.add)
-            tab = B("TAB", 1 + n + b0 * n, 1 + n + b1 * n)
-            ts(tab, B("PM", b0 * n, b1 * n), 4095, O.bitwise_and)
-            cp(B("P2U", b0 * n, b1 * n), tab)
+            tab = table(h, s, 1 + n + b0 * n, 1 + n + b1 * n)
+            place_of(B("PM", b0 * n, b1 * n), tab, B("P2U", b0 * n, b1 * n))
+        phase[0] = H + "void"
         for r in range(16):
             mm(R("ph", 0, n), R("B1", 16 - r, 144 - r), B("A", r, 16 * n, 16), r == 0, r == 15)
-        act(B("EM"), R("ph", 0, n), F.Relu, 2.0 ** 11, -4088.0 * 2.0 ** 22)
+        act(B("EM"), R("ph", 0, n), F.Relu, 2.0 ** 11, -4088.0 * 2.0 ** 25)
         act(B("ZH"), R("ph", 0, n), F.Relu, -2.0 ** 14, HIT)
         cuts = (0, 320, 640) if h == 0 else (0, 384)
 
         def child(b):
             at = b * 16 * n
+            phase[0] = H + "two"
             if b not in (SHARE[h] if s else SHARE0):
                 c = CUT[h] if b < 7 else LAST[h]
                 for k in range(c):
@@ -388,53 +452,81 @@ def rank_program(g, core, T, topo):
                 if b < 7:
                     act(B("A", at + 16 * n, at + 32 * n), B("D2", at, at + 16 * n), F.Abs)
                 return
+            phase[0] = H + "sg"
             sgather(B("D2", at, at + 16 * n), PLACES, B("P2U", b * n, b * n + n))
+            phase[0] = H + "sub"
             for lo, hi in zip(cuts, cuts[1:]):
                 less_q(at + 16 * n, "D2", at, lo, hi)
 
         for b in range(8):
             child(b)
-        tt(B("VD"), B("TAB", 1 + n, 1 + 9 * n), R("pp", HALF[h], HALF[h] + 8 * n), O.is_equal)
+        phase[0] = H + "sum"
+        tt(B("VD"), table(h, s, 1 + n, 1 + 9 * n), R("pp", HALF[h], HALF[h] + 8 * n), O.is_equal)
         last = len(GROUPS[h]) - 1
         for k, (blk, nblk) in enumerate(GROUPS[h]):
-            if k == last:
+            if k == VOIDAT[h]:
                 for b in range(8):
                     mm(R(pk, (1 + b) * n, (2 + b) * n), R("NI"), B("EM"))
-                    mm(R(pk, 9 * n, 9 * n + nb), R("ID"), B("ZH", b * nb, b * nb + nb))
+                mm(R(pk, 9 * n, 10 * n), R("ID"), B("ZH"))
                 if h == 1:
-                    mm(R(pk, 9 * n, 9 * n + nb), R("ID"), R("QE"))
+                    mm(R(pk, 10 * n, keys), R("VI"), R("QE"))
+            if k == last:
                 mm(R(pk, n, 9 * n), R("VI"), B("VD"))
             for r in range(16):
                 mm(R(pk, blk * n, (blk + nblk) * n), R("B1", 16 - r, 144 - r),
                    B("A", blk * 16 * n + r, (blk + nblk) * 16 * n, 16), False, k == last and r == 15)
+        phase[0] = H + "path"
         for l in range(nb):
-            red(R("KMI" if RINT else "KM", 5 * h + l, 5 * h + l + 1), R(pk, l, 73 * nb, nb), O.max)
+            red(R("KMI" if RINT else "KM", 5 * h + l, 5 * h + l + 1), R(pk, l, keys, nb), O.max)
 
     def arrivals(s):
         for k in (0, 1):
             act(R("QA", 48 * k, 48 * k + 48), R("AR%d" % s))
         for k in (1, 2, 3):
             act(R("QA", 96 * k, 96 * k + 96), R("QA", 0, 96))
-        hashes(R("pu", 0, 24), "QA", 0, 24)
-        first_level(R("pu", 0, 24), "TA FA SQA KRA KUA HHA PMA P1UA P1FA", 0, 24, R("TAB_1", 1, 25))
-        ts(R("QE"), R("pu", 0, 3), R("W256"), O.is_gt, HIT, O.mult)
+        if DIRECT:
+            u = R("pu", 0, 3)
+            hashes(u, "AR%d" % s, 0, 3)
+            ts(R("TA", 0, 3), u, 4096.0, O.mult)
+            ts(R("HHA", 0, 3), R("TA", 0, 3), 4095, O.bitwise_and)
+            tt(R("SQA", 0, 3), R("HHA", 0, 3), R("HHA", 0, 3), O.mult)
+            cp(R("FA", 0, 3), R("HHA", 0, 3))
+            ts(R("KUA", 0, 3), R("SQA", 0, 3), -12.0, O.add, 2.0 ** 28 + 2.0 ** 17, O.add)
+            for l in range(3):
+                ts(R("PMA", l, 24, 3), R("KQ"), R("FA", l, l + 1), O.mult, R("KUA", l, l + 1), O.add)
+            ts(R("TAB_1", 1, 25), R("PMA"), 5, O.arith_shift_right, 4095, O.bitwise_and)
+            cp(R("P1UA"), R("TAB_1", 1, 25))
+            cp(R("P1FA"), R("TAB_1", 1, 25))
+        else:
+            hashes(R("pu", 0, 24), "QA", 0, 24)
+            first_level(R("pu", 0, 24), "TA FA SQA KRA KUA HHA PMA P1UA P1FA", 0, 24, R("TAB_1", 1, 25))
+        act(R("QE"), R("pu", 0, 3), F.Sign, -1.0, R("W256"))
+        phase[0] = "Apar"
         parents(1, R("P1FA"))
 
-    def send(nl, s, blocked):
-        slot = R("ph", 0, nl)
-        tt(R("GO", 0, nl), blocked, R("GW", 0, nl), O.is_lt)
-        tt(R("BL", 0, nl), blocked, R("GC", 0, nl), O.min)
-        mm(slot, R("ID"), R("DM2", 0, nl), True)
-        mm(slot, R("NI"), R("GC", 0, nl))
-        mm(slot, R("TRI"), R("GO", 0, nl))
-        for k in range(1, nl):
-            mm(R("ph", k, nl), R("BD"), R("GO", 0, nl - k))
-        mm(slot, R("ID"), R("BL", 0, nl), False, True)
-        cp(R("SU", 0, nl), slot)
-        scatter(R("SB%d" % s), R("SU", 0, nl), R("VIC", 0, 16 * nl))
+    def slots(l0, l1, s, bank):
+        slot = R(bank, l0, l1)
+        L = lambda name: R(name, l0, l1)
+        blocked = R("CS", 32 * l0 + 31, 32 * l1, 32)
+        mm(slot, R("ID"), L("DM2"), True)
+        mm(slot, R("NI"), L("GC"))
+        for k in range(1, l1 if l0 else 0):
+            a, b = max(l0, k), min(l1, l0 + k)
+            mm(R(bank, a, b), R("BD"), R("GO", a - k, b - k))
+        tt(L("GO"), blocked, L("GC"), O.is_lt)
+        tt(L("BL"), blocked, L("GC"), O.min)
+        mm(slot, R("TRI"), L("GO"))
+        for k in range(1, l1 - l0):
+            mm(R(bank, l0 + k, l1), R("BD"), R("GO", l0, l1 - k))
+        mm(slot, R("ID"), L("BL"), False, True)
+        at = l0 + l0 % 2
+        cp(R("SU", at, at + l1 - l0), slot)
+        scatter(R("SB%d" % s), R("SU", at, at + l1 - l0), R("VIC", 16 * l0, 16 * l1))
+
+    def send(s):
         m = mask_of(core, dst)
         op("g", g.remote_dma, (T["AR%d" % s][:], T["SB%d" % s][:, 0:48], T.sem["arr%d" % s], T.sem["ls%d" % s], pid, rid, m),
-           [R("SB%d" % s, 0, 48)], [], 200.0, "ls%d" % s, bits(m), 2500.0, [R("AR%d" % s)])
+           [R("SB%d" % s, 0, 48)], [], 200.0, "ls%d" % s, bits(m), REMOTE, [R("AR%d" % s)])
 
     def commit(h, s):
         more = s < STEPS - 1
@@ -444,69 +536,104 @@ def rank_program(g, core, T, topo):
         B = lambda name, lo=0, hi=None, step=1: R("%s_%d" % (name, h), lo, hi, step)
         L = lambda name: R(name, l0, l1)
         W = lambda name: R(name, lo, hi)
-        rows, meet = R("pu", 0, hi - lo), ("pc", "ph")[h]
-        if not RINT:
-            cp(L("KMI"), L("KM"))
+        rows, meet = R(("pu", "st0")[h], 0, hi - lo), ("pc", "ph")[h]
+        H = "DA"[h] if s else "0"
+        phase[0] = H + "path"
         i1, iv = R("IX", 2 * l0, 2 * l1, 2), R("IX", 2 * l0 + 1, 2 * l1, 2)
-        ts(L("BI"), L("KMI"), 15, O.bitwise_and)
-        ts(i1, L("KMI"), 4, O.arith_shift_right, 63, O.bitwise_and)
-        tt(L("BT"), L("BI"), L("C1"), O.mult)
-        tt(iv, i1, L("BT"), O.add)
-        cp(R("IU", 2 * l0, 2 * l1), R("IX", 2 * l0, 2 * l1))
-        tgather(W("E"), B("TAB", 0, 1 + 72 * nb), R("IU", 2 * l0, 2 * l1), W("MK"), O.mult)
+        if h:
+            ts(L("BT"), L("KMI"), 255, O.bitwise_and)
+            ts(i1, L("KMI"), 8, O.arith_shift_right, 31, O.bitwise_and)
+        else:
+            ts(L("BI"), L("KMI"), 127, O.bitwise_and)
+            ts(i1, L("KMI"), 7, O.arith_shift_right, 63, O.bitwise_and)
+            ts(L("BT"), L("BI"), 5.0, O.mult)
+        if TTU16:
+            cp(R("IU", 2 * l0, 2 * l1, 2), i1)
+            tt(R("IU", 2 * l0 + 1, 2 * l1, 2), i1, L("BT"), O.add)
+        else:
+            tt(iv, i1, L("BT"), O.add)
+            cp(R("IU", 2 * l0, 2 * l1), R("IX", 2 * l0, 2 * l1))
+        tgather(W("E"), table(h, s, 0, 1 + 72 * nb), R("IU", 2 * l0, 2 * l1), W("MK"), O.mult)
         mm(rows, R("BDF"), W("E"), True, True)
         scan(W("SC"), W("R16"), W("E"), 0.0, O.mult, O.add)
         p1, pv = R("SC", lo + 15, hi, 32), R("SC", lo + 31, hi, 32)
-        cp(W("P16"), rows)
+        signs = SIGNS[h] if s else SIGNS0
+        if len(signs) < 2 * l1:
+            cp(W("P16"), rows)
+        phase[0] = H + "side"
         cp(B("PU", 0, nb), p1)
         act(B("VB", 0, 16 * nb), R("QS", 80 * s, 80 * s + 80) if h == 0 else R("AR%d" % s))
         sgather(B("VB", 16 * nb, 32 * nb), PLACES, B("PU", 0, nb))
         if more:
             cp(B("PU", 8, 8 + nb), pv)
             sgather(R("VIC", 16 * l0, 16 * l1), PLACES, B("PU", 8, 8 + nb))
-            ts(L("GW"), L("KMI"), 0.0, O.is_lt)
-            tt(L("GC"), L("GW"), L("DM2"), O.mult)
-        act(B("PZ", 0, nb), p1)
-        tt(L("L2"), p1, pv, O.is_equal)
-        tt(L("L2"), L("L2"), R("DM", nb, 2 * nb), O.mult)
-        tt(B("PZ", nb, 2 * nb), L("L2"), pv, O.max)
+            if not (MERGE and s):
+                ts(L("GW"), L("KMI"), 0.0, O.is_lt)
+                tt(L("GC"), L("GW"), L("DM2"), O.mult)
+            elif h:
+                ts(R("GW"), R("KMI"), 0.0, O.is_lt)
+                tt(R("GC"), R("GW"), R("DM2"), O.mult)
+        ts(L("L2"), L("BT"), 0.5, O.is_lt, 8192.0, O.mult)
+        tt(L("PZ"), L("L2"), pv, O.add)
+        phase[0] = H + "meet"
         mm(R(meet, 0, hi - lo), R("ID"), W("NM"), True)
-        at = 1600 * h
+        if h == 0 and (signs or s and SIGNS[1]):
+            for k in (0, 1):
+                act(R("SG", 10 * k, 10 * k + 10), R("SC", 15, 160, 16), F.Identity, 1.0, 0.5 - k)
+        at = 3200 * h
         for l in range(l1):
             for pa in range(2):
                 c = max(32 * l, lo)
-                own = R("SC", 32 * l + 16 * pa + 15, 32 * l + 16 * pa + 16)
-                ts(R("EQ", at, at + hi - c), R("P16", c, hi), own, O.is_equal, 8192.0, O.mult)
                 d = 32 if l >= l0 else 0
-                if l < l1 - 1:
-                    mm(R(meet, c + d - lo, hi - lo), R("BD"), R("EQ", at + d, at + hi - c))
-                if d:
-                    mm(R(meet, c - lo, c + d - lo), R("TRI"), R("EQ", at, at + d), False, l == l1 - 1 and pa == 1)
-                at += hi - lo
+                j = 2 * l + pa
+                if j in signs:
+                    ways = [("BDP", "TRP", at), ("BDN", "TRN", at + hi - lo)]
+                    for k in (0, 1):
+                        act(R("EQ", ways[k][2], ways[k][2] + hi - c), R(rows[0], c - lo, hi - lo), F.Sign, -1.0,
+                            R("SG", 10 * k + j, 10 * k + j + 1))
+                else:
+                    ways = [("BD", "TRI", at)]
+                    ts(R("EQ", at, at + hi - c), R("P16", c, hi), R("SC", 16 * j + 15, 16 * j + 16), O.is_equal, 8192.0, O.mult)
+                for bd, tri, e in ways:
+                    if l < l1 - 1:
+                        mm(R(meet, c + d - lo, hi - lo), R(bd), R("EQ", e + d, e + hi - c))
+                    if d:
+                        mm(R(meet, c - lo, c + d - lo), R(tri), R("EQ", e, e + d), False,
+                           l == l1 - 1 and pa == 1 and e == ways[-1][2])
+                at += 2 * (hi - lo)
         scan(W("CS"), W("R32"), R(meet, 0, hi - lo), 0.0, O.mult, O.max)
         blocked = R("CS", lo + 31, hi, 32)
-        tt(B("MM", 0, nb), blocked, R("DM", 0, nb), O.min)
-        tt(B("MM", nb, 2 * nb), blocked, R("DM", nb, 2 * nb), O.min)
-        tt(B("OF", 0, 2 * nb), B("MM", 0, 2 * nb), B("PZ", 0, 2 * nb), O.max)
-        cp(B("OU", 0, 2 * nb), B("OF", 0, 2 * nb))
+        tt(B("MM", 0, nb), blocked, p1, O.add)
+        tt(B("MM", nb, 2 * nb), blocked, L("PZ"), O.add)
+        if TTU16:
+            tt(B("OU", 0, 2 * nb), B("MM", 0, 2 * nb), R("DM", 0, 2 * nb), O.min)
+        else:
+            tt(B("OF", 0, 2 * nb), B("MM", 0, 2 * nb), R("DM", 0, 2 * nb), O.min)
+            cp(B("OU", 0, 2 * nb), B("OF", 0, 2 * nb))
+        phase[0] = H + "put"
         scatter(PLACES, B("OU", 0, 2 * nb), B("VB", 0, 32 * nb))
 
     for s in range(STEPS):
         nl = 8 if s else 5
+        phase[0] = "par"
         parents(0, R("P1F", 40 * s, 40 * s + 40))
-        cp(R("TAB_0", 1, 41), R("P1I", 40 * s, 40 * s + 40))
         tree(0, s)
         if s:
+            phase[0] = "arr"
             arrivals(s)
             tree(1, s)
-        at = len(calls)
         commit(0, s)
         if s:
-            for c in calls[at:-1]:
-                c["early"] = EARLY
             commit(1, s)
         if s < STEPS - 1:
-            send(nl, s + 1, R("CS", 31, 32 * nl, 32))
+            phase[0] = "Dslot" if s else "0slot"
+            if s and SPLIT:
+                slots(0, 5, s + 1, "pc")
+                phase[0] = "Aslot"
+                slots(5, 8, s + 1, "st1")
+            else:
+                slots(0, nl, s + 1, "pc")
+            send(s + 1)
     dma("y", T.y[:], T.X[:, 0:4096], [R("X", 0, 4096)], [], "sy", 5000.0)
 
     count = {}
@@ -515,19 +642,21 @@ def rank_program(g, core, T, topo):
     for s in (1, 2, 3):
         nm = "arr%d" % s
         count[nm] = bits(mask_of(src, core))
-        seen["AR%d" % s] = [(0, 48, True, "remote", nm, count[nm], {})]
+        seen["AR%d" % s] = [(0, 48, True, "remote", nm, count[nm], {}, 1)]
 
     def wait(q, reads, writes):
         need = []
         for kind, rs in ((False, reads), (True, writes)):
-            for (name, lo, hi, _) in rs:
+            for (name, lo, hi, _, step) in rs:
                 bank = name in PSUM
                 for a in seen.get(name, []):
                     if bank and a[3] != q:
                         need.append(a)
                     elif bank and q == "p":
                         pass
-                    elif a[0] < hi and lo < a[1] and (kind or a[2]):
+                    elif kind and a[3] == q and q in INORDER:
+                        pass
+                    elif meets(a, lo, hi, step) and (kind or a[2]):
                         need.append(a)
         best = {}
         for a in need:
@@ -549,15 +678,15 @@ def rank_program(g, core, T, topo):
         snap = dict(clock[q])
         snap[sem] = count[sem]
         for kind, rs in ((False, reads), (True, writes)):
-            for (name, lo, hi, _) in rs:
+            for (name, lo, hi, _, step) in rs:
                 old = seen.get(name, [])
                 if name in PSUM:
                     old = [a for a in old if a[3] != q or (a[2] and not kind)]
                 elif kind:
-                    old = [a for a in old if not (lo <= a[0] and a[1] <= hi)]
+                    old = [a for a in old if not within(a, lo, hi, step)]
                 else:
-                    old = [a for a in old if not (not a[2] and a[3] == q and lo <= a[0] and a[1] <= hi)]
-                old.append((lo, hi, kind, q, sem, count[sem], snap))
+                    old = [a for a in old if not (not a[2] and a[3] == q and within(a, lo, hi, step))]
+                old.append((lo, hi, kind, q, sem, count[sem], snap, step))
                 seen[name] = old
 
     if not ORDER:

from concourse.mybir import AluOpType as O, AxisListType, ActivationFunctionType as F

BIG = float(2 ** 27)
MID = float(2 ** 26)
HIT = float(2 ** 28)
FLOOR = -0.5 + 2.0 ** -13
SENT = 4096
XW = 4368
NB = (5, 3)
SHARE = ((1, 3), (1, 3))
GROUPS = (((0, 2), (2, 3), (5, 2), (7, 2)), ((0, 3), (3, 3), (6, 3)))
SHARE0 = (0, 2)
FIRST = (20, 12)
CUT = (2, 1)
LAST = (1, 2)
RINT = True
SPLIT = True
MERGE = True
DIRECT = True
INORDER = ""
SIGNS = ((), ())
SIGNS0 = ()
TTU16 = True
ANDU16 = False
KPE = (False, False)
PPE = (False, False)
VOIDAT = (2, 1)
REMOTE = 2200.0
ENG = 2
LEAD = {"Dpathv": 2000.0, "Dpathp": 2000.0, "Dmeetv": 2000.0, "Dmeetp": 2000.0}
STEPS = 4
HOP = 230.0
PATIENCE = 0.2
PASSES = 6
PCYC = 0.45
GATHER = 1.3
CYC, SCATTER = 0.83, 3.8

SCRATCH = {}
for _dt, _names in (
        ("bfloat16", "X:4368 QS:320 WT:1 Q8:2560 QA:384 AR1:48 AR2:48 AR3:48 SB1:384 SB2:384 SB3:384 ONE:128 T1:128 BD:128 "
                     "ID:128 NI:128 VI:128 TRI:128 B1:160 BW:160 KC:648 DM2:8 QE:3 D1_0:640 D1_1:384 D2_0:5120 "
                     "D2_1:3072 A_0:5760 A_1:3456 VD_0:320 VD_1:192 EM_0:40 EM_1:24 ZH_0:40 ZH_1:24 EQ:6272 BDP:128 BDN:128 TRP:128 TRN:128 VB_0:160 VB_1:96 "
                     "VIC:128 GO:8 BL:8 GC:8 NM:256 ZR:32"),
        ("float32", "KF:8 KQ:8 KD:1024 W256:1 BDF:128 IDF:128 IC:1 RW:256 MK:256 DM:16 R16:256 R32:256 KR:160 F0:160 SQ0:160 KU0:160 "
                    "P1F:160 KRA:24 FA:24 SQA:24 KUA:24 P1FA:24 UF_0:40 UF_1:24 SQ_0:40 SQ_1:24 KM:8 E:256 SC:256 "
                    "SG:20 PZ:8 L2:8 CS:256 MM_0:10 MM_1:6 OF_0:10 OF_1:6 GW:8"),
        ("int32", "KI:8 PI:1 ICI:1 T0:160 HH0:160 PM0:160 P1I:160 TA:24 HHA:24 PMA:24 UI_0:40 UI_1:24 HH_0:80 HH_1:48 "
                  "PM_0:320 PM_1:192 TAB_0:1600 TAB_1:240 KMI:8 BI:8 BT:8 IX:16"),
        ("uint16", "P1U:160 P1UA:24 P2U_0:320 P2U_1:192 IU:16 PU_0:16 PU_1:16 P16:256 OU_0:10 OU_1:6 SU:10")):
    for _n in _names.split():
        SCRATCH[_n.split(":")[0]] = ("sbuf", [128, int(_n.split(":")[1])], _dt)
PSUM = "pu pk0 pk1 pp pc ph st0 st1".split()
for _n in PSUM:
    SCRATCH[_n] = ("psum", [128, 512], "float32")
HALF = (0, 320)
CODE = (0, 400)
SEMAPHORES = "cv cs cp cg lqs lwt lki lx sy arr1 arr2 arr3 ls1 ls2 ls3".split()


def place(calls, before, after, urge):
    left = [len(b) for b in before]
    ready = [0.0] * len(calls)
    end = [0.0] * len(calls)
    free = {c["q"]: 0.0 for c in calls}
    open_ = {q: [] for q in free}
    for i, c in enumerate(calls):
        if not left[i]:
            open_[c["q"]].append(i)
    out = []
    while len(out) < len(calls):
        t, q = min((max(free[q], min(ready[i] for i in open_[q])), q) for q in open_ if open_[q])
        i = max((k for k in open_[q] if ready[k] <= t), key=lambda k: (urge[k], -k))
        soon = [k for k in open_[q] if t < ready[k] < t + PATIENCE * calls[i]["busy"] and urge[k] > urge[i]]
        if soon:
            i = max(soon, key=lambda k: (urge[k], -k))
            t = ready[i]
        open_[q].remove(i)
        free[q] = t + calls[i]["busy"]
        end[i] = t + calls[i]["done"]
        out.append(i)
        for k, gap in after[i]:
            ready[k] = max(ready[k], end[i] + gap)
            left[k] -= 1
            if not left[k]:
                open_[calls[k]["q"]].append(k)
    return out, end


def arrange(calls):
    before = [list(c["after"].items()) for c in calls]
    after = [[] for _ in calls]
    for i, b in enumerate(before):
        for j, gap in b:
            after[j].append((i, gap))
    urge = [0.0] * len(calls)
    for i in range(len(calls) - 1, -1, -1):
        urge[i] = calls[i]["done"] + max([gap + urge[k] for k, gap in after[i]] + [0.0])
    best = None
    for _ in range(PASSES):
        out, end = place(calls, before, after, [u + c.get("early", 0.0) for u, c in zip(urge, calls)])
        if best is None or max(end) < best[0]:
            best = (max(end), out)
        urge = place(calls, after, before, end)[1]
    return best[1]


ORDER = []


def rank_program(g, core, T, topo):
    rank = T.rank_of(core)
    if rank is None:
        return
    queue = {"v": g.vector, "s": g.scalar, "p": g.tensor, "g": g, "y": g.sync}
    calls = []
    wrote, read, turns = {}, {}, {}
    phase = ["con"]

    def R(name, lo=0, hi=None, step=1):
        if hi is None:
            hi = T[name].shape[1]
        return (name, lo, hi, T[name][:, lo:hi:step] if step != 1 else T[name][:, lo:hi], step)

    def meets(a, lo, hi, step):
        return a[0] < hi and lo < a[1] and not (a[-1] == step and (a[0] - lo) % step)

    def within(a, lo, hi, step):
        return lo <= a[0] and a[1] <= hi and (step == 1 or a[-1] == step and not (a[0] - lo) % step)

    def width(r):
        return r[3].shape[1]

    def narrow(*rs):
        return all(r[0] in SCRATCH and SCRATCH[r[0]][2] in ("bfloat16", "uint16") for r in rs)

    def op(q, call, args, reads, writes, busy, sem=None, n=1, done=None, lands=(), **kw):
        i = len(calls)
        after = {}
        for kind, refs in ((False, reads), (True, list(writes) + list(lands))):
            for (name, lo, hi, _, step) in refs:
                if name in PSUM:
                    t = turns.setdefault(name, [q, [], []])
                    if t[0] != q:
                        t[:] = [q, [], t[1][-1:] if t[0] == "p" else t[1]]
                    for j in t[2]:
                        after[j] = HOP
                    if q == "p":
                        for j in t[1][-1:]:
                            after.setdefault(j, 0.0)
                        t[1].append(i)
                        continue
                    t[1].append(i)
                for a in wrote.get(name, []) + (read.get(name, []) if kind else []):
                    if meets(a, lo, hi, step):
                        if kind and q in INORDER and calls[a[2]]["q"] == q:
                            after.setdefault(a[2], 0.0)
                        else:
                            after[a[2]] = HOP
        for (name, lo, hi, _, step) in reads:
            read.setdefault(name, []).append((lo, hi, i, step))
        for (name, lo, hi, _, step) in list(writes) + list(lands):
            for d in (wrote, read):
                d[name] = [a for a in d.get(name, []) if not within(a, lo, hi, step)]
            wrote[name].append((lo, hi, i, step))
        after.pop(i, None)
        calls.append({"early": LEAD.get(phase[0] + q, 0.0), "q": q, "call": call, "args": args, "kw": kw, "reads": reads, "writes": writes, "sem": sem or "c" + q,
                      "n": n, "busy": busy, "done": done or busy, "after": after})

    def ref(x):
        return x[3] if isinstance(x, tuple) else x

    def refs(*xs):
        return [x for x in xs if isinstance(x, tuple)]

    def cost(n, rate=1.0):
        return max(64.0, n * rate) * CYC

    V, S, P = g.vector, g.scalar, g.tensor

    def cp(out, in_):
        op("v", V.tensor_copy, (out[3], in_[3]), [in_], [out], cost(width(out), 0.5 if narrow(out, in_) else 1))

    def tt(out, a, b, o):
        op("v", V.tensor_tensor, (out[3], a[3], b[3], o), [a, b], [out],
           cost(width(out), 1 if a[0] in PSUM or b[0] in PSUM else 2))

    def ts(out, a, s1, o1, *more):
        s2 = more[0] if more else None
        op("v", V.tensor_scalar, (out[3], a[3], ref(s1), ref(s2), o1) + more[1:], [a] + refs(s1, s2), [out],
           cost(width(out), 0.5 if narrow(out, a) else 1))

    def red(out, a, o):
        op("v", V.tensor_reduce, (out[3], a[3], AxisListType.X, o), [a], [out], cost(width(a)))

    def scan(out, d0, d1, init, o0, o1):
        op("v", V.tensor_tensor_scan, (out[3], d0[3], d1[3], init, o0, o1), [d0, d1], [out], cost(width(out)))

    def ms(out, c):
        op("v", V.memset, (out[3], c), [], [out], cost(width(out), 0.5 if narrow(out) else 1))

    def act(out, in_, func=F.Copy, scale=1.0, bias=None):
        kw = {} if bias is None else {"bias": ref(bias)}
        op("s", S.activation, (out[3], in_[3], func), [in_] + refs(scale, bias), [out], cost(width(out)), scale=ref(scale), **kw)

    def mm(out, l, r, start=False, stop=False):
        op("p", P.matmul, (out[3], l[3], r[3], start, stop), [l, r], [out],
           max(64, width(out)) * PCYC * (1 if narrow(l) else 4))

    def tgather(out, win, off, in1, o):
        op("v", V.tensor_tensor, (out[3], win[3].indirect(off[3]), in1[3], o), [win, off, in1], [out],
           50 + width(out) * GATHER * CYC)

    def sgather(out, win, off):
        op("s", S.activation, (out[3], win[3].indirect(off[3]), F.Copy), [win, off], [out], 65 + width(out) * GATHER * CYC)

    def scatter(win, off, in_):
        op("v", V.tensor_copy, (win[3].indirect(off[3]), in_[3]), [in_, off], [win], 50 + width(in_) * SCATTER * CYC)

    def dma(q, out, in_, reads, writes, sem, done):
        op(q, queue[q].dma_start, (out, in_), reads, writes, 50.0, sem, 16, done)

    dma("y", T.QS[:], T.qs[:], [], [R("QS")], "lqs", 2000.0)
    dma("s", T.WT[:], T.wt[:], [], [R("WT")], "lwt", 2000.0)
    dma("s", T.KI[:], T.kk[:], [], [R("KI")], "lki", 2000.0)
    dma("y", T.X[:, 0:4096], T.x0[:], [], [R("X", 0, 4096)], "lx", 6000.0)
    calls[-1]["after"][0] = -2000.0

    dst = T.cores[(rank + 1) % len(T.cores)]
    src = T.cores[(rank - 1) % len(T.cores)]
    rid, pid, _ = topo.addr(dst)

    def mask_of(a, b):
        return sum(1 << e for e in topo.engines(a, b)[::ENG])

    def bits(m):
        return bin(m).count("1")

    POOL = ("pool", 0, 1, None, 1)

    def aff(out, in_, pattern, cmp, base, cm):
        op("g", g.affine_select, (out[3], in_[3], pattern, cmp, 0.0, base, cm), [in_], [out, POOL],
           170 + 2 * CYC * width(out))

    def iota(out, pattern, base, cm):
        kw = {} if SCRATCH[out[0]][2] == "int32" else {"allow_small_or_imprecise_dtypes": True}
        op("g", g.iota, (out[3], pattern, base, cm), [], [out, POOL], 130 + 2 * CYC * width(out), **kw)

    def row(p, lo, hi):
        return ("KC", lo, hi, T.KC[p:p + 1, lo:hi], 1)

    def double(f, name, lo, w, n):
        while w < n:
            f(R(name, lo + w, lo + 2 * w), R(name, lo, lo + w))
            w *= 2

    def eight(s):
        f = act if s else cp
        at = 640 * s
        for k in (0, 1):
            f(R("Q8", at + 80 * k, at + 80 * k + 80), R("QS", 80 * s, 80 * s + 80))
        for k in (1, 2, 3):
            f(R("Q8", at + 160 * k, at + 160 * k + 160), R("Q8", at, at + 160))

    def hashes(out, data, base, n, start=True):
        for r in range(16):
            mm(out, R("BW", 16 - r, 144 - r), R(data, base + r, base + 16 * n, 16), start and r == 0, r == 15)

    def remainder(u, whole, frac, square):
        ts(whole, u, FLOOR, O.add)
        tt(frac, u, whole, O.subtract)
        tt(square, frac, frac, O.mult)

    def h_of(out, square):
        ts(out, square, 2.0 ** 19, O.mult, -0.375, O.add)

    def place_of(pm, whole, offsets):
        if ANDU16:
            ts(offsets, pm, 4095, O.bitwise_and)
        ts(whole, pm, 4095, O.bitwise_and)
        if not ANDU16:
            cp(offsets, whole)

    def first_level(u, names, lo, hi, p1):
        whole, frac, square, k, ku, hh, pm, p1u, p1f = [R(x, lo, hi) for x in names.split()]
        remainder(u, whole, frac, square)
        tt(ku, frac, k, O.mult)
        h_of(hh, square)
        tt(pm, hh, ku, O.add)
        place_of(pm, p1, p1u)
        cp(p1f, p1)

    def drawn(bank, lo, hi):
        first_level(R(bank, lo, hi), "T0 F0 SQ0 KR KU0 HH0 PM0 P1U P1F", lo, hi, R("P1I", lo, hi))

    def parents(h, p1f):
        n = 8 * NB[h]
        if PPE[h]:
            for b in range(8):
                mm(R("pp", HALF[h] + b * n, HALF[h] + b * n + n), R("IDF"), p1f, b == 0, b == 7)
            return
        act(R("pp", HALF[h], HALF[h] + n), p1f)
        double(act, "pp", HALF[h], n, 8 * n)

    ms(R("ONE"), 1.0)
    ms(R("KC"), 0.0)
    aff(R("T1"), R("ONE"), [[-16, 8], [0, 16]], O.is_ge, 0, 1)
    aff(R("BD"), R("T1"), [[16, 8], [0, 16]], O.is_ge, 15, -1)
    aff(R("ID"), R("ONE"), [[-1, 128]], O.is_equal, 0, 1)
    iota(R("PI"), [[0, 1]], 0, 1)
    iota(R("DM"), [[16, 16]], SENT + 16, 0)
    iota(R("DM2"), [[16, 8]], 128, 0)
    iota(R("RW"), [[0, 16], [1, 16]], 0, 0)
    aff(R("TRI"), R("BD"), [[1, 128]], O.is_ge, -1, -1)
    ms(row(0, 0, 648), -MID)
    for h in (0, 1):
        n1 = 8 * NB[h]
        at = CODE[h]
        a, b = ((128, 8), (256, 24))[h]
        iota(row(32, at, at + n1), [[a, n1]], a, 0)
        iota(row(32, at + n1, at + 9 * n1), [[0, 8], [a, n1]], 8192 + a, 0)
        iota(row(64, at + n1, at + 9 * n1), [[b, 8], [0, n1]], b, 0)
        ms(row(32, at + 9 * n1, at + 10 * n1), -MID)
    ms(row(32, 640, 643), MID)

    ms(R("ZR"), 0.0)
    ms(R("B1"), 0.0)
    ms(R("BW"), 0.0)
    ms(R("X", 4096, XW), 512.0)
    cp(R("B1", 16, 144, 16), R("BD", 0, 128, 16))
    ts(R("BW", 16, 144, 16), R("B1", 16, 144, 16), R("WT"), O.mult, 2.0 ** -12, O.mult)
    ts(R("B1", 16, 144, 16), R("B1", 16, 144, 16), 2.0 ** 14, O.mult)
    eight(0)
    hashes(R("pu", 0, 40), "Q8", 0, 40)
    mm(R("ph", 0, 1), R("BD"), R("WT"), True, True)
    ts(R("KF"), R("KI"), 4096.0, O.mult)
    for l in range(5):
        ts(R("KR", l, 40, 5), R("KI"), 4096.0, O.mult)
    drawn("pu", 0, 40)
    for k in (1, 2, 3):
        eight(k)
    hashes(R("pk1", 40, 160), "Q8", 640, 120)
    double(act, "KR", 0, 40, 160)
    drawn("pk1", 40, 160)
    ts(R("W256"), R("ph", 0, 1), 2.0 ** -4, O.mult)
    act(R("IDF"), R("ID"))
    for b in range(8 if any(KPE) else 0):
        act(R("KD", 128 * b, 128 * b + 128), R("ID"), F.Copy, R("KF", b, b + 1))
    act(R("NI"), R("ID"), F.Copy, -1.0)
    act(R("VI"), R("ID"), F.Copy, -BIG)
    act(R("BDF"), R("BD"))
    for name, of, c in (("BDP", "BD", 4096.0), ("BDN", "BD", -4096.0), ("TRP", "TRI", 4096.0), ("TRN", "TRI", -4096.0)):
        act(R(name), R(of), F.Copy, c)
    ts(R("ICI"), R("PI"), 15, O.bitwise_and)
    cp(R("IC"), R("ICI"))
    ts(R("MK"), R("RW"), R("IC"), O.is_equal)
    ts(R("NM"), R("RW"), R("IC"), O.not_equal, -BIG, O.mult)
    ms(R("R16"), 1.0)
    ms(R("R32"), 1.0)
    ms(R("R16", 0, 256, 16), 0.0)
    ms(R("R32", 0, 256, 32), 0.0)
    ts(R("DM"), R("DM"), R("IC"), O.add)
    ts(R("DM2"), R("DM2"), R("IC"), O.add)
    ms(R("TAB_0", 0, 1600, 400), SENT)
    for s in range(STEPS):
        cp(R("TAB_0", 400 * s + 1, 400 * s + 41), R("P1I", 40 * s, 40 * s + 40))
    ms(R("TAB_1", 0, 1), SENT)
    for l in range(0 if DIRECT else 3):
        ts(R("KRA", l, 24, 3), R("KI"), 4096.0, O.mult)
    ts(R("KQ"), R("KI"), -4096.0, O.add, 32.0, O.mult)
    for s in (1, 2, 3):
        ms(R("SB%d" % s), 512.0)
    PLACES = R("X", 0, XW)

    def queries(h, s, lo=0, hi=None):
        return R("Q8", 640 * s + lo, 640 * s + (hi or 640)) if h == 0 else R("QA", lo, hi or 384)

    def table(h, s, lo, hi):
        at = 0 if h else 400 * s
        return R("TAB_%d" % h, at + lo, at + hi)

    def tree(h, s):
        nb = NB[h]
        n = 8 * nb
        pk = "pk%d" % h
        B = lambda name, lo=0, hi=None, step=1: R("%s_%d" % (name, h), lo, hi, step)
        u = R("pu", 0, n)
        turn = [0]
        H = "DA"[h] if s else "0"
        phase[0] = H + "one"

        def less_q(out, data, at, lo, hi):
            stage = R("st%d" % (turn[0] % 2), 0, hi - lo)
            turn[0] += 1
            mm(stage, R("NI"), queries(h, s, lo, hi), True)
            mm(stage, R("ID"), B(data, at + lo, at + hi), False, True)
            act(B("A", out + lo, out + hi), stage, F.Abs)

        f, p1u, at = ("F0", "P1U", 40 * s) if h == 0 else ("FA", "P1UA", 0)
        m = n - FIRST[h]
        if h and DIRECT:
            for r in range(16):
                mm(R("pu", 0, m), R("BW", 16 - r, 144 - r), R("QA", r, 16 * m, 16), r == 0)
        else:
            mm(R("pu", 0, m), R("IDF"), R(f, at, at + m), True)
        tgather(B("D1", 0, 16 * m), PLACES, R(p1u, at, at + m), queries(h, s, 0, 16 * m), O.subtract)
        if m < n:
            mm(R("pu", m, n), R("ID"), R("ZR", 0, n - m))
            sgather(B("D1", 16 * m, 16 * n), PLACES, R(p1u, at + m, at + n))
        hashes(u, "D1_%d" % h, 0, n, False)
        hashed = len(calls) - 1
        phase[0] = H + "abs1"
        act(B("A", 0, 16 * m), B("D1", 0, 16 * m), F.Abs)
        if m < n:
            less_q(0, "D1", 0, 16 * m, 16 * n)
        phase[0] = H + "hash"
        keys = 10 * n + h * nb
        mm(R(pk, 0, keys), R("ONE"), R("KC", CODE[h], CODE[h] + keys), True)
        calls[-1]["after"].setdefault(hashed, 0.0)
        remainder(u, B("UI"), B("UF"), B("SQ"))
        for k in (0, 1):
            h_of(B("HH", k * n, k * n + n), B("SQ"))
        for bank, b0, b1 in (("ph", 0, 2), ("pc", 2, 8)):
            phase[0] = H + ("rest" if b0 else "hash")
            for b in range(b0, b1):
                if KPE[h]:
                    mm(R(bank, (b - b0) * n, (b - b0 + 1) * n), R("KD", 128 * b, 128 * b + 128), B("UF"), b == b0, b == b1 - 1)
                else:
                    act(R(bank, (b - b0) * n, (b - b0 + 1) * n), B("UF"), F.Copy, R("KF", b, b + 1))
            for b in range(b0, b1, 2):
                tt(B("PM", b * n, (b + 2) * n), R(bank, (b - b0) * n, (b - b0 + 2) * n), B("HH"), O.add)
            tab = table(h, s, 1 + n + b0 * n, 1 + n + b1 * n)
            place_of(B("PM", b0 * n, b1 * n), tab, B("P2U", b0 * n, b1 * n))
        phase[0] = H + "void"
        for r in range(16):
            mm(R("ph", 0, n), R("B1", 16 - r, 144 - r), B("A", r, 16 * n, 16), r == 0, r == 15)
        act(B("EM"), R("ph", 0, n), F.Relu, 2.0 ** 11, -4088.0 * 2.0 ** 25)
        act(B("ZH"), R("ph", 0, n), F.Relu, -2.0 ** 14, HIT)
        cuts = (0, 320, 640) if h == 0 else (0, 384)

        def child(b):
            at = b * 16 * n
            phase[0] = H + "two"
            if b not in (SHARE[h] if s else SHARE0):
                c = CUT[h] if b < 7 else LAST[h]
                for k in range(c):
                    lo, hi = k * n // c, (k + 1) * n // c
                    tgather(B("D2", at + 16 * lo, at + 16 * hi), PLACES, B("P2U", b * n + lo, b * n + hi),
                            queries(h, s, 16 * lo, 16 * hi), O.subtract)
                    if b == 7:
                        act(B("A", at + 16 * (n + lo), at + 16 * (n + hi)), B("D2", at + 16 * lo, at + 16 * hi), F.Abs)
                if b < 7:
                    act(B("A", at + 16 * n, at + 32 * n), B("D2", at, at + 16 * n), F.Abs)
                return
            phase[0] = H + "sg"
            sgather(B("D2", at, at + 16 * n), PLACES, B("P2U", b * n, b * n + n))
            phase[0] = H + "sub"
            for lo, hi in zip(cuts, cuts[1:]):
                less_q(at + 16 * n, "D2", at, lo, hi)

        for b in range(8):
            child(b)
        phase[0] = H + "sum"
        tt(B("VD"), table(h, s, 1 + n, 1 + 9 * n), R("pp", HALF[h], HALF[h] + 8 * n), O.is_equal)
        last = len(GROUPS[h]) - 1
        for k, (blk, nblk) in enumerate(GROUPS[h]):
            if k == VOIDAT[h]:
                for b in range(8):
                    mm(R(pk, (1 + b) * n, (2 + b) * n), R("NI"), B("EM"))
                mm(R(pk, 9 * n, 10 * n), R("ID"), B("ZH"))
                if h == 1:
                    mm(R(pk, 10 * n, keys), R("VI"), R("QE"))
            if k == last:
                mm(R(pk, n, 9 * n), R("VI"), B("VD"))
            for r in range(16):
                mm(R(pk, blk * n, (blk + nblk) * n), R("B1", 16 - r, 144 - r),
                   B("A", blk * 16 * n + r, (blk + nblk) * 16 * n, 16), False, k == last and r == 15)
        phase[0] = H + "path"
        for l in range(nb):
            red(R("KMI" if RINT else "KM", 5 * h + l, 5 * h + l + 1), R(pk, l, keys, nb), O.max)

    def arrivals(s):
        for k in (0, 1):
            act(R("QA", 48 * k, 48 * k + 48), R("AR%d" % s))
        for k in (1, 2, 3):
            act(R("QA", 96 * k, 96 * k + 96), R("QA", 0, 96))
        if DIRECT:
            u = R("pu", 0, 3)
            hashes(u, "AR%d" % s, 0, 3)
            ts(R("TA", 0, 3), u, 4096.0, O.mult)
            ts(R("HHA", 0, 3), R("TA", 0, 3), 4095, O.bitwise_and)
            tt(R("SQA", 0, 3), R("HHA", 0, 3), R("HHA", 0, 3), O.mult)
            cp(R("FA", 0, 3), R("HHA", 0, 3))
            ts(R("KUA", 0, 3), R("SQA", 0, 3), -12.0, O.add, 2.0 ** 28 + 2.0 ** 17, O.add)
            for l in range(3):
                ts(R("PMA", l, 24, 3), R("KQ"), R("FA", l, l + 1), O.mult, R("KUA", l, l + 1), O.add)
            ts(R("TAB_1", 1, 25), R("PMA"), 5, O.arith_shift_right, 4095, O.bitwise_and)
            cp(R("P1UA"), R("TAB_1", 1, 25))
            cp(R("P1FA"), R("TAB_1", 1, 25))
        else:
            hashes(R("pu", 0, 24), "QA", 0, 24)
            first_level(R("pu", 0, 24), "TA FA SQA KRA KUA HHA PMA P1UA P1FA", 0, 24, R("TAB_1", 1, 25))
        act(R("QE"), R("pu", 0, 3), F.Sign, -1.0, R("W256"))
        phase[0] = "Apar"
        parents(1, R("P1FA"))

    def slots(l0, l1, s, bank):
        slot = R(bank, l0, l1)
        L = lambda name: R(name, l0, l1)
        blocked = R("CS", 32 * l0 + 31, 32 * l1, 32)
        mm(slot, R("ID"), L("DM2"), True)
        mm(slot, R("NI"), L("GC"))
        for k in range(1, l1 if l0 else 0):
            a, b = max(l0, k), min(l1, l0 + k)
            mm(R(bank, a, b), R("BD"), R("GO", a - k, b - k))
        tt(L("GO"), blocked, L("GC"), O.is_lt)
        tt(L("BL"), blocked, L("GC"), O.min)
        mm(slot, R("TRI"), L("GO"))
        for k in range(1, l1 - l0):
            mm(R(bank, l0 + k, l1), R("BD"), R("GO", l0, l1 - k))
        mm(slot, R("ID"), L("BL"), False, True)
        at = l0 + l0 % 2
        cp(R("SU", at, at + l1 - l0), slot)
        scatter(R("SB%d" % s), R("SU", at, at + l1 - l0), R("VIC", 16 * l0, 16 * l1))

    def send(s):
        m = mask_of(core, dst)
        op("g", g.remote_dma, (T["AR%d" % s][:], T["SB%d" % s][:, 0:48], T.sem["arr%d" % s], T.sem["ls%d" % s], pid, rid, m),
           [R("SB%d" % s, 0, 48)], [], 200.0, "ls%d" % s, bits(m), REMOTE, [R("AR%d" % s)])

    def commit(h, s):
        more = s < STEPS - 1
        nb = NB[h]
        l0 = 5 * h
        l1, lo, hi = l0 + nb, 32 * l0, 32 * (l0 + nb)
        B = lambda name, lo=0, hi=None, step=1: R("%s_%d" % (name, h), lo, hi, step)
        L = lambda name: R(name, l0, l1)
        W = lambda name: R(name, lo, hi)
        rows, meet = R(("pu", "st0")[h], 0, hi - lo), ("pc", "ph")[h]
        H = "DA"[h] if s else "0"
        phase[0] = H + "path"
        i1, iv = R("IX", 2 * l0, 2 * l1, 2), R("IX", 2 * l0 + 1, 2 * l1, 2)
        if h:
            ts(L("BT"), L("KMI"), 255, O.bitwise_and)
            ts(i1, L("KMI"), 8, O.arith_shift_right, 31, O.bitwise_and)
        else:
            ts(L("BI"), L("KMI"), 127, O.bitwise_and)
            ts(i1, L("KMI"), 7, O.arith_shift_right, 63, O.bitwise_and)
            ts(L("BT"), L("BI"), 5.0, O.mult)
        if TTU16:
            cp(R("IU", 2 * l0, 2 * l1, 2), i1)
            tt(R("IU", 2 * l0 + 1, 2 * l1, 2), i1, L("BT"), O.add)
        else:
            tt(iv, i1, L("BT"), O.add)
            cp(R("IU", 2 * l0, 2 * l1), R("IX", 2 * l0, 2 * l1))
        tgather(W("E"), table(h, s, 0, 1 + 72 * nb), R("IU", 2 * l0, 2 * l1), W("MK"), O.mult)
        mm(rows, R("BDF"), W("E"), True, True)
        scan(W("SC"), W("R16"), W("E"), 0.0, O.mult, O.add)
        p1, pv = R("SC", lo + 15, hi, 32), R("SC", lo + 31, hi, 32)
        signs = SIGNS[h] if s else SIGNS0
        if len(signs) < 2 * l1:
            cp(W("P16"), rows)
        phase[0] = H + "side"
        cp(B("PU", 0, nb), p1)
        act(B("VB", 0, 16 * nb), R("QS", 80 * s, 80 * s + 80) if h == 0 else R("AR%d" % s))
        sgather(B("VB", 16 * nb, 32 * nb), PLACES, B("PU", 0, nb))
        if more:
            cp(B("PU", 8, 8 + nb), pv)
            sgather(R("VIC", 16 * l0, 16 * l1), PLACES, B("PU", 8, 8 + nb))
            if not (MERGE and s):
                ts(L("GW"), L("KMI"), 0.0, O.is_lt)
                tt(L("GC"), L("GW"), L("DM2"), O.mult)
            elif h:
                ts(R("GW"), R("KMI"), 0.0, O.is_lt)
                tt(R("GC"), R("GW"), R("DM2"), O.mult)
        ts(L("L2"), L("BT"), 0.5, O.is_lt, 8192.0, O.mult)
        tt(L("PZ"), L("L2"), pv, O.add)
        phase[0] = H + "meet"
        mm(R(meet, 0, hi - lo), R("ID"), W("NM"), True)
        if h == 0 and (signs or s and SIGNS[1]):
            for k in (0, 1):
                act(R("SG", 10 * k, 10 * k + 10), R("SC", 15, 160, 16), F.Identity, 1.0, 0.5 - k)
        at = 3200 * h
        for l in range(l1):
            for pa in range(2):
                c = max(32 * l, lo)
                d = 32 if l >= l0 else 0
                j = 2 * l + pa
                if j in signs:
                    ways = [("BDP", "TRP", at), ("BDN", "TRN", at + hi - lo)]
                    for k in (0, 1):
                        act(R("EQ", ways[k][2], ways[k][2] + hi - c), R(rows[0], c - lo, hi - lo), F.Sign, -1.0,
                            R("SG", 10 * k + j, 10 * k + j + 1))
                else:
                    ways = [("BD", "TRI", at)]
                    ts(R("EQ", at, at + hi - c), R("P16", c, hi), R("SC", 16 * j + 15, 16 * j + 16), O.is_equal, 8192.0, O.mult)
                for bd, tri, e in ways:
                    if l < l1 - 1:
                        mm(R(meet, c + d - lo, hi - lo), R(bd), R("EQ", e + d, e + hi - c))
                    if d:
                        mm(R(meet, c - lo, c + d - lo), R(tri), R("EQ", e, e + d), False,
                           l == l1 - 1 and pa == 1 and e == ways[-1][2])
                at += 2 * (hi - lo)
        scan(W("CS"), W("R32"), R(meet, 0, hi - lo), 0.0, O.mult, O.max)
        blocked = R("CS", lo + 31, hi, 32)
        tt(B("MM", 0, nb), blocked, p1, O.add)
        tt(B("MM", nb, 2 * nb), blocked, L("PZ"), O.add)
        if TTU16:
            tt(B("OU", 0, 2 * nb), B("MM", 0, 2 * nb), R("DM", 0, 2 * nb), O.min)
        else:
            tt(B("OF", 0, 2 * nb), B("MM", 0, 2 * nb), R("DM", 0, 2 * nb), O.min)
            cp(B("OU", 0, 2 * nb), B("OF", 0, 2 * nb))
        phase[0] = H + "put"
        scatter(PLACES, B("OU", 0, 2 * nb), B("VB", 0, 32 * nb))

    for s in range(STEPS):
        nl = 8 if s else 5
        phase[0] = "par"
        parents(0, R("P1F", 40 * s, 40 * s + 40))
        tree(0, s)
        if s:
            phase[0] = "arr"
            arrivals(s)
            tree(1, s)
        commit(0, s)
        if s:
            commit(1, s)
        if s < STEPS - 1:
            phase[0] = "Dslot" if s else "0slot"
            if s and SPLIT:
                slots(0, 5, s + 1, "pc")
                phase[0] = "Aslot"
                slots(5, 8, s + 1, "st1")
            else:
                slots(0, nl, s + 1, "pc")
            send(s + 1)
    dma("y", T.y[:], T.X[:, 0:4096], [R("X", 0, 4096)], [], "sy", 5000.0)

    count = {}
    clock = {q: {} for q in queue}
    seen = {}
    for s in (1, 2, 3):
        nm = "arr%d" % s
        count[nm] = bits(mask_of(src, core))
        seen["AR%d" % s] = [(0, 48, True, "remote", nm, count[nm], {}, 1)]

    def wait(q, reads, writes):
        need = []
        for kind, rs in ((False, reads), (True, writes)):
            for (name, lo, hi, _, step) in rs:
                bank = name in PSUM
                for a in seen.get(name, []):
                    if bank and a[3] != q:
                        need.append(a)
                    elif bank and q == "p":
                        pass
                    elif kind and a[3] == q and q in INORDER:
                        pass
                    elif meets(a, lo, hi, step) and (kind or a[2]):
                        need.append(a)
        best = {}
        for a in need:
            if clock[q].get(a[4], 0) < a[5] and (a[4] not in best or best[a[4]][5] < a[5]):
                best[a[4]] = a
        for s in list(best):
            a = best[s]
            if any(o != s and best[o][6].get(s, 0) >= a[5] for o in best):
                continue
            queue[q].wait_ge(T.sem[s], a[5])
        for s in best:
            a = best[s]
            for k in a[6]:
                clock[q][k] = max(clock[q].get(k, 0), a[6][k])
            clock[q][s] = max(clock[q].get(s, 0), a[5])

    def note(q, reads, writes, sem, n):
        count[sem] = count.get(sem, 0) + n
        snap = dict(clock[q])
        snap[sem] = count[sem]
        for kind, rs in ((False, reads), (True, writes)):
            for (name, lo, hi, _, step) in rs:
                old = seen.get(name, [])
                if name in PSUM:
                    old = [a for a in old if a[3] != q or (a[2] and not kind)]
                elif kind:
                    old = [a for a in old if not within(a, lo, hi, step)]
                else:
                    old = [a for a in old if not (not a[2] and a[3] == q and within(a, lo, hi, step))]
                old.append((lo, hi, kind, q, sem, count[sem], snap, step))
                seen[name] = old

    if not ORDER:
        ORDER.extend(arrange(calls))
    for i in ORDER:
        c = calls[i]
        wait(c["q"], c["reads"], c["writes"])
        done = c["call"](*c["args"], **c["kw"])
        if not c["sem"].startswith("ls"):
            done.then_inc(T.sem[c["sem"]], c["n"])
        note(c["q"], c["reads"], c["writes"], c["sem"], c["n"])
    for sem in count:
        if clock["y"].get(sem, 0) < count[sem]:
            g.sync.wait_ge(T.sem[sem], count[sem])
